import numpy as np, ml_dtypes
CORES = [35,38,43,46]
N = 4
BF = ml_dtypes.bfloat16
V, VB, S, L, LB, B, RO = 4096, 12, 2048, 256, 128, 2, 4
def picks(lm, s, j):
    g = np.arange(8)[:, None, None]; k = np.arange(16)[None, :, None]
    a = lm[g, k, s[:, None, :]] >> VB
    return lm[g, (j[:, None, :] + k) & 15, a] & (V - 1)
def sample(f, lm, x, p, q, s, t):
    g = np.arange(8)[:, None, None, None]; i = np.arange(16)[None, :, None, None]; k = np.arange(16)[None, :, None]
    j = (np.sum(x, axis=1) + t) & 15
    m = picks(lm, s, j)
    void = np.any(m[:, :, None, :] == q[:, None, :, :], axis=2)
    n = np.where((p >= 0) & (((j[:, None, :] + k) & 1) == 1), p, np.where(void, -1, m))
    fz = f[g, i, np.maximum(n, 0)[:, None, :, :]]
    dist = np.where(n < 0, 1 << 20, np.sum(np.abs(fz - x[:, :, None, :]), axis=1))
    return j, n, dist, np.argmin(dist, axis=1)
def names(rng, pop, share, n):
    i = rng.integers(0, 64, (N, 8, 16, n)); g = np.arange(8).reshape(1, 8, 1, 1)
    return np.where(rng.random(i.shape) < share, pop[g, i], rng.integers(0, V, i.shape))
def parts(rng, share=0.5, fp=0.5, fq=0.6):
    pop = rng.integers(0, V, (8, 64)); d = {}
    d["f"] = rng.integers(0, 256, (N, 8, 16, V)); d["lm"] = rng.integers(0, S, (N, 8, 16, S)) * V + names(rng, pop, share, S)
    d["sn"] = rng.integers(0, S, (N, 8, V)); d["th"] = rng.integers(500, 1200, (N, 8, L)); d["x"] = rng.integers(0, 256, (N, 8, 16, L))
    d["p"] = np.where(rng.random((N, 8, 16, L)) < fp, names(rng, pop, share, L), -1)
    d["q"] = np.where(rng.random((N, 8, 16, L)) < fq, names(rng, pop, share, L), -1)
    d["s"] = rng.integers(0, S, (N, 8, L)); d["v"] = rng.integers(0, V, (N, 8, L))
    return d
def pack(d):
    o = {"feat": d["f"].reshape(N, 128, V).astype(np.float32).astype(BF), "lm": d["lm"].reshape(N, 128, S).astype(np.int32), "sn": d["sn"].astype(np.int32), "th": d["th"].astype(np.int32),
         "lx": d["x"].reshape(N, 128, L).astype(np.float32).astype(BF), "lp": d["p"].reshape(N, 128, L).astype(np.int32), "lq": d["q"].reshape(N, 128, L).astype(np.int32),
         "ls": d["s"].astype(np.int32), "lv": d["v"].astype(np.int32)}
    return {k: np.ascontiguousarray(a) for k, a in o.items()}
def setup_inputs(rng):
    return pack(parts(rng))
def setup_inputs_spread(rng):
    d = parts(rng, share=rng.choice(np.array([0.0, 0.3, 0.7, 0.95]), (N, 8, 1, 1)), fp=rng.random((N, 8, 1, L)), fq=rng.random((N, 8, 1, L)))
    d["f"] = np.minimum((np.exp2(8 * rng.random((N, 8, 1, V))) * rng.random((N, 8, 16, V))).astype(np.int64), 255)
    d["x"] = np.minimum((np.exp2(8 * rng.random((N, 8, 1, L))) * rng.random((N, 8, 16, L))).astype(np.int64), 255)
    d["th"] = np.minimum(np.exp2(12 * rng.random((N, 8, L))).astype(np.int64), 4095)
    d["lm"] = np.minimum((S * rng.random((N, 8, 16, S)) ** 4).astype(np.int64), S - 1) * V + (d["lm"] & (V - 1))
    d["sn"] = np.minimum((S * rng.random((N, 8, V)) ** 3).astype(np.int64), S - 1)
    d["s"] = np.minimum((S * rng.random((N, 8, L)) ** 2).astype(np.int64), S - 1)
    return pack(d)
def twoends(rng, lo, hi, *shape):
    share = np.array([1.0, 0.7, 1.0, 0.7, 0.9, 0.7, 0.8, 1.0]).reshape((1, 8) + (1,) * (len(shape) - 2))
    return np.where(rng.random(shape) < share, np.where(rng.random(shape) < 0.5, lo, hi), rng.integers(lo, hi + 1, shape))
def byrecord(rng, lo, hi, n):
    c = rng.integers(0, 4, (N, 8, 1, n))
    return np.where(c == 0, lo, np.where(c == 1, hi, twoends(rng, lo, hi, N, 8, 16, n)))
def setup_inputs_ends(rng):
    d = {"f": byrecord(rng, 0, 255, V), "x": byrecord(rng, 0, 255, L), "p": byrecord(rng, -1, V - 1, L), "q": byrecord(rng, -1, V - 1, L), "lm": twoends(rng, 0, S * V - 1, N, 8, 16, S),
         "sn": twoends(rng, 0, S - 1, N, 8, V), "th": twoends(rng, 0, 4095, N, 8, L), "s": twoends(rng, 0, S - 1, N, 8, L), "v": twoends(rng, 0, V - 1, N, 8, L)}
    r = N - 1
    d["f"][r, 7, :, 0] = 255; d["f"][r, 7, :, V - 1] = 255; d["x"][r, 7, :, 0::2] = 255; d["x"][r, 7, :, 1::2] = 0
    d["th"][r, 7, 1::4] = 4095; d["th"][r, 7, L - 1] = 4095; d["sn"][r, 7, 0] = 0; d["sn"][r, 7, V - 1] = S - 1
    d["s"][r, 7, L - 1] = 0; d["p"][r, 7, :, L - 1] = -1; d["q"][r, 7, :, L - 1] = -1
    d["lm"][r, 7, 0, 0] = S * V - 1; d["lm"][r, 7, 0, S - 1] = S * V - 1; d["lm"][r, 7, 15, 0] = 0
    d["sn"][0, 6:] = S - 1; d["s"][0, 6:] = 0; d["th"][0, 6:] = 4095; d["q"][0, 6:] = -1; d["s"][0, 6, L - 1] = S - 1
    return pack(d)
def setup_inputs_corners(rng):
    d = parts(rng)
    u = rng.random((N, 8, 16, S)); w = rng.random((N, 8, 16, S)); c = np.arange(S)
    link = np.where(u < 0.2, c, np.where(u < 0.3, 0, np.where(u < 0.4, S - 1, d["lm"] >> VB)))
    d["lm"] = link * V + np.where(w < 0.05, 0, np.where(w < 0.1, V - 1, d["lm"] & (V - 1)))
    u = rng.random((N, 8, L)); d["s"] = np.where(u < 0.05, 0, np.where(u < 0.1, S - 1, d["s"]))
    u = rng.random((N, 8, L)); d["v"] = np.where(u < 0.05, 0, np.where(u < 0.1, V - 1, d["v"]))
    k = np.arange(16)[None, :, None]
    for r in range(N):
        m = picks(d["lm"][r], d["s"][r], np.sum(d["x"][r], axis=1) & 15)
        kind = rng.integers(0, 7, (8, 1, L)); kind[:, 0, :7] = np.arange(7); kind[:, 0, L - 7:] = np.arange(7)[::-1]
        o = rng.integers(0, 16, (8, 1, L)); keep = np.take_along_axis(m, o, 1); full = rng.integers(0, V, (8, 16, L))
        p, q = d["p"][r], d["q"][r]
        p = np.where((kind == 0) | (kind == 1) | (kind == 3), -1, np.where(kind == 2, full, np.where(kind == 4, np.where(k == o, full, -1), np.where(kind == 5, m[:, ::-1], p))))
        q = np.where((kind == 0) | (kind == 2), m, np.where(kind == 1, np.where(m == keep, -1, m), np.where(kind == 3, -1, np.where((kind == 4) | (kind == 5), full[::-1], q))))
        d["p"][r] = p; d["q"][r] = q
        j, n, dist, best = sample(d["f"][r], d["lm"][r], d["x"][r], p, q, d["s"][r], 0)
        nb = np.take_along_axis(n, best[:, None, :], 1)[:, 0]; db = np.take_along_axis(dist, best[:, None, :], 1)[:, 0]
        e = rng.integers(0, 6, (8, L))
        d["th"][r] = np.minimum(np.where(e == 0, db, np.where(e == 1, db + 1, np.where(e == 2, 0, np.where(e == 3, 4095, d["th"][r])))), 4095)
        gi, li = np.nonzero((nb >= 0) & (rng.random((8, L)) < 0.1))
        d["sn"][r][gi, nb[gi, li]] = d["s"][r][gi, li]
    d["lm"][:, 5] = (d["lm"][:, 5] >> VB) * V + 7; d["v"][:, 5] = 7; d["p"][:, 5] = -1; d["th"][:, 5] = 4095
    d["q"][:, 5] = 7; d["q"][:, 5, :, :31] = -1; d["sn"][:, 5, 7] = 10 + np.arange(N); d["s"][:, 5, :31] = 100
    return pack(d)
def setup_inputs_crowd(rng):
    d = parts(rng)
    d["f"][:, 1::2] = np.tile(rng.integers(0, 256, (N, 8, 16, 16)), V >> 4)[:, 1::2]
    d["sn"][:, 1::2] = np.take_along_axis(rng.integers(0, S, (N, 8, 2)), rng.integers(0, 2, (N, 8, V)), 2)[:, 1::2]
    c = np.stack([rng.permutation(S)[:N] for g in range(8)], axis=1); c[:, 6] = c[0, 6]
    a = (100 + np.arange(N) % 3)[:, None, None]
    for g in (0, 2, 4, 6):
        d["sn"][:, g] = c[:, g, None]; d["s"][:, g] = (c[:, g, None] + 1 + rng.integers(0, S - 1, (N, L))) % S
        d["q"][:, g] = -1; d["th"][:, g] = 4095
        if g < 4: d["f"][:, g] = a; d["x"][:, g] = a; d["th"][:, g] = 1
        if g == 2 or g == 4:
            pos = rng.integers(0, L, N); pos[N - 1] = L - 1; d["s"][np.arange(N), g, pos] = c[:, g]
    return pack(d)
def setup_inputs_turns(rng):
    d = parts(rng)
    base = rng.integers(0, 100, (8, 16)); base[:, 0] ^= 1 - (np.sum(base, axis=1) & 1)
    lev = np.stack([6 * rng.permutation(N) for g in range(8)], axis=1) + rng.integers(0, 14, 8) + 100 * (np.arange(N) & 1)[:, None]
    d["f"][:] = (base + lev[:, :, None])[..., None]; d["x"][:] = (base + lev[:, :, None])[..., None]
    c = rng.choice(np.array([0, 1, 31, L - 1, L]), (N, 8)); c[0] = L; c[N - 1] = L - 1
    for r in range(N):
        for g in range(8):
            z = rng.permutation(V)[:L]; u = rng.permutation(S)[:L]; go = rng.permutation(L) < c[r, g]
            d["sn"][r, g, z] = u; d["p"][r, g, 0] = z
            d["s"][r, g] = np.where(go, (u + 1 + rng.integers(0, S - 1, L)) % S, u)
    h = 1 + np.arange(L) // LB; rr = np.arange(N)[:, None]; here = lev[:, :, None]
    one = lev[(rr - h) % N].transpose(0, 2, 1); two = lev[(rr - 2 * h) % N].transpose(0, 2, 1)
    d1 = 16 * np.abs(here - one); d2 = 16 * np.abs(here - ((one + two) >> 1)); e = rng.integers(0, 2, (N, 8, L))
    d["th"] = d1 - (c[:, :, None] & 31) + e
    calm = np.where((d2 > 0) & (d2 + 32 <= d1), d2 + e, 1)
    for g in (1, 6): d["th"][:, g] = calm[:, g]
    return pack(d)
def check_inputs(d):
    bad = []
    for k, lo, hi in (("feat", 0, 255), ("lm", 0, S * V - 1), ("sn", 0, S - 1), ("th", 0, 4095), ("lx", 0, 255), ("lp", -1, V - 1), ("lq", -1, V - 1), ("ls", 0, S - 1), ("lv", 0, V - 1)):
        a = np.asarray(d[k]).astype(np.float64)
        if not np.all((a >= lo) & (a <= hi) & (np.floor(a) == a)): bad.append("range of " + k)
    return bad
def reference(feat, lm, sn, th, lx, lp, lq, ls, lv):
    f = feat.astype(np.float32).astype(np.int64).reshape(N, 8, 16, V); rec = lm.astype(np.int64).reshape(N, 8, 16, S)
    sup = sn.astype(np.int64); thr = th.astype(np.int64)
    x = lx.astype(np.float32).astype(np.int64).reshape(N, 8, 16, L); p = lp.astype(np.int64).reshape(N, 8, 16, L); q = lq.astype(np.int64).reshape(N, 8, 16, L)
    s = ls.astype(np.int64); v = lv.astype(np.int64); moved = np.zeros((N, 8), np.int64)
    g2 = np.arange(8)[:, None]; g3 = np.arange(8)[:, None, None]; i3 = np.arange(16)[None, :, None]
    for t in range(RO):
        for r in range(N):
            j, n, dist, best = sample(f[r], rec[r], x[r], p[r], q[r], s[r], t)
            nb = np.take_along_axis(n, best[:, None, :], 1)[:, 0]; db = np.take_along_axis(dist, best[:, None, :], 1)[:, 0]
            live = nb >= 0; z = np.maximum(nb, 0); s2 = sup[r][g2, z]
            go = live & (db < thr[r] + (moved[r][:, None] & 31)) & (s2 != s[r])
            m2 = picks(rec[r], s2, j)
            eq = n[:, :, None, :] == m2[:, None, :, :]
            p[r] = np.where(go[:, None, :], np.where(np.any(eq, axis=2), -1, n), p[r])
            q[r] = np.where(go[:, None, :], np.where(np.any(eq, axis=1), -1, m2), q[r])
            for g in range(8):
                w = np.flatnonzero(go[g]); u, first = np.unique(s2[g, w], return_index=True); w = w[first]
                rec[r, g, j[g, w], u] = s[r, g, w] * V + v[r, g, w]
            x[r] = np.where(live[:, None, :], (x[r] + f[r][g3, i3, z[:, None, :]]) >> 1, x[r])
            s[r] = np.where(go, s2, s[r]); moved[r] = np.sum(go, axis=1)
        if t < RO - 1:
            for b in range(B):
                lo, hi = b * LB, (b + 1) * LB
                for a in (x, p, q, s, v): a[..., lo:hi] = np.roll(a[..., lo:hi], 1 + b, axis=0)
    return {"ylm": rec.reshape(N, 128, S).astype(np.float32), "yx": x.reshape(N, 128, L).astype(np.float32), "yp": p.reshape(N, 128, L).astype(np.float32),
            "yq": q.reshape(N, 128, L).astype(np.float32), "ys": s.astype(np.float32)}

@@ -1,0 +1,634 @@
+import math
+from concourse.mybir import AluOpType, ActivationFunctionType
+
+OP = AluOpType
+AF = ActivationFunctionType
+RO, NH, H = 4, 2, 128
+VOID0, FEAT0 = 1024, 1040
+MEM0 = 2064
+W19 = float(2 ** 19)
+MAGIC = 1.5 * 2.0 ** 42
+MAGIC1 = 1.5 * 2.0 ** 23
+FOLD = False
+BY_MAX = [0, 1]
+ORDER = (
+    "000A0E020I0M0Q040y0S081I1K0G0K0U0O100C0i1E1q1c1224231x3c1i1u1a1m2O1y1o0w1e261U1G202F2I2M2c2k1A061S1k2U2Y2s3O1Y2G3q1O180e0s0o2A1W282C0W0a0Y"
+    "0k140q170m0c1Q1M1C0g0u2K2a4Q2e3C4E1g1s2W2o2y302u343w3A3W4g3I2S2i3U362m3G3i46484S4u4a4m504W4c524y5A5I4o5G5O5V5a5e5i5o685u5k6c6o6w6g6u726m70"
+    "786W6k7C7K7O7T7W7Y7c80868K8s92969G8A8E8U8a8o908g8e8j8y9A9O9S3S9W9E8l9KAWA2AEAmAIAcAuAAAQAw9sA6AyB1B6BABG9U9k9u9yA02x3E429I3m8Q9Y9o2Q2g2q3M"
+    "32383K3Y3a414A3s4C4I3k3u4K3o4G4O3y4M4U4Y4e4i4k4q4t4w54585C5E5M5K5S5Q5W5Y5c5g5m5q5s5w5z6062646B6E6L6Q666C6G6S6Y6q6O6M747A6i767I3e7M6a6U6y8c"
+    "7a8M8m7m8q8u848w987G7U9C9M9i9q9w7E7Q7e7g7o3Q44576e3g6I6s7i7s7u7y82888C8G8WA4A8ACAGAKAMASAY9Q9a9e9gAOAgAiAUAkB4AsAaBKBQBeBuByCGCMCSCgC0CACi"
+    "C8CYCmCQCeCqCwCyD2D6DCDIDUD8E8EGEMDwE6EOECEKESE4EAEUEaEcEgEeEqF0FKFQFUFeGWGgGsFSFYFiFoFwGmGOFsG2GIG0GKGSAqGYG4GGGuHWH4HGHkHMHaIEHAHoIMHuIG"
+    "IQIVIYIaIeGiGoH0H6HEB2BCBIGaBSGAGyH87k7q8Y7w8SAeAoBEB8BPBiBYBgBmBMBWBoBUBaBqBcBkBsBxC2C4C6CCCFCICKCOCWCUCcCaCoCkCuCsD0D4DADEDGDKDNDODQDWDb"
+    "DcDjDoDSDYDeDmDyEEDqDkE0EWDsEoEw94F2DuEQEiFgF6FkG6FqG8GEFOGCGMEYEmGcGqH2HwIAEkEuF8FAFC8J8O9mE29cDgEIEyFEFIFMFWFaFcFmGeHKHQHUHYHeHiHqHsGkHC"
+    "HIHcI0I2HyICIIISIgHgIWIiJ0JIJOJeJiK0K8JWJsKAJMJkKCJyK6KGKLKOKQKUKaKgKsKWLSLaLgLKLQLiLYLeLmLMLULoM0M4MBMCMIMQMmMsMwN4NCO2OAMuN0N8NENMO6NoNI"
+    "NUNgNSNiNmI4NsNWNONqPGOmP2PWOKOYPcOwPOPeOcPAPgPjPmPqPuO0O4OGOMOSHmI6IONwJCNQOEOOEsF4GwFGHOI8IKIcIkIxJ4IsJ2J8ImIqJAIoIuJEIyJ6JGJLJQJSJUJYJb"
+    "JcJgJmJoJqJwJuK4K2KIKEKMKSKYKcKeKiKlKmKoKuKzL0L7LCKqKwL2LALELWLsL8LOLqLGM8MEFyMMLkLILcMqNGNYNeMWNcNyMeNAOCLuM6OUOkP8PIPQLwM2MSMUMYFuGQGVLy"
+    "HSL4MKMaMcMgMkMoMyN2N6OIOaOeOiOoOsOyP6PCNaOgOuP4Q4PKPEPUPkPaOqPoQ0QKQaQgRCR0RARKQoRGRSQwR2RUQeRQRaRdRgRiRmRsRwS8RoSiSyT6SYSgT8SmT4TASeSoTC"
+    "TGTITRTMTUTcTyU4UEUKUgUoU8UGUOUSUaVAV0UYUeUwUcV2VKWEWKWOUqV8VuVMVWW4VSVyW8VkW6WAVcVmWCWHWMWQWUWWWaV4VEVIVUVYP0PSPwV6Q6UmVGVOMGMOO8MiOWPMPY"
+    "PsPyQHQOQCQMQSQ2QAQUQ8QEQWQIQQQYQdQiQkQmQqQtQuQyR4R6R8RIRERORMRYRWReRkRqRuRyS0S3S4S6SCSHSISPSASESKSUSaT0SQSSSkSqStTKTaTqUQUWScSwU2TiTuUMTO"
+    "UCUkUUUiUsTYU6UyVCVQVaWIWSWYSuTETSTWTgNKNkNvSWOQSMT2TeTkTmToTsTwU0UAUIVeVgViVoVqVsVwW0UuW2"
+)
+LETTERS = "0123456789ABCDEFGHIJKLMNOPQRSTUVWXYZabcdefghijklmnopqrstuvwxyz"
+
+SCRATCH = {
+    "fw": ("sbuf", [128, FEAT0 + 4096], "bfloat16"),
+    "tab0": ("sbuf", [128, 2 * MEM0], "float32"),
+    "tab1": ("sbuf", [128, 2 * MEM0], "float32"),
+    "lmi": ("sbuf", [128, 2048], "int32"),
+    "lmt": ("sbuf", [128, 2048], "int32"),
+    "snr": ("sbuf", [128, 4096], "int32"),
+    "trip": ("sbuf", [128, 2048], "bfloat16"),
+    "af": ("sbuf", [128, 12544], "float32"),
+    "ab": ("sbuf", [128, 26400], "bfloat16"),
+    "ah": ("sbuf", [128, 15872], "float16"),
+    "ai": ("sbuf", [128, 2688], "int32"),
+    "au": ("sbuf", [128, 4992], "uint16"),
+}
+for _b in range(8):
+    SCRATCH["ps%d" % _b] = ("psum", [128, 512], "float32")
+SEMAPHORES = ["cV", "cS", "cP", "cG", "left"] + ["d%d" % i for i in range(40)] + ["a%d" % i for i in range(18)]
+
+CY, PE, GA, SC = 1.0, 0.5, 1.56, 3.8
+SAME, OTHER, REMOTE = 60.0, 110.0, 3000.0
+
+
+def build(g, core, T, topo):
+    rank = T.rank_of(core)
+    n = len(T.cores)
+    ops = []
+    used = {"af": 0, "ab": 0, "ah": 0, "ai": 0, "au": 0}
+    kept = {}
+    cur = [None, None]
+    V, S, P = g.vector, g.scalar, g.tensor
+
+    def al(arena, w):
+        a = used[arena]
+        used[arena] = a + (w + 15) // 16 * 16
+        assert used[arena] <= SCRATCH[arena][1][1], arena
+        return [arena, a, w, "%s@%d" % (arena, a)]
+
+    def tmp(name, h, w, arena="af"):
+        if (name, h) not in kept:
+            kept[name, h] = al(arena, w)
+        return kept[name, h]
+
+    def ap(b, lo=0, hi=None, step=1, p1=128):
+        hi = b[2] if hi is None else hi
+        if step == 1:
+            return T[b[0]][0:p1, b[1] + lo:b[1] + hi]
+        return T[b[0]][0:p1, b[1] + lo:b[1] + hi:step]
+
+    def sub(b, q):
+        return "%s/%d" % (b[3], q)
+
+    def keys(xs):
+        return [x if isinstance(x, str) else x[3] for x in xs]
+
+    def op(eng, fn, cost, r=(), w=(), t=(), lat=0.0, kind="c"):
+        ops.append({"e": eng, "fn": fn, "c": float(cost), "r": keys(r), "w": keys(w), "t": list(t), "lat": lat, "k": kind, "tv": cur[0], "stage": cur[1]})
+
+    def tile():
+        return {"bank": None, "ops": []}
+
+    def ps(t, lo, hi, step=1, p1=128):
+        if step == 1:
+            return T["ps%d" % t["bank"]][0:p1, lo:hi]
+        return T["ps%d" % t["bank"]][0:p1, lo:hi:step]
+
+    def vc(w, rate=1.0):
+        return 15 + max(64, w * rate) * CY
+
+    def sc(w):
+        return 60 + w * CY
+
+    def ts(out, in0, s1, s2, o0, o1=None):
+        if o1 is None:
+            return V.tensor_scalar(out, in0, s1, None, o0)
+        return V.tensor_scalar(out, in0, s1, s2, o0, o1)
+
+    def vts(o, i, s1, s2, o0, o1=None, r=()):
+        op("V", lambda: [ts(ap(o), ap(i), s1, s2, o0, o1)], vc(o[2]), [i] + list(r), [o])
+
+    def vtt(o, a, b, o0):
+        op("V", lambda: [V.tensor_tensor(ap(o), ap(a), ap(b), o0)], vc(o[2], 2.0), [a, b], [o])
+
+    def act(e, o, i, func=AF.Identity, bias=0.0, scale=1.0):
+        if e == "S":
+            return S.activation(o, i, func, bias=bias, scale=scale)
+        if func == AF.Sigmoid:
+            return ts(o, i, 0.0, 1.0 / 64, OP.is_equal, OP.mult)
+        if func == AF.Relu:
+            return ts(o, i, bias, 0.0, OP.add, OP.max)
+        if bias == 0.0 and scale == 1.0:
+            return V.tensor_copy(o, i)
+        return ts(o, i, scale, bias, OP.mult, OP.add)
+
+    def flex(fn, cs, cv, r=(), w=(), t=()):
+        op("F", fn, min(cs, cv), r, w, t)
+        ops[-1]["cost"] = {"S": cs, "V": cv}
+
+    def sact(o, i, bias=0.0, scale=1.0):
+        flex(lambda e, _: [act(e, ap(o), ap(i, 0, o[2]), AF.Identity, bias, scale)], sc(o[2]), vc(o[2]), [i], [o])
+
+    def pick(o, lo, hi, win, lst, a, b, r, w):
+        flex(lambda e, _: [act(e, ap(o, lo, hi), win.indirect(ap(lst, a, b)))], 75 + (hi - lo) * GA, 60 + (hi - lo) * GA, r + [lst], w)
+
+    def rounded(o, okey, tl, w, magic, r1):
+        def fn(e, chain):
+            if e == "V":
+                return [ts(o, ps(tl, 0, w), magic, -magic, OP.add, OP.add)]
+            chain(S.activation(ap(r1), ps(tl, 0, w), AF.Identity, bias=magic))
+            return [S.activation(o, ap(r1), AF.Identity, bias=-magic)]
+        flex(fn, 2 * sc(w) + 60, vc(w), [], [okey, r1], [tl])
+
+    def mm(t, calls, cyc, r):
+        def fn():
+            last = None
+            for c in calls:
+                last = P.matmul(ps(t, c[0], c[1], c[2], c[7] if len(c) > 7 else 128), c[3], c[4], c[5], c[6])
+            return [last]
+        op("P", fn, 20 + cyc * PE, r, [], [t])
+
+    clock = [1500.0]
+
+    def dma(q, pairs, nbytes, r=(), w=()):
+        clock[0] += nbytes / 250.0
+        eng = g.sync if q == "Y" else g.scalar
+        op(q, lambda: [eng.dma_start(o, i) for o, i in pairs], 60 * len(pairs), r, w, lat=(clock[0] if not r else 2000 + nbytes / 250.0), kind="d")
+
+    arr = [0]
+
+    def send(h, out, in_, r, w, nbytes):
+        dst = T.cores[(rank + 1 + h) % n]
+        rid, pid, _ = topo.addr(dst)
+        eng = topo.engines(core, dst)[:8]
+        m = sum(1 << e for e in eng)
+        sem = "a%d" % arr[0]
+        arr[0] += 1
+        op("G", lambda: [g.remote_dma(out, in_, T.sem[sem], T.sem.left, pid, rid, m)], 400, r, w, lat=REMOTE + nbytes / 50.0, kind="r")
+        ops[-1]["sem"] = sem
+        ops[-1]["n"] = len(eng)
+
+    def strip(t, h):
+        return (7 - (2 * t + h)) * H
+
+    def xap(t, h):
+        return T.fw[:, strip(t, h):strip(t, h) + H]
+
+    svt, lpq = al("ai", 768), al("ai", 512)
+    dma("Y", [(ap(svt, 0, 256, p1=8), T.ls[:, :]), (ap(svt, 256, 512, p1=8), T.lv[:, :]), (ap(svt, 512, 768, p1=8), T.th[:, :])], 24576, w=[svt])
+    dma("Y", [(xap(0, h), T.lx[:, H * h:H * h + H]) for h in range(NH)], 65536, w=["x00", "x01"])
+    for q in range(2):
+        dma("Y" if q == 0 else "S", [(T.lmi[:, 1024 * q:1024 * q + 1024], T.lm[:, 1024 * q:1024 * q + 1024])], 524288, w=["lmi%d" % q])
+    dma("Y", [(ap(lpq, 0, 256), T.lp[:, :]), (ap(lpq, 256, 512), T.lq[:, :])], 262144, w=[lpq])
+    dma("Y", [(T.fw[:, FEAT0:FEAT0 + 4096], T.feat[:, :])], 1048576, w=["feat"])
+    dma("Y", [(T.snr[i:128:16, :], T.sn[:, :]) for i in range(16)], 2097152, w=["snr"])
+
+    ioq, ioc, iow, gc, pc = al("ai", 1), al("ai", 128), al("ai", 144), al("ai", 256), al("ai", 256)
+    op("G", lambda: [g.iota(ap(ioq), [[0, 1]], 0, 1)], 140, [], [ioq])
+    op("G", lambda: [g.iota(ap(pc), [[0, 16], [1, 16]], 0, 0)], 650, [], [pc])
+    op("G", lambda: [g.iota(ap(gc), [[0, 2], [1, 8], [0, 16]], 0, 0)], 650, [], [gc])
+    op("G", lambda: [g.iota(ap(ioc), [[1, 128]], 0, 0)], 400, [], [ioc])
+    op("G", lambda: [g.iota(ap(iow), [[1, 144]], -15, 0)], 420, [], [iow])
+    op("G", lambda: [g.iota(T.trip[:, :], [[0, 2048]], 0, 0, allow_small_or_imprecise_dtypes=True)], 4300, [ioq, pc, gc, ioc, iow], ["trip0"])
+    pqi, gqi = al("ai", 1), al("ai", 1)
+    qf, pq, gq, q16, q0, p16, dum = [al("af", 1) for _ in range(7)]
+    vts(pqi, ioq, 15, None, OP.bitwise_and)
+    vts(gqi, ioq, 4, None, OP.logical_shift_right)
+    vts(qf, ioq, 1.0, None, OP.mult)
+    vts(pq, pqi, 1.0, None, OP.mult)
+    vts(gq, gqi, 1.0, None, OP.mult)
+    vts(q16, ioq, 16.0, None, OP.mult)
+    i32, bo32, diag, wsel, wone = al("af", 128), al("af", 256), al("af", 256), al("af", 144), al("ab", 144)
+    vts(i32, ioc, ap(qf), None, OP.is_equal, r=[qf])
+    vts(bo32, gc, ap(gq), None, OP.is_equal, r=[gq])
+    vts(diag, pc, ap(pq), None, OP.is_equal, r=[pq])
+    vts(wsel, iow, ap(q16), None, OP.is_equal, r=[q16])
+    vts(q0, pq, 1000.0, ap(qf), OP.mult, OP.add, r=[qf])
+    vts(wone, iow, ap(q0), None, OP.is_equal, r=[q0])
+
+    def scaled(src, w, k, arena="ab"):
+        b = al(arena, w)
+        sact(b, src, scale=float(k))
+        return b
+    bo, bow, bo16, bo16n, bo32b = [scaled(bo32, 128, k) for k in (1, -W19, 16, -16, 32)]
+    ib, ineg, i16n, ihalf, iquar, i8n, iw = [scaled(i32, 128, k) for k in (1, -1, -16, 0.5, -0.25, -8192, -W19)]
+    bo8n, bo8p, i32n = scaled(bo32, 256, -8192), scaled(bo32, 256, 8192), scaled(i32, 128, -1, "af")
+    ring = al("ab", 4112)
+    for a, b in ((0, 256), (256, 512), (512, 1024), (1024, 2048), (2048, 4096), (4096, 4112)):
+        flex(lambda e, _, a=a, b=b: [act(e, ap(ring, a, b), ap(ring, 0, b - a) if a else ap(diag))], sc(b - a), vc(b - a, 0.5 if a else 1.0), [diag, ring], [ring])
+    ones, d0, d0a = al("ab", 256), al("af", 128), al("af", 128)
+    op("V", lambda: [V.memset(ap(ones), 1.0)], vc(256, 0.5), [], [ones])
+    op("V", lambda: [V.memset(T.fw[:, VOID0:FEAT0], 16384.0), V.memset(T.tab0[:, 2048:MEM0], 0.0), V.memset(T.tab0[:, MEM0 + 2048:2 * MEM0], 0.0)],
+       3 * vc(16), [], ["void", "pad0"])
+    pc1 = [pc[0], pc[1], 128, pc[3]]
+    bo1 = [bo32[0], bo32[1], 128, bo32[3]]
+    vts(d0a, pc1, 0.0, 2.0 ** 23 + 1, OP.is_equal, OP.mult)
+    sact(d0, d0a, bias=-1.0)
+    pa, pb, pcf, par, tra, trf = al("ai", 128), al("ai", 128), al("af", 128), al("ab", 128), al("af", 128), al("af", 128)
+    vts(pa, pc1, ap(pq), None, OP.add, r=[pq])
+    vts(pb, pa, 1, None, OP.bitwise_and)
+    vts(pcf, pb, -1.0, 8192.0, OP.add, OP.mult)
+    vtt(par, pcf, bo1, OP.mult)
+    vts(tra, pc1, ap(pq), None, OP.is_gt, r=[pq])
+    vtt(trf, tra, bo1, OP.mult)
+    op("S", lambda: [S.activation(T.trip[:, 16 * k:16 * k + 129 * 15 + 1:129], ap(trf, 16 * k, 16 * k + 16), AF.Identity) for k in range(8)],
+       8 * sc(16), ["trip0", trf], ["trip"])
+    c16, c8 = [ioc[0], ioc[1], 16, ioc[3]], [ioc[0], ioc[1], 8, ioc[3]]
+    l_end, l_col, l_oh, l_rec = [al("au", 16) for _ in range(4)]
+    ca, cb, cc, cd, lane8 = al("ai", 16), al("ai", 16), al("af", 16), al("af", 16), al("af", 8)
+    vts(l_end, c16, 16.0, 15.0, OP.mult, OP.add)
+    vts(l_col, c16, 1.0, None, OP.mult)
+    vts(p16, pq, 16.0, None, OP.mult)
+    vts(ca, c16, 1, None, OP.logical_shift_right)
+    vts(cb, c16, 1, None, OP.bitwise_and)
+    vts(l_oh, ca, 256.0, ap(p16), OP.mult, OP.add, r=[p16])
+    vts(cc, cb, -8.0, 16.0, OP.mult, OP.add)
+    vtt(cd, cc, ca, OP.add)
+    vts(l_rec, cd, 1.0, None, OP.mult)
+    vts(lane8, c8, 16.0, ap(pq), OP.mult, OP.add, r=[pq])
+    vts(dum, pq, 2048.0, None, OP.add)
+    xc, colr = {}, {}
+    for t in range(RO):
+        colr[t] = al("af", 1)
+        sact(colr[t], pq, bias=float(t))
+        for h in range(NH):
+            xc[t, h] = al("af", 8)
+            sact(xc[t, h], lane8, bias=-float(FEAT0 - strip(t, h) + 2048))
+
+    for q in range(2):
+        a, b = 1024 * q, 1024 * q + 1024
+        op("V", lambda a=a, b=b: [ts(T.lmt[:, a:b], T.lmi[:, a:b], 4095, None, OP.bitwise_and)], vc(1024), ["lmi%d" % q], ["lmt%d" % q])
+        op("V", lambda a=a, b=b: [ts(T.tab0[:, MEM0 + a:MEM0 + b], T.lmt[:, a:b], -2048.0, None, OP.add)], vc(1024), ["lmt%d" % q], ["mem0%d" % q])
+        op("V", lambda a=a, b=b: [V.tensor_copy(T.tab0[:, a:b], T.lmi[:, a:b])], vc(1024), ["lmi%d" % q], ["rec0%d" % q])
+    svf, th16, ea, eb = al("af", 768), al("af", 16), al("ah", 512), al("ah", 512)
+    op("V", lambda: [V.tensor_copy(ap(svf, p1=8), ap(svt, p1=8))], vc(768), [svt], [svf])
+    t0 = tile()
+    mm(t0, [(0, 48, 1, ap(wsel, 15 - p, 143 - p, p1=8), ap(svf, p, 768, 16, p1=8), p == 0, p == 15) for p in range(16)], 16 * 256, [wsel, svf])
+    sv = {(t, h): al("af", 24) for t in range(RO) for h in range(NH)}
+    pm = {(t, h): al("ah", 256) for t in range(RO) for h in range(NH)}
+    for h in range(NH):
+        op("V", lambda h=h: [V.tensor_copy(ap(sv[0, h], 0, 8), ps(t0, 8 * h, 8 * h + 8)),
+                             ts(ap(sv[0, h], 8, 16), ps(t0, 16 + 8 * h, 24 + 8 * h), -2048.0, None, OP.add)], 2 * vc(8), [], [sv[0, h]], [t0])
+    op("V", lambda: [ts(ap(th16), ps(t0, 32, 48), 16.0, -15.0, OP.mult, OP.add)], vc(16), [], [th16], [t0])
+    vts(ea, lpq, 0.0, 2047.0, OP.min, OP.mult)
+    vts(eb, lpq, -2048.0, -2048.0, OP.add, OP.max)
+    for h in range(NH):
+        tl = tile()
+        mm(tl, [(128 * m, 128 * m + 128, 1, ap(e, 256 * m + H * h, 256 * m + H * h + H), ap(ib), e is ea, e is eb) for m in range(2) for e in (ea, eb)],
+           512, [ea, eb, ib])
+        op("V", lambda h=h, tl=tl: [V.tensor_copy(ap(pm[0, h]), ps(tl, 0, 256))], vc(256), [], [pm[0, h]], [tl])
+
+    mask = {(u, h): al("ab", 2048) for u in range(2) for h in range(NH)}
+    gm = {h: al("ah", 2048) for h in range(NH)}
+    gn = {h: al("ah", 2048) for h in range(NH)}
+    sg = {h: al("ab", 2048) for h in range(NH)}
+    fb = {h: al("ab", 2048) for h in range(NH)}
+
+    def spread(o, src, r, cols, lst):
+        def fn(e, _):
+            if e == "V":
+                return [V.tensor_tensor(ap(o), ap(src).indirect(ap(lst, 0, len(cols))), ap(diag, 0, o[2]), OP.mult)]
+            return [S.activation(ap(o, 16 * c, 16 * c + 16), ap(diag, 0, 16), AF.Identity, scale=ap(src, x, x + 1)) for c, x in enumerate(cols)]
+        flex(fn, len(cols) * sc(16), 60 + o[2] * GA, r + [lst, diag], [o])
+
+    def members(dst, win, rw, lst, mk, tab, MEM):
+        a = al("au", H)
+        op("V", lambda: [ts(ap(a), win.indirect(ap(lst)), 1.0 / 4096, -0.5 + 1.0 / 8192, OP.mult, OP.add)], 60 + H * GA, rw + [lst], [a])
+        for q in range(2):
+            op("V", lambda q=q: [V.tensor_tensor(ap(dst, 1024 * q, 1024 * q + 1024), tab[:, MEM0:MEM0 + 2048].indirect(ap(a, 64 * q, 64 * q + 64)),
+                                                 ap(mk, 1024 * q, 1024 * q + 1024), OP.mult)],
+               60 + 1024 * GA, MEM + [a, sub(mk, q)], [sub(dst, q)])
+
+    def compare(src, other, okey, h, after):
+        for b in range(4):
+            tl = tile()
+            calls = []
+            for u in range(4):
+                calls.append((128 * u, 128 * u + 128, 1, ap(bo), ap(src, 4 * b + u, 2048, 16), True, False))
+                calls.append((128 * u, 128 * u + 128, 1, other, ap(ineg), False, True))
+            mm(tl, calls, 1024, [bo, ineg, okey, sub(src, 0), sub(src, 1)])
+            flex(lambda e, _, b=b, tl=tl: [act(e, ap(sg[h], 512 * b, 512 * b + 512), ps(tl, 0, 512), AF.Sigmoid, -math.log(63.0), 64.0)],
+                 sc(512), vc(512), [], [sub(sg[h], b)], [tl])
+            after(b)
+
+    def settle(tl, w, o, rr, other, h):
+        rounded(ap(rr), rr, tl, w, MAGIC, tmp("r1%d" % w, h, w))
+        if FOLD:
+            mm(tl, [(0, w, 1, ap(ineg), ap(rr), False, True)], w, [ineg, rr])
+            op("V", lambda: [V.tensor_tensor(ap(o), ps(tl, 0, w), ap(other), OP.max)], vc(w), [other], [o], [tl])
+        else:
+            op("V", lambda: [V.tensor_tensor(ap(other), ps(tl, 0, w), ap(rr), OP.subtract)], vc(w), [rr], [other], [tl])
+            op("V", lambda: [V.tensor_tensor(ap(o), ps(tl, w, 2 * w), ap(other), OP.max)], vc(w), [other], [o], [tl])
+
+    def half(t, h, tab, MEM, REC, PAD, thr, xout):
+        last = t == RO - 1
+        mk, db, xk, x, s_ = mask[t % 2, h], sg[h], "x%d%d" % (t, h), xap(t, h), sv[t, h]
+        both = lambda b: [sub(b, 0), sub(b, 1)]
+        tj = tile()
+        mm(tj, [(0, H, 1, ap(bo), x, True, True)], 128, [bo, xk])
+        ji = al("au", H)
+        op("V", lambda: [ts(ap(ji), ps(tj, 0, H), ap(colr[t]), None, OP.add)], vc(H), [colr[t]], [ji], [tj])
+        for q in range(2):
+            pick(mk, 1024 * q, 1024 * q + 1024, ap(ring), ji, 64 * q, 64 * q + 64, [ring], [sub(mk, q)])
+        su = al("au", 8)
+        op("V", lambda: [V.tensor_copy(ap(su), ap(s_, 0, 8))], vc(8), [s_], [su])
+        if t == 0:
+            members(gm[h], T.lmi[:, :], ["lmi0", "lmi1"], su, mk, tab, MEM)
+        else:
+            members(gm[h], tab[:, 0:2048], REC, su, mk, tab, MEM)
+        ty = tile()
+        mm(ty, [(H, 2 * H, 1, ap(ib), ap(pm[t, h], 0, H), True, False), (H, 2 * H, 1, ap(mk, 0, 2048, 16), ap(par), False, True)], 256,
+           [ib, par, pm[t, h], sub(gm[h], 0)] + both(mk))
+        val, pf = tmp("val", h, H, "ab"), tmp("pf", h, H)
+        flex(lambda e, _: [act(e, ap(val), ps(ty, H, 2 * H), AF.Relu, 3000.0)], sc(H), vc(H), [], [val], [ty])
+        if FOLD:
+            flex(lambda e, _: [act(e, ap(pf), ps(ty, H, 2 * H))], sc(H), vc(H), [], [pf], [ty])
+        mm(ty, [(0, H, 1, ap(i16n), ap(val), True, False)] + [(k, H, 16, ap(gm[h], k, 2048, 16), ap(bo, 0, 128, 16), False, False) for k in range(16)],
+           128 + 1024, [i16n, val, bo] + both(gm[h]))
+        compare(gm[h], ap(pm[t, h], H, 2 * H), pm[t, h], h, lambda b: mm(
+            ty, [(k, H, 16, ap(sg[h], H * k, H * k + H), ap(bow, 0, 128, 16), False, k == 15 and not FOLD) for k in range(4 * b, 4 * b + 4)], 256, [bow, sub(sg[h], b)]))
+        nl, nu = al("ah", H), al("au", H)
+        settle(ty, H, nl, tmp("rr", h, H, "ab" if FOLD else "af"), pf, h)
+        tn = tile()
+        mm(tn, [(0, H, 1, ap(nl), ap(ib), True, True)], 128, [nl, ib])
+        op("V", lambda: [ts(ap(nu), ps(tn, 0, H), 2064.0, 0.0, OP.add, OP.max)], vc(H), [], [nu], [tn])
+        for q in range(2):
+            pick(fb[h], 1024 * q, 1024 * q + 1024, T.fw[:, VOID0:FEAT0 + 4096], nu, 64 * q, 64 * q + 64, ["void", "feat"], [sub(fb[h], q)])
+        td = tile()
+        mm(td, [(H, 2 * H, 1, ap(ib), ap(nl), True, True)], 128, [nl, ib])
+        if BY_MAX[h]:
+            txp = tile()
+            mm(txp, [(0, H, 1, ap(ib), x, True, True)], 128, [ib, xk, sub(fb[h], 0)])
+            mm(td, [(0, H, 1, x, ap(bo16n), True, False)] + [(k, H, 16, ap(fb[h], k, 2048, 16), ap(bo16n, 0, 128, 16), False, False) for k in range(16)],
+               128 + 1024, [bo16n, xk] + both(fb[h]))
+        for b in range(4):
+            ks = range(4 * b, 4 * b + 4)
+            if BY_MAX[h]:
+                op("V", lambda ks=ks: [V.tensor_tensor(ap(db, H * k, H * k + H), ps(txp, 0, H), ap(fb[h], k, 2048, 16), OP.max) for k in ks],
+                   4 * vc(H), both(fb[h]), [sub(db, b)], [txp])
+                mm(td, [(k, H, 16, ap(db, H * k, H * k + H), ap(bo32b, 0, 128, 16), False, k == 15) for k in ks], 256, [bo32b, sub(db, b)])
+            else:
+                tl = tile()
+                calls = []
+                for u in range(4):
+                    calls.append((128 * u, 128 * u + 128, 1, ap(ib), ap(fb[h], 4 * b + u, 2048, 16), True, False))
+                    calls.append((128 * u, 128 * u + 128, 1, ap(ineg), x, False, True))
+                mm(tl, calls, 1024, [ib, ineg, xk] + both(fb[h]))
+                op("S", lambda b=b, tl=tl: [S.activation(ap(db, 512 * b, 512 * b + 512), ps(tl, 0, 512), AF.Abs)], sc(512), [], [sub(db, b)], [tl])
+                mm(td, [(k, H, 16, ap(db, H * k, H * k + H), ap(bo16, 0, 128, 16), True, True) for k in ks], 256, [bo16, sub(db, b)])
+        sp2, tk, nt, z, lo = tmp("sp2", h, 256), tmp("tk", h, H), tmp("nt", h, H), tmp("z", h, H), tmp("lo", h, 256)
+        op("V", lambda: [V.tensor_tensor_scan(ap(sp2, 0, H), ap(d0), ps(td, 0, H), 0.0, OP.add, OP.min)], vc(H), [d0], [sub(sp2, 0)], [td])
+        op("V", lambda: [V.tensor_tensor(ap(tk), ps(td, 0, H), ap(sp2, 0, H), OP.is_equal)], vc(H), [sub(sp2, 0)], [tk], [td])
+        sact(nt, tk, bias=1.0, scale=-1.0)
+        op("V", lambda: [V.tensor_tensor(ap(z), ps(td, H, 2 * H), ap(tk), OP.mult)], vc(H), [tk], [z], [td])
+        op("V", lambda: [V.tensor_tensor_scan(ap(sp2, H, 2 * H), ap(nt), ap(z), 0.0, OP.mult, OP.add)], vc(H), [nt, z], [sub(sp2, 1)])
+        spread(lo, sp2, both(sp2), [16 * c + 15 for c in range(16)], l_end)
+        to = tile()
+        mm(to, [(8 * m, 8 * m + 8, 1, ap(lo, H * m, H * m + H), ap(bo32, 0, 128, 16), True, True) for m in range(2)], 512, [lo, bo32])
+        o1, of, osn, far = al("af", 8), al("au", 8), al("au", 8), al("af", 8)
+        op("V", lambda: [ts(ap(osn), ps(to, 8, 16), 2048.0, 0.0, OP.add, OP.max),
+                         V.tensor_tensor(ap(o1), ps(to, 8, 16), ap(xc[t, h]), OP.max),
+                         V.tensor_tensor(ap(far), ps(to, 0, 8), ap(thr, 8 * h, 8 * h + 8), OP.is_ge)], 3 * vc(8), [xc[t, h], thr], [osn, o1, far], [to])
+        vts(of, o1, float(FEAT0 - strip(t, h) + 2048), None, OP.add)
+        fs = tmp("fs", h, H, "ab")
+        pick(fs, 0, H, T.fw[:, strip(t, h):FEAT0 + 4096], of, 0, 8,
+             ["void", "feat"] + ["x%d%d" % (u, v) for u in range(t + 1) for v in range(NH) if 2 * u + v <= 2 * t + h], [fs])
+        tx = tile()
+        mm(tx, [(0, H, 1, ap(ihalf), x, True, False), (0, H, 1, ap(iquar), ap(ones, 0, H), False, False), (0, H, 1, ap(ihalf), ap(fs), False, True)], 384,
+           [ihalf, iquar, ones, xk, fs])
+        if last:
+            rounded(ap(xout, H * h, H * h + H), sub(xout, h), tx, H, MAGIC1, tmp("x1", h, H))
+        else:
+            x2 = al("ab", H)
+            rounded(ap(x2), x2, tx, H, MAGIC1, tmp("x1", h, H))
+            send(h, xap(t + 1, h), ap(x2), [x2], ["x%d%d" % (t + 1, h)], 32768)
+        sr = al("ah", H)
+        op("V", lambda: [V.tensor_copy(ap(sr), T.snr[:, :].indirect(ap(osn)))], 60 + H * GA, ["snr", osn], [sr])
+        tq = tile()
+        mm(tq, [(0, 8, 1, ap(wone, 15 - p, 143 - p), ap(sr, p, H, 16), p == 0, p == 15) for p in range(16)], 1024, [wone, sr])
+        su2, il, sp, same, ngo = al("au", 8), al("au", 16), al("af", 8), al("af", 8), al("af", 8)
+        op("V", lambda: [V.tensor_copy(ap(su2), ps(tq, 0, 8)), V.tensor_tensor(ap(same), ps(tq, 0, 8), ap(s_, 0, 8), OP.is_equal), V.tensor_copy(ap(sp), ps(tq, 0, 8))],
+           3 * vc(8), [s_], [su2, sp, same], [tq])
+        members(gn[h], tab[:, 0:2048], REC, su2, mk, tab, MEM)
+        op("V", lambda: [ts(ap(il, 0, 16, 2), ap(sp), 0.0, None, OP.add), ts(ap(il, 1, 16, 2), ap(sp), float(MEM0), None, OP.add)], 2 * vc(8), [sp], [il])
+        vtt(ngo, same, far, OP.max)
+        so, kt, ko, u1, u2 = al("af", 16), al("af", 8), al("af", 8), al("af", 8), al("af", 8)
+        sact(kt, ngo, scale=-4096.0)
+        vtt(ko, kt, sp, OP.add)
+        sact(u1, ngo, bias=-4096.0, scale=4096.0)
+        op("V", lambda: [V.tensor_tensor(ap(u2), ap(u1), ap(s_, 0, 8), OP.add)], vc(8), [u1, s_], [u2])
+        op("V", lambda: [V.tensor_tensor(ap(so, 0, 8), ap(ko), ap(u2), OP.max)], vc(8), [ko, u2], [sub(so, 0)])
+        cnt = None
+        if not last:
+            flex(lambda e, _: [act(e, ap(so, 8, 16), ap(s_, 8, 16))], sc(8), vc(8), [s_], [sub(so, 1)])
+            send(h, ap(sv[t + 1, h], 0, 16), ap(so), both(so), [sv[t + 1, h]], 8192)
+            cnt, junk = al("af", 1), al("af", 8)
+            op("S", lambda: [S.activation(ap(junk), ap(ngo), AF.Identity, accum_out=ap(cnt))], sc(8) + 20, [ngo], [junk, cnt])
+        else:
+            tys, ysb = tile(), al("af", H)
+            mm(tys, [(p, H, 16, ap(i32, p, 128, 16), ap(so, 0, 8), True, True, 8) for p in range(16)], 16 * 4 * 8, [i32, sub(so, 0)])
+            flex(lambda e, _: [act(e, ap(ysb, p1=8), ps(tys, 0, H, 1, 8))], sc(H), vc(H), [], [ysb], [tys])
+            dma("Y", [(T.ys[:, H * h:H * h + H], ap(ysb, p1=8))], 4096, r=[ysb])
+        zg, nv = tmp("zg", h, H, "ab"), tmp("nv", h, 256)
+        spread(zg, ngo, [ngo], list(range(8)), l_col)
+        tr = tile()
+        mm(tr, [(256, 512, 1, ap(ib), ap(pm[t, h]), True, False), (256, 512, 1, ap(i8n), ap(ones), False, False), (256, 512, 1, ap(zg), ap(bo8p), False, True)], 768,
+           [ib, i8n, ones, zg, bo8p, pm[t, h], sub(gn[h], 0)])
+        if FOLD:
+            flex(lambda e, _: [act(e, ap(nv), ps(tr, 256, 512))], sc(256), vc(256), [], [nv], [tr])
+        mm(tr, [(0, 256, 1, ap(zg), ap(bo8n), True, False), (0, H, 1, ap(ib), ap(nl), False, False)]
+           + [(H + k, 2 * H, 16, ap(gn[h], k, 2048, 16), ap(bo, 0, 128, 16), False, False) for k in range(16)],
+           384 + 1024, [zg, bo8n, ib, nl, bo] + both(gn[h]))
+
+        def after(b):
+            calls = []
+            for k in range(4 * b, 4 * b + 4):
+                calls.append((H + k, 2 * H, 16, ap(sg[h], H * k, H * k + H), ap(bow, 0, 128, 16), False, False))
+                calls.append((0, H, 1, ap(sg[h], H * k, H * k + H), ap(iw), False, k == 15 and not FOLD))
+            mm(tr, calls, 768, [bow, iw, sub(sg[h], b)])
+        compare(gn[h], ap(nl), nl, h, after)
+        po = al("ah", 256)
+        settle(tr, 256, po, tmp("r2", h, 256, "ab" if FOLD else "af"), nv, h)
+        if not last:
+            send(h, ap(pm[t + 1, h]), ap(po), [po], [pm[t + 1, h]], 65536)
+        else:
+            tf, yo = tile(), al("af", 256)
+            mm(tf, [(H * m, H * m + H, 1, ap(po, H * m, H * m + H), ap(ib), True, True) for m in range(2)], 256, [po, ib])
+            op("V", lambda: [ts(ap(yo), ps(tf, 0, 256), 2048.0, -1.0, OP.add, OP.max)], vc(256), [], [yo], [tf])
+            dma("Y", [(T.yp[:, H * h:H * h + H], ap(yo, 0, H)), (T.yq[:, H * h:H * h + H], ap(yo, H, 2 * H))], 131072, r=[yo])
+        eqb = tmp("eqb", h, H, "ab")
+        op("V", lambda: [V.tensor_tensor(ap(eqb), ap(ko).indirect(ap(l_col, 0, 8)), ap(sr), OP.is_equal)], 60 + H * GA, [ko, sr, l_col], [eqb])
+        tw = tile()
+        mm(tw, [(0, 8, 1, ap(i32), ap(ngo), True, False)] + [(0, 8, 1, T.trip[:, 128 * p:128 * p + 128], ap(eqb, p, H, 16), False, p == 15) for p in range(1, 16)],
+           256 + 960, [i32, ngo, "trip", eqb])
+        w1, w2, wl, ra = al("af", 8), al("af", 8), al("au", 16), al("af", 8)
+        op("V", lambda: [ts(ap(w1), ps(tw, 0, 8), 0.5, ap(dum), OP.is_gt, OP.mult)], vc(8), [dum], [w1], [tw])
+        vtt(w2, w1, sp, OP.max)
+        op("V", lambda: [ts(ap(wl, 0, 16, 2), ap(w2), 0.0, None, OP.add), ts(ap(wl, 1, 16, 2), ap(w2), float(MEM0), None, OP.add)], 2 * vc(8), [w2], [wl])
+        sact(ra, s_, bias=2048.0, scale=4096.0)
+        op("V", lambda: [V.tensor_tensor(ap(s_, 16, 24), ap(ra), ap(s_, 8, 16), OP.add)], vc(8), [ra, s_], [sub(s_, 2)])
+        zr, old, oh, dl = tmp("zr", h, 256), tmp("old", h, 256), tmp("oh", h, 256, "ab"), tmp("dl", h, 256)
+        spread(zr, s_, [s_, sub(s_, 2)], [16 - 8 * (c % 2) + c // 2 for c in range(16)], l_rec)
+        pick(old, 0, 256, tab[:, :], il, 0, 16, REC + MEM + PAD, [old])
+        pick(oh, 0, 256, ap(mk), l_oh, 0, 16, both(mk), [oh])
+        tu = tile()
+        mm(tu, [(0, 256, 1, ap(bo32, 0, 128), ap(zr), True, False)], 1024, [bo32, zr, osn])
+        mm(tu, [(0, 256, 1, ap(i32n), ap(old), False, True)], 1024, [i32n, old])
+        op("V", lambda: [V.tensor_tensor(ap(dl), ps(tu, 0, 256), ap(oh), OP.mult)], vc(256), [oh], [dl], [tu])
+        return wl, old, dl, cnt
+
+    thr = th16
+    xout = al("af", 256)
+    for t in range(RO):
+        last = t == RO - 1
+        u, w = t % 2, 1 - t % 2
+        tab, nxt = T["tab%d" % u], T["tab%d" % w]
+        MEM, REC, PAD = ["mem%d0" % u, "mem%d1" % u], ["rec%d0" % u, "rec%d1" % u], ["pad%d" % u]
+        MEMN, RECN, PADN = ["mem%d0" % w, "mem%d1" % w], ["rec%d0" % w, "rec%d1" % w], ["pad%d" % w]
+        dma("Y", [(nxt[:, a:a + 1032], tab[:, a:a + 1032]) for a in (0, 1032)], 1056768, r=REC + PAD, w=RECN + PADN)
+        if not last:
+            dma("Y", [(nxt[:, a:a + 1032], tab[:, a:a + 1032]) for a in (MEM0, MEM0 + 1032)], 1056768, r=MEM + PAD, w=MEMN + ["padm%d" % w])
+        PAD, PADN = PAD + ["padm%d" % u], PADN + ["padm%d" % w]
+        upd = {}
+        for h in range(NH):
+            cur[0] = (t, h)
+            upd[h] = half(t, h, tab, MEM, REC, PAD, thr, xout)
+        cur[0] = (t, 2)
+        for h in (1, 0):
+            wl, old, dl, _ = upd[h]
+            m = 1 if last else 2
+            for c in range(7, -1, -1):
+                op("V", lambda wl=wl, old=old, dl=dl, c=c, m=m, nxt=nxt: [
+                    V.tensor_tensor(nxt[:, 0:m * MEM0].indirect(ap(wl, 2 * c, 2 * c + m)), ap(old, 32 * c, 32 * c + 16 * m), ap(dl, 32 * c, 32 * c + 16 * m), OP.add)],
+                   60 + 16 * m * SC, [wl, old, dl], RECN + (PADN[:1] if last else MEMN + PADN))
+        if not last:
+            ta = tile()
+            mm(ta, [(0, 1, 1, ap(bo32, 0, 128), ap(upd[h][3]), h == 0, h == 1) for h in range(NH)], 512, [bo32, upd[0][3], upd[1][3]])
+            a1, a2, a3, nthr = al("ai", 1), al("ai", 1), al("af", 1), al("af", 16)
+            op("V", lambda ta=ta, a1=a1: [ts(ap(a1), ps(ta, 0, 1), -1.0, 256.0, OP.mult, OP.add)], vc(1), [], [a1], [ta])
+            vts(a2, a1, 31, None, OP.bitwise_and)
+            vts(a3, a2, 16.0, None, OP.mult)
+            op("S", lambda a3=a3, nthr=nthr: [S.activation(ap(nthr), ap(th16), AF.Identity, bias=ap(a3))], sc(16), [th16, a3], [nthr])
+            thr = nthr
+    dma("Y", [(T.yx[:, :], ap(xout))], 131072, r=[sub(xout, 0), sub(xout, 1)])
+    dma("Y", [(T.ylm[:, a:a + 1024], nxt[:, a:a + 1024]) for a in (0, 1024)], 1048576, r=RECN)
+    return ops
+
+
+def links(ops):
+    lastw, readers = {}, {}
+    succ = [[] for _ in ops]
+    for i, o in enumerate(ops):
+        d = set(lastw[k] for k in o["r"] + o["w"] if k in lastw)
+        for k in o["w"]:
+            d.update(readers.get(k, []))
+        for t in o["t"]:
+            d.update(t["ops"][-1:])
+            t["ops"].append(i)
+        d.discard(i)
+        o["d"] = d
+        for j in d:
+            succ[j].append(i)
+        for k in o["r"]:
+            readers.setdefault(k, []).append(i)
+        for k in o["w"]:
+            lastw[k] = i
+            readers[k] = []
+    return succ
+
+
+def plan(ops, order):
+    n = len(ops)
+    succ = links(ops)
+    assert len(order) == 2 * n
+    rank = [62 * LETTERS.index(order[2 * i]) + LETTERS.index(order[2 * i + 1]) for i in range(n)]
+    for i, o in enumerate(ops):
+        o["flex"] = o["e"] == "F"
+        if o["flex"]:
+            o["e"] = "V" if rank[i] % 2 else "S"
+            o["c"] = o["cost"][o["e"]]
+        if o["k"] == "d" and not o["r"]:
+            rank[i] = i - 10 ** 9
+    left = [len(o["d"]) for o in ops]
+    rdy = [0.0] * n
+    busy = {e: [] for e in "VSPGY"}
+    ready = [i for i in range(n) if left[i] == 0]
+    while ready:
+        i = min(ready, key=lambda j: (rank[j], j))
+        ready.remove(i)
+        o = ops[i]
+        b, st = busy[o["e"]], rdy[i]
+        k = len(b)
+        while k > 0 and b[k - 1][1] > st:
+            k -= 1
+        while k < len(b) and b[k][0] < st + o["c"]:
+            st = max(st, b[k][1])
+            k += 1
+        b.insert(k, (st, st + o["c"]))
+        o["st"] = st
+        for j in succ[i]:
+            e = ops[j]["e"]
+            hop = 0.0 if o["e"] == e == "P" else o["lat"] + (SAME if o["e"] == e else OTHER)
+            rdy[j] = max(rdy[j], st + o["c"] + hop)
+            left[j] -= 1
+            if left[j] == 0:
+                ready.append(j)
+    seq = sorted(range(n), key=lambda i: (ops[i]["st"], i))
+    bank = [None] * 8
+    for i in seq:
+        for t in ops[i]["t"]:
+            if t["bank"] is None:
+                tb, b = min((-1e9 if bank[b] is None else ops[bank[b]]["st"] + ops[bank[b]]["c"], b) for b in range(8))
+                assert tb <= ops[i]["st"]
+                if bank[b] is not None:
+                    ops[i]["d"].add(bank[b])
+                t["bank"] = b
+                bank[b] = t["ops"][-1]
+    return seq, max(o["st"] + o["c"] + o["lat"] for o in ops)
+
+
+def rank_program(g, core, T, topo):
+    if T.rank_of(core) is None:
+        return
+    ops = build(g, core, T, topo)
+    seq, _ = plan(ops, ORDER)
+    queue = {"V": g.vector, "S": g.scalar, "P": g.tensor, "G": g, "Y": g.sync}
+    count, waited, nd = {}, {}, [0]
+    for i in seq:
+        o = ops[i]
+        e = o["e"]
+        need = {}
+        for j in o["d"]:
+            p = ops[j]
+            if p["e"] == "P" and e == "P":
+                continue
+            s, c = p["mark"]
+            need[s] = max(need.get(s, 0), c)
+        for s in sorted(need):
+            if waited.get((e, s), 0) < need[s]:
+                queue[e].wait_ge(T.sem[s], need[s])
+                waited[e, s] = need[s]
+
+        def chain(x, e=e):
+            x.then_inc(T.sem["c" + e], 1)
+            count["c" + e] = count.get("c" + e, 0) + 1
+            queue[e].wait_ge(T.sem["c" + e], count["c" + e])
+            waited[e, "c" + e] = count["c" + e]
+        ins = o["fn"](e, chain) if o["flex"] else o["fn"]()
+        if o["k"] == "r":
+            count["left"] = count.get("left", 0) + o["n"]
+            count[o["sem"]] = o["n"]
+            o["mark"] = (o["sem"], o["n"])
+            continue
+        if o["k"] == "d":
+            s, inc = "d%d" % nd[0], 16
+            nd[0] += 1
+        else:
+            s, inc = "c" + e, 1
+        for x in ins:
+            x.then_inc(T.sem[s], inc)
+            count[s] = count.get(s, 0) + inc
+        o["mark"] = (s, count[s])
+    for s in sorted(count):
+        g.wait_ge(T.sem[s], count[s])

@@ -5,51 +5,44 @@ OP = AluOpType
 AF = ActivationFunctionType
 RO, NH, H = 4, 2, 128
 VOID0, FEAT0 = 1024, 1040
-MEM0 = 2064
+MEM0 = 2080
 W19 = float(2 ** 19)
 MAGIC = 1.5 * 2.0 ** 42
 MAGIC1 = 1.5 * 2.0 ** 23
-FOLD = False
-BY_MAX = [0, 1]
-ORDER = (
-    "000A0E020I0M0Q040y0S081I1K0G0K0U0O100C0i1E1q1c1224231x3c1i1u1a1m2O1y1o0w1e261U1G202F2I2M2c2k1A061S1k2U2Y2s3O1Y2G3q1O180e0s0o2A1W282C0W0a0Y"
-    "0k140q170m0c1Q1M1C0g0u2K2a4Q2e3C4E1g1s2W2o2y302u343w3A3W4g3I2S2i3U362m3G3i46484S4u4a4m504W4c524y5A5I4o5G5O5V5a5e5i5o685u5k6c6o6w6g6u726m70"
-    "786W6k7C7K7O7T7W7Y7c80868K8s92969G8A8E8U8a8o908g8e8j8y9A9O9S3S9W9E8l9KAWA2AEAmAIAcAuAAAQAw9sA6AyB1B6BABG9U9k9u9yA02x3E429I3m8Q9Y9o2Q2g2q3M"
-    "32383K3Y3a414A3s4C4I3k3u4K3o4G4O3y4M4U4Y4e4i4k4q4t4w54585C5E5M5K5S5Q5W5Y5c5g5m5q5s5w5z6062646B6E6L6Q666C6G6S6Y6q6O6M747A6i767I3e7M6a6U6y8c"
-    "7a8M8m7m8q8u848w987G7U9C9M9i9q9w7E7Q7e7g7o3Q44576e3g6I6s7i7s7u7y82888C8G8WA4A8ACAGAKAMASAY9Q9a9e9gAOAgAiAUAkB4AsAaBKBQBeBuByCGCMCSCgC0CACi"
-    "C8CYCmCQCeCqCwCyD2D6DCDIDUD8E8EGEMDwE6EOECEKESE4EAEUEaEcEgEeEqF0FKFQFUFeGWGgGsFSFYFiFoFwGmGOFsG2GIG0GKGSAqGYG4GGGuHWH4HGHkHMHaIEHAHoIMHuIG"
-    "IQIVIYIaIeGiGoH0H6HEB2BCBIGaBSGAGyH87k7q8Y7w8SAeAoBEB8BPBiBYBgBmBMBWBoBUBaBqBcBkBsBxC2C4C6CCCFCICKCOCWCUCcCaCoCkCuCsD0D4DADEDGDKDNDODQDWDb"
-    "DcDjDoDSDYDeDmDyEEDqDkE0EWDsEoEw94F2DuEQEiFgF6FkG6FqG8GEFOGCGMEYEmGcGqH2HwIAEkEuF8FAFC8J8O9mE29cDgEIEyFEFIFMFWFaFcFmGeHKHQHUHYHeHiHqHsGkHC"
-    "HIHcI0I2HyICIIISIgHgIWIiJ0JIJOJeJiK0K8JWJsKAJMJkKCJyK6KGKLKOKQKUKaKgKsKWLSLaLgLKLQLiLYLeLmLMLULoM0M4MBMCMIMQMmMsMwN4NCO2OAMuN0N8NENMO6NoNI"
-    "NUNgNSNiNmI4NsNWNONqPGOmP2PWOKOYPcOwPOPeOcPAPgPjPmPqPuO0O4OGOMOSHmI6IONwJCNQOEOOEsF4GwFGHOI8IKIcIkIxJ4IsJ2J8ImIqJAIoIuJEIyJ6JGJLJQJSJUJYJb"
-    "JcJgJmJoJqJwJuK4K2KIKEKMKSKYKcKeKiKlKmKoKuKzL0L7LCKqKwL2LALELWLsL8LOLqLGM8MEFyMMLkLILcMqNGNYNeMWNcNyMeNAOCLuM6OUOkP8PIPQLwM2MSMUMYFuGQGVLy"
-    "HSL4MKMaMcMgMkMoMyN2N6OIOaOeOiOoOsOyP6PCNaOgOuP4Q4PKPEPUPkPaOqPoQ0QKQaQgRCR0RARKQoRGRSQwR2RUQeRQRaRdRgRiRmRsRwS8RoSiSyT6SYSgT8SmT4TASeSoTC"
-    "TGTITRTMTUTcTyU4UEUKUgUoU8UGUOUSUaVAV0UYUeUwUcV2VKWEWKWOUqV8VuVMVWW4VSVyW8VkW6WAVcVmWCWHWMWQWUWWWaV4VEVIVUVYP0PSPwV6Q6UmVGVOMGMOO8MiOWPMPY"
-    "PsPyQHQOQCQMQSQ2QAQUQ8QEQWQIQQQYQdQiQkQmQqQtQuQyR4R6R8RIRERORMRYRWReRkRqRuRyS0S3S4S6SCSHSISPSASESKSUSaT0SQSSSkSqStTKTaTqUQUWScSwU2TiTuUMTO"
-    "UCUkUUUiUsTYU6UyVCVQVaWIWSWYSuTETSTWTgNKNkNvSWOQSMT2TeTkTmToTsTwU0UAUIVeVgViVoVqVsVwW0UuW2"
-)
-LETTERS = "0123456789ABCDEFGHIJKLMNOPQRSTUVWXYZabcdefghijklmnopqrstuvwxyz"
+LOW = 2.0 ** 23
+CFG = {
+    "pos": {},
+    "on_v": [],
+    "chunks": 2,
+    "same": 90.0, "other": 260.0, "psum": 440.0, "remote": 1200.0,
+    "pe": 0.45, "turns": 1, "rate": 400.0, "double": True,
+}
+
+ORDER = """pe1 pe0- set1r1- setm0 ofu1 jq1- mem1l0 mv0++ distc0+ mem2l1 sp0 x20 cmp1b0- mem1b1 feata1++ cmp1d1- yo0+++ ys1+ mem2a1- mem2l0 thr0 cmp2d1- setpr1+ ofu0 setm1 fs0+ wl0 distb1- sb1 feata0 su1 mem2b0+ mem1b0- distd0+ cmp2b0 up1 mem2b1- set11- x21 sn0 mask0- old0- n00- set10- setp0 su21 osn1- fs1 distd1 wl1 cmp2c1- mem1a1- cmp2a1- cmp1b1- j1-- sr0+ cmp1a0 dista0+ up0+ cmp1c0- of0+ mv1 su0- zg0 vo0 cmp1d0+ cmp1c1- cmp2d0 nu0 scat0+ n01- old1- sr1- scat1- cmp2c0- set1r0- osn0- featb1- setmr0- setp1 distc1 mem1l1- distb0 eqb1 sp1+ mem1a0- cmp2a0- arg1 featb0- cnt0- sb0- su20- ys0++ cmp2b1 setmr1- of1 j0-- nu1- eqb0 jq0-- yo1- mask1-- arg0- mem2a0- setpr0- zg1 dista1- cmp1a1 vo1- sn1-""".split()
+ON_V = """cmp1b0 cmp1c0 cmp1d1 cmp1d3 cmp2b1 cnt2 dista0 dista2 dista3 distb1 distc1 distc3 distd3 eb0 feata2 featb0 fs2 jq1 jq2 jq3 k00 k10 k20 k30 mask1 mem00 mem1l0 nu0 nu2 osn1 osn3 pm00 rec00 sb1 sb3 set1r0 set1r1 set1r2 set1r3 setmr0 setmr2 setmr3 setpr0 setpr2 sh0 sn0 sn1 sn3 sp0 sp3 sr2 sr3 su0 su1 up0 vo2 x22 x23""".split()
+for _i, _x in enumerate(ORDER):
+    CFG["pos"][_x.strip("+-")[:-1], int(_x.strip("+-")[-1])] = _x.count("+") - _x.count("-") + _i / len(ORDER)
+CFG["on_v"] = [(_x[:-1], int(_x[-1])) for _x in ON_V]
 
 SCRATCH = {
     "fw": ("sbuf", [128, FEAT0 + 4096], "bfloat16"),
-    "tab0": ("sbuf", [128, 2 * MEM0], "float32"),
-    "tab1": ("sbuf", [128, 2 * MEM0], "float32"),
+    "tab": ("sbuf", [128, 2 * MEM0], "float32"),
     "lmi": ("sbuf", [128, 2048], "int32"),
     "lmt": ("sbuf", [128, 2048], "int32"),
     "snr": ("sbuf", [128, 4096], "int32"),
-    "trip": ("sbuf", [128, 2048], "bfloat16"),
-    "af": ("sbuf", [128, 12544], "float32"),
-    "ab": ("sbuf", [128, 26400], "bfloat16"),
-    "ah": ("sbuf", [128, 15872], "float16"),
-    "ai": ("sbuf", [128, 2688], "int32"),
-    "au": ("sbuf", [128, 4992], "uint16"),
+    "tab1": ("sbuf", [128, 2 * MEM0], "float32"),
+    "ramp": ("sbuf", [128, 2048], "float32"),
+    "af": ("sbuf", [128, 8704], "float32"),
+    "ab": ("sbuf", [128, 29696], "bfloat16"),
+    "ah": ("sbuf", [128, 18944], "float16"),
+    "ai": ("sbuf", [128, 3072], "int32"),
+    "au": ("sbuf", [128, 5120], "uint16"),
 }
 for _b in range(8):
     SCRATCH["ps%d" % _b] = ("psum", [128, 512], "float32")
-SEMAPHORES = ["cV", "cS", "cP", "cG", "left"] + ["d%d" % i for i in range(40)] + ["a%d" % i for i in range(18)]
+SEMAPHORES = ["cV", "cS", "cP", "cG", "left"] + ["d%d" % i for i in range(40)] + ["a%d" % i for i in range(30)]
 
-CY, PE, GA, SC = 1.0, 0.5, 1.56, 3.8
-SAME, OTHER, REMOTE = 60.0, 110.0, 3000.0
+CY, GA, SC = 0.85, 1.28, 3.1
 
 
 def build(g, core, T, topo):
@@ -58,8 +51,10 @@ def build(g, core, T, topo):
     ops = []
     used = {"af": 0, "ab": 0, "ah": 0, "ai": 0, "au": 0}
     kept = {}
-    cur = [None, None]
+    cur = [(-1, 0)]
     V, S, P = g.vector, g.scalar, g.tensor
+    NC = CFG["chunks"]
+    CW = 2048 // NC
 
     def al(arena, w):
         a = used[arena]
@@ -72,6 +67,9 @@ def build(g, core, T, topo):
             kept[name, h] = al(arena, w)
         return kept[name, h]
 
+    def part(b, lo, w):
+        return [b[0], b[1] + lo, w, b[3]]
+
     def ap(b, lo=0, hi=None, step=1, p1=128):
         hi = b[2] if hi is None else hi
         if step == 1:
@@ -81,25 +79,28 @@ def build(g, core, T, topo):
     def sub(b, q):
         return "%s/%d" % (b[3], q)
 
+    def subs(b, m):
+        return [sub(b, q) for q in range(m)]
+
     def keys(xs):
         return [x if isinstance(x, str) else x[3] for x in xs]
 
-    def op(eng, fn, cost, r=(), w=(), t=(), lat=0.0, kind="c"):
-        ops.append({"e": eng, "fn": fn, "c": float(cost), "r": keys(r), "w": keys(w), "t": list(t), "lat": lat, "k": kind, "tv": cur[0], "stage": cur[1]})
+    def op(eng, fn, cost, r=(), w=(), t=(), lat=0.0, kind="c", name=""):
+        ops.append({"e": eng, "fn": fn, "c": float(cost), "r": keys(r), "w": keys(w) + list(t), "lat": lat, "k": kind, "tv": cur[0], "name": name, "flex": False, "free": False})
 
-    def tile():
-        return {"bank": None, "ops": []}
+    def tile(kind):
+        return "ps%d" % (4 * (cur[0][1] % 2) + kind)
 
     def ps(t, lo, hi, step=1, p1=128):
         if step == 1:
-            return T["ps%d" % t["bank"]][0:p1, lo:hi]
-        return T["ps%d" % t["bank"]][0:p1, lo:hi:step]
+            return T[t][0:p1, lo:hi]
+        return T[t][0:p1, lo:hi:step]
 
     def vc(w, rate=1.0):
-        return 15 + max(64, w * rate) * CY
+        return 5 + max(64, w * rate) * CY
 
     def sc(w):
-        return 60 + w * CY
+        return 50 + w * CY
 
     def ts(out, in0, s1, s2, o0, o1=None):
         if o1 is None:
@@ -109,8 +110,11 @@ def build(g, core, T, topo):
     def vts(o, i, s1, s2, o0, o1=None, r=()):
         op("V", lambda: [ts(ap(o), ap(i), s1, s2, o0, o1)], vc(o[2]), [i] + list(r), [o])
 
-    def vtt(o, a, b, o0):
-        op("V", lambda: [V.tensor_tensor(ap(o), ap(a), ap(b), o0)], vc(o[2], 2.0), [a, b], [o])
+    def v1(name, fn, w, r, wr, t=(), rate=1.0):
+        op("V", lambda: [fn()], vc(w, rate), r, wr, t, name=name)
+
+    def gat(name, fn, w, r, wr):
+        op("V", lambda: [fn()], 60 + w * GA, r, wr, name=name)
 
     def act(e, o, i, func=AF.Identity, bias=0.0, scale=1.0):
         if e == "S":
@@ -119,42 +123,47 @@ def build(g, core, T, topo):
             return ts(o, i, 0.0, 1.0 / 64, OP.is_equal, OP.mult)
         if func == AF.Relu:
             return ts(o, i, bias, 0.0, OP.add, OP.max)
-        if bias == 0.0 and scale == 1.0:
-            return V.tensor_copy(o, i)
         return ts(o, i, scale, bias, OP.mult, OP.add)
 
-    def flex(fn, cs, cv, r=(), w=(), t=()):
-        op("F", fn, min(cs, cv), r, w, t)
-        ops[-1]["cost"] = {"S": cs, "V": cv}
+    def engine(name, h=None):
+        return "V" if (name, cur[0][1] + 2 * (cur[0][0] == 0) if h is None else h) in CFG["on_v"] else "S"
 
-    def sact(o, i, bias=0.0, scale=1.0):
-        flex(lambda e, _: [act(e, ap(o), ap(i, 0, o[2]), AF.Identity, bias, scale)], sc(o[2]), vc(o[2]), [i], [o])
+    def flex(name, fn, cs, cv, r=(), w=(), t=()):
+        e = engine(name)
+        op(e, fn, cs if e == "S" else cv, r, w, t, name=name)
+        ops[-1]["flex"] = True
 
-    def pick(o, lo, hi, win, lst, a, b, r, w):
-        flex(lambda e, _: [act(e, ap(o, lo, hi), win.indirect(ap(lst, a, b)))], 75 + (hi - lo) * GA, 60 + (hi - lo) * GA, r + [lst], w)
+    def lin(name, o, i, n_, r, w, t=(), func=AF.Identity, bias=0.0, scale=1.0):
+        flex(name, lambda e, _: [act(e, o, i() if t else i, func, bias, scale)], sc(n_), vc(n_), r, w, t)
 
-    def rounded(o, okey, tl, w, magic, r1):
+    def sact(o, i, bias=0.0, scale=1.0, r=()):
+        op("S", lambda: [S.activation(ap(o), ap(i, 0, o[2]), AF.Identity, bias=bias, scale=scale)], sc(o[2]), [i] + list(r), [o])
+
+    def pick(name, o, lo, hi, win, lst, a, b, r, w):
+        flex(name, lambda e, _: [act(e, ap(o, lo, hi), win.indirect(ap(lst, a, b)))], 75 + (hi - lo) * GA, 60 + (hi - lo) * GA, r + [lst], w)
+
+    def rounded(name, o, okey, tl, w, magic, r1, lo=0):
         def fn(e, chain):
             if e == "V":
-                return [ts(o, ps(tl, 0, w), magic, -magic, OP.add, OP.add)]
-            chain(S.activation(ap(r1), ps(tl, 0, w), AF.Identity, bias=magic))
+                return [ts(o, ps(tl, lo, lo + w), magic, -magic, OP.add, OP.add)]
+            chain(S.activation(ap(r1), ps(tl, lo, lo + w), AF.Identity, bias=magic))
             return [S.activation(o, ap(r1), AF.Identity, bias=-magic)]
-        flex(fn, 2 * sc(w) + 60, vc(w), [], [okey, r1], [tl])
+        flex(name, fn, 2 * sc(w) + 60, vc(w), [], [okey, r1], [tl])
 
-    def mm(t, calls, cyc, r):
+    def mm(t, calls, cyc, r, name=""):
         def fn():
             last = None
             for c in calls:
                 last = P.matmul(ps(t, c[0], c[1], c[2], c[7] if len(c) > 7 else 128), c[3], c[4], c[5], c[6])
             return [last]
-        op("P", fn, 20 + cyc * PE, r, [], [t])
+        op("P", fn, 10 + cyc * CFG["pe"], r, [], [t], name=name)
 
     clock = [1500.0]
 
     def dma(q, pairs, nbytes, r=(), w=()):
-        clock[0] += nbytes / 250.0
+        clock[0] += nbytes / CFG["rate"] if not r else 0.0
         eng = g.sync if q == "Y" else g.scalar
-        op(q, lambda: [eng.dma_start(o, i) for o, i in pairs], 60 * len(pairs), r, w, lat=(clock[0] if not r else 2000 + nbytes / 250.0), kind="d")
+        op(q, lambda: [eng.dma_start(o, i) for o, i in pairs], 60 * len(pairs), r, w, lat=(clock[0] if not r else 1500 + nbytes / CFG["rate"]), kind="d")
 
     arr = [0]
 
@@ -165,7 +174,7 @@ def build(g, core, T, topo):
         m = sum(1 << e for e in eng)
         sem = "a%d" % arr[0]
         arr[0] += 1
-        op("G", lambda: [g.remote_dma(out, in_, T.sem[sem], T.sem.left, pid, rid, m)], 400, r, w, lat=REMOTE + nbytes / 50.0, kind="r")
+        op("G", lambda: [g.remote_dma(out, in_, T.sem[sem], T.sem.left, pid, rid, m)], 400, r, w, lat=CFG["remote"] + nbytes / 50.0, kind="r", name="send")
         ops[-1]["sem"] = sem
         ops[-1]["n"] = len(eng)
 
@@ -175,109 +184,131 @@ def build(g, core, T, topo):
     def xap(t, h):
         return T.fw[:, strip(t, h):strip(t, h) + H]
 
-    svt, lpq = al("ai", 768), al("ai", 512)
-    dma("Y", [(ap(svt, 0, 256, p1=8), T.ls[:, :]), (ap(svt, 256, 512, p1=8), T.lv[:, :]), (ap(svt, 512, 768, p1=8), T.th[:, :])], 24576, w=[svt])
-    dma("Y", [(xap(0, h), T.lx[:, H * h:H * h + H]) for h in range(NH)], 65536, w=["x00", "x01"])
-    for q in range(2):
-        dma("Y" if q == 0 else "S", [(T.lmi[:, 1024 * q:1024 * q + 1024], T.lm[:, 1024 * q:1024 * q + 1024])], 524288, w=["lmi%d" % q])
+    s0, vt0, lpq = al("ai", 256), al("ai", 512), al("ai", 512)
+    dma("Y", [(ap(s0, p1=8), T.ls[:, :])], 8192, w=[s0])
+    dma("S", [(xap(0, h), T.lx[:, H * h:H * h + H]) for h in range(NH)], 65536, w=["x00", "x01"])
+    for q in range(4):
+        dma("YS"[q % 2], [(T.lmi[:, 512 * q:512 * q + 512], T.lm[:, 512 * q:512 * q + 512])], 262144, w=["lmi%d" % q])
     dma("Y", [(ap(lpq, 0, 256), T.lp[:, :]), (ap(lpq, 256, 512), T.lq[:, :])], 262144, w=[lpq])
     dma("Y", [(T.fw[:, FEAT0:FEAT0 + 4096], T.feat[:, :])], 1048576, w=["feat"])
+    dma("Y", [(ap(vt0, 0, 256, p1=8), T.lv[:, :]), (ap(vt0, 256, 512, p1=8), T.th[:, :])], 16384, w=[vt0])
     dma("Y", [(T.snr[i:128:16, :], T.sn[:, :]) for i in range(16)], 2097152, w=["snr"])
 
-    ioq, ioc, iow, gc, pc = al("ai", 1), al("ai", 128), al("ai", 144), al("ai", 256), al("ai", 256)
-    op("G", lambda: [g.iota(ap(ioq), [[0, 1]], 0, 1)], 140, [], [ioq])
-    op("G", lambda: [g.iota(ap(pc), [[0, 16], [1, 16]], 0, 0)], 650, [], [pc])
-    op("G", lambda: [g.iota(ap(gc), [[0, 2], [1, 8], [0, 16]], 0, 0)], 650, [], [gc])
-    op("G", lambda: [g.iota(ap(ioc), [[1, 128]], 0, 0)], 400, [], [ioc])
-    op("G", lambda: [g.iota(ap(iow), [[1, 144]], -15, 0)], 420, [], [iow])
-    op("G", lambda: [g.iota(T.trip[:, :], [[0, 2048]], 0, 0, allow_small_or_imprecise_dtypes=True)], 4300, [ioq, pc, gc, ioc, iow], ["trip0"])
-    pqi, gqi = al("ai", 1), al("ai", 1)
-    qf, pq, gq, q16, q0, p16, dum = [al("af", 1) for _ in range(7)]
-    vts(pqi, ioq, 15, None, OP.bitwise_and)
-    vts(gqi, ioq, 4, None, OP.logical_shift_right)
-    vts(qf, ioq, 1.0, None, OP.mult)
-    vts(pq, pqi, 1.0, None, OP.mult)
-    vts(gq, gqi, 1.0, None, OP.mult)
-    vts(q16, ioq, 16.0, None, OP.mult)
-    i32, bo32, diag, wsel, wone = al("af", 128), al("af", 256), al("af", 256), al("af", 144), al("ab", 144)
-    vts(i32, ioc, ap(qf), None, OP.is_equal, r=[qf])
-    vts(bo32, gc, ap(gq), None, OP.is_equal, r=[gq])
-    vts(diag, pc, ap(pq), None, OP.is_equal, r=[pq])
-    vts(wsel, iow, ap(q16), None, OP.is_equal, r=[q16])
-    vts(q0, pq, 1000.0, ap(qf), OP.mult, OP.add, r=[qf])
-    vts(wone, iow, ap(q0), None, OP.is_equal, r=[q0])
-
-    def scaled(src, w, k, arena="ab"):
-        b = al(arena, w)
-        sact(b, src, scale=float(k))
+    def iota(arena, pat, base, cm):
+        b = al(arena, math.prod(c for _, c in pat))
+        if arena == "ai":
+            op("G", lambda: [g.iota(ap(b), pat, base, cm)], 130 + 2 * b[2], [], [b])
+        else:
+            op("G", lambda: [g.iota(ap(b), pat, base, cm, allow_small_or_imprecise_dtypes=True)], 130 + 2 * b[2], [], [b])
         return b
-    bo, bow, bo16, bo16n, bo32b = [scaled(bo32, 128, k) for k in (1, -W19, 16, -16, 32)]
-    ib, ineg, i16n, ihalf, iquar, i8n, iw = [scaled(i32, 128, k) for k in (1, -1, -16, 0.5, -0.25, -8192, -W19)]
-    bo8n, bo8p, i32n = scaled(bo32, 256, -8192), scaled(bo32, 256, 8192), scaled(i32, 128, -1, "af")
-    ring = al("ab", 4112)
-    for a, b in ((0, 256), (256, 512), (512, 1024), (1024, 2048), (2048, 4096), (4096, 4112)):
-        flex(lambda e, _, a=a, b=b: [act(e, ap(ring, a, b), ap(ring, 0, b - a) if a else ap(diag))], sc(b - a), vc(b - a, 0.5 if a else 1.0), [diag, ring], [ring])
-    ones, d0, d0a = al("ab", 256), al("af", 128), al("af", 128)
-    op("V", lambda: [V.memset(ap(ones), 1.0)], vc(256, 0.5), [], [ones])
-    op("V", lambda: [V.memset(T.fw[:, VOID0:FEAT0], 16384.0), V.memset(T.tab0[:, 2048:MEM0], 0.0), V.memset(T.tab0[:, MEM0 + 2048:2 * MEM0], 0.0)],
-       3 * vc(16), [], ["void", "pad0"])
-    pc1 = [pc[0], pc[1], 128, pc[3]]
-    bo1 = [bo32[0], bo32[1], 128, bo32[3]]
-    vts(d0a, pc1, 0.0, 2.0 ** 23 + 1, OP.is_equal, OP.mult)
-    sact(d0, d0a, bias=-1.0)
-    pa, pb, pcf, par, tra, trf = al("ai", 128), al("ai", 128), al("af", 128), al("ab", 128), al("af", 128), al("af", 128)
-    vts(pa, pc1, ap(pq), None, OP.add, r=[pq])
-    vts(pb, pa, 1, None, OP.bitwise_and)
-    vts(pcf, pb, -1.0, 8192.0, OP.add, OP.mult)
-    vtt(par, pcf, bo1, OP.mult)
-    vts(tra, pc1, ap(pq), None, OP.is_gt, r=[pq])
-    vtt(trf, tra, bo1, OP.mult)
-    op("S", lambda: [S.activation(T.trip[:, 16 * k:16 * k + 129 * 15 + 1:129], ap(trf, 16 * k, 16 * k + 16), AF.Identity) for k in range(8)],
-       8 * sc(16), ["trip0", trf], ["trip"])
-    c16, c8 = [ioc[0], ioc[1], 16, ioc[3]], [ioc[0], ioc[1], 8, ioc[3]]
-    l_end, l_col, l_oh, l_rec = [al("au", 16) for _ in range(4)]
-    ca, cb, cc, cd, lane8 = al("ai", 16), al("ai", 16), al("af", 16), al("af", 16), al("af", 8)
-    vts(l_end, c16, 16.0, 15.0, OP.mult, OP.add)
-    vts(l_col, c16, 1.0, None, OP.mult)
-    vts(p16, pq, 16.0, None, OP.mult)
-    vts(ca, c16, 1, None, OP.logical_shift_right)
-    vts(cb, c16, 1, None, OP.bitwise_and)
-    vts(l_oh, ca, 256.0, ap(p16), OP.mult, OP.add, r=[p16])
-    vts(cc, cb, -8.0, 16.0, OP.mult, OP.add)
-    vtt(cd, cc, ca, OP.add)
-    vts(l_rec, cd, 1.0, None, OP.mult)
-    vts(lane8, c8, 16.0, ap(pq), OP.mult, OP.add, r=[pq])
-    vts(dum, pq, 2048.0, None, OP.add)
-    xc, colr = {}, {}
-    for t in range(RO):
-        colr[t] = al("af", 1)
-        sact(colr[t], pq, bias=float(t))
-        for h in range(NH):
-            xc[t, h] = al("af", 8)
-            sact(xc[t, h], lane8, bias=-float(FEAT0 - strip(t, h) + 2048))
 
-    for q in range(2):
-        a, b = 1024 * q, 1024 * q + 1024
-        op("V", lambda a=a, b=b: [ts(T.lmt[:, a:b], T.lmi[:, a:b], 4095, None, OP.bitwise_and)], vc(1024), ["lmi%d" % q], ["lmt%d" % q])
-        op("V", lambda a=a, b=b: [ts(T.tab0[:, MEM0 + a:MEM0 + b], T.lmt[:, a:b], -2048.0, None, OP.add)], vc(1024), ["lmt%d" % q], ["mem0%d" % q])
-        op("V", lambda a=a, b=b: [V.tensor_copy(T.tab0[:, a:b], T.lmi[:, a:b])], vc(1024), ["lmi%d" % q], ["rec0%d" % q])
-    svf, th16, ea, eb = al("af", 768), al("af", 16), al("ah", 512), al("ah", 512)
-    op("V", lambda: [V.tensor_copy(ap(svf, p1=8), ap(svt, p1=8))], vc(768), [svt], [svf])
-    t0 = tile()
-    mm(t0, [(0, 48, 1, ap(wsel, 15 - p, 143 - p, p1=8), ap(svf, p, 768, 16, p1=8), p == 0, p == 15) for p in range(16)], 16 * 256, [wsel, svf])
-    sv = {(t, h): al("af", 24) for t in range(RO) for h in range(NH)}
+    def where(src, pat, cmp, base, cm, arena="ab", w=None):
+        m = math.prod(c for _, c in pat)
+        b = al(arena, w or m)
+        op("G", lambda: [g.affine_select(ap(b, 0, m), ap(src, 0, m), pat, cmp, 0.0, base, cm)], 170 + 2 * m, [src], [b])
+        return b
+
+    def in_group(src, pat):
+        neg = [[-s, c] for s, c in pat]
+        return where(where(src, pat, OP.is_ge, 0, 1), neg, OP.is_ge, 15, -1)
+
+    def scaled(src, k, arena="ab", bias=0.0):
+        b = al(arena, src[2])
+        flex("k%d" % (len(ops) % 4), lambda e, _: [act(e, ap(b), ap(src), AF.Identity, bias, float(k))], sc(src[2]), vc(src[2], 0.5), [src], [b])
+        return b
+
+    ones = al("ab", 256)
+    op("V", lambda: [V.memset(ap(ones), 1.0)], vc(256, 0.5), [], [ones])
+    op("V", lambda: [V.memset(T.fw[:, VOID0:FEAT0], 16384.0), V.memset(T.tab[:, 2048:MEM0], 0.0), V.memset(T.tab[:, MEM0 + 2048:2 * MEM0], 0.0)],
+       3 * vc(16), [], ["void", "pad0", "padm0"])
+    bo = in_group(ones, [[-16, 8], [0, 16]])
+    ib = where(ones, [[-1, 128]], OP.is_equal, 0, 1)
+    wsel = where(ones, [[1, 144]], OP.is_equal, -15, -16)
+    keep = where(ones, [[0, 8], [1, 16]], OP.not_equal, 0, 0)
+    keep8 = where(ones, [[0, 16], [1, 8]], OP.not_equal, 0, 0)
+    bo8 = in_group(ones, [[0, 16], [-16, 8]])
+    perm = [where(ones, [[-16, 8], [-1, 8], [0, 2]], OP.is_equal, -8 * m, 1) for m in range(2)]
+    shift = where(ones, [[-1, 16], [-16, 8]], OP.is_equal, 0, 1, w=1024)
+    for a in (128, 256, 512):
+        op("S", lambda a=a: [S.activation(ap(shift, a, 2 * a), ap(shift, 0, a), AF.Identity)], sc(a), [shift], [shift])
+    ioq, ion, pc, ioa = iota("ai", [[0, 1]], 0, 1), iota("ai", [[-1, 20]], 32, 1), iota("af", [[0, 16], [1, 16]], 0, 0), iota("ai", [[1, 128]], 0, 1)
+    c8, c16 = iota("ai", [[1, 8]], 0, 0), iota("af", [[16, 8]], 0, 0)
+    op("G", lambda: [g.iota(T.ramp[:, :], [[1, 2048]], 0, 0, allow_small_or_imprecise_dtypes=True)], 4300, [], ["ramp"], name="late")
+    pqi, pui, ni, pa = al("ai", 1), al("ai", 1), al("ai", 20), al("ai", 128)
+    pq, pu, odd, memo = [al("af", 1) for _ in range(4)]
+    cols, diag, paf, tra, l_col, lane8 = al("ab", 20), al("ab", 256), al("ab", 128), al("ab", 256), al("au", 8), al("af", 8)
+    vts(pqi, ioq, 15, None, OP.bitwise_and)
+    vts(pq, pqi, 1.0, None, OP.mult)
+    vts(pui, pqi, 1, None, OP.logical_shift_right)
+    vts(pu, pui, 1.0, None, OP.mult)
+    vts(ni, ion, 15, None, OP.bitwise_and)
+    vts(cols, ni, 1.0 / 16, None, OP.mult)
+    vts(diag, pc, ap(pq), None, OP.is_equal, r=[pq])
+    vts(pa, ioa, 1, None, OP.bitwise_and)
+    vts(paf, pa, -1.0, 8192.0, OP.add, OP.mult)
+    par = in_group(paf, [[-16, 8], [0, 16]])
+    vts(tra, pc, ap(pq), 4096.0, OP.is_gt, OP.mult, r=[pq])
+    trb, trip = where(tra, [[1, 8], [0, 4], [-1, 8]], OP.is_equal, 0, 0), al("ab", 2048)
+    bo32 = scaled(bo8, 1, "af")
+
+    def spread(name, o, src):
+        for k in range(8):
+            flex(name, lambda e, _, k=k: [act(e, ap(o, 256 * k, 256 * k + 256), ap(src), AF.Identity, 0.0, ap(bo32, k, k + 1))], sc(256), vc(256, 0.5),
+                 [src, bo32], [sub(o, k)])
+    spread("trip", trip, trb)
+    vts(l_col, c8, 1.0, None, OP.mult)
+    vts(lane8, c16, ap(pq), None, OP.add, r=[pq])
+    dum = [scaled(pu, 1, "af", 2048.0 + 8 * m) for m in range(2)]
+    sact(odd, pu, scale=-2.0, bias=ap(pq), r=[pq])
+    sact(memo, odd, scale=float(MEM0))
+    dum2, least = [al("af", 1) for _ in range(2)], [al("af", 1) for _ in range(2)]
+    for m in range(2):
+        sact(dum2[m], odd, scale=16.0, bias=ap(dum[m]), r=[dum[m]])
+        sact(least[m], dum2[m], scale=ap(odd), r=[odd])
+    bo_16, bow, bo16, bo16n, bo32b, bo2p = [scaled(bo, k) for k in (1.0 / 16, -W19, 16, -16, 32, 2)]
+    bo2n = al("ab", 256)
+    op("S", lambda: [S.activation(ap(bo2n, a, a + H), ap(bo), AF.Identity, scale=-2.0) for a in (0, H)], 2 * sc(H), [bo], [bo2n])
+    ineg, i16n, ihalf, iquar, i8n, iw, ilow, i64k, i128, i128n, i4k = [scaled(ib, k) for k in (-1, -16, 0.5, -0.25, -8192, -W19, LOW, -65536, 128, -128, 4096)]
+    if {engine("old", h) for h in range(4)} != {"V"}:
+        ihigh = scaled(ib, -2.0 ** 24)
+    if {engine("mask", h) for h in range(4)} != {"V"}:
+        colr = [scaled(pq, 1, "af", float(t)) for t in range(RO)]
+    if {engine("sn", h) for h in range(4)} != {"V"}:
+        wall = in_group(where(ones, [[0, 9], [1, 16]], OP.is_equal, -15, 0), [[-16, 9], [0, 16]])
+    i32 = scaled(ib, 1, "af")
+    d0 = scaled(keep, -2.0 ** 23 - 1, "af", 2.0 ** 23)
+    rst8, offm = scaled(keep8, 2.0 ** 21, "af", -2.0 ** 21), scaled(bo8, 2.0 ** 20, "ab", -2.0 ** 20)
+    xc = {}
+    for t in range(RO):
+        for h in range(NH):
+            xc[t, h] = scaled(lane8, 1, "af", -float(FEAT0 - strip(t, h) + 2048))
+
+    for q in range(4):
+        a, b = 512 * q, 512 * q + 512
+        op("V", lambda a=a, b=b: [ts(T.lmt[:, a:b], T.lmi[:, a:b], 4095, None, OP.bitwise_and)], vc(512), ["lmi%d" % q], ["lmt%d" % q])
+        lin("mem0", T.tab[:, MEM0 + a:MEM0 + b], T.lmt[:, a:b], 512, ["lmt%d" % q], ["mem%d" % q], bias=-2048.0)
+        lin("rec0", T.tab[:, a:b], T.lmi[:, a:b], 512, ["lmi%d" % q], ["rec%d" % q])
+    sh, vth, thl, ea, eb = al("ah", 256), al("ah", 512), al("af", 16), al("ah", 512), al("ah", 512)
+    lin("sh", ap(sh, p1=8), ap(s0, p1=8), 256, [s0], [sh])
+    lin("vth", ap(vth, p1=8), ap(vt0, p1=8), 512, [vt0], [vth], bias=-2048.0)
+    t0, t1 = tile(1), tile(2)
+    mm(t0, [(0, 16, 1, ap(wsel, 15 - p, 143 - p, p1=8), ap(sh, p, 256, 16, p1=8), p == 0, p == 15) for p in range(16)], 16 * 64, [wsel, sh])
+    sv = {(t, h): al("af", 8) for t in range(RO) for h in range(NH)}
+    vb = {(t, h): al("ah", H) for t in range(RO) for h in range(NH)}
     pm = {(t, h): al("ah", 256) for t in range(RO) for h in range(NH)}
     for h in range(NH):
-        op("V", lambda h=h: [V.tensor_copy(ap(sv[0, h], 0, 8), ps(t0, 8 * h, 8 * h + 8)),
-                             ts(ap(sv[0, h], 8, 16), ps(t0, 16 + 8 * h, 24 + 8 * h), -2048.0, None, OP.add)], 2 * vc(8), [], [sv[0, h]], [t0])
-    op("V", lambda: [ts(ap(th16), ps(t0, 32, 48), 16.0, -15.0, OP.mult, OP.add)], vc(16), [], [th16], [t0])
-    vts(ea, lpq, 0.0, 2047.0, OP.min, OP.mult)
-    vts(eb, lpq, -2048.0, -2048.0, OP.add, OP.max)
+        op("S", lambda h=h: [S.activation(ap(sv[0, h]), ps(t0, 8 * h, 8 * h + 8), AF.Identity)], sc(8), [], [sv[0, h]], [t0])
+    dma("Y", [(T.ah[i:128:16, vb[0, 0][1]:vb[0, 0][1] + 256], ap(vth, 0, 256, p1=8)) for i in range(16)], 65536, r=[vth], w=[vb[0, 0], vb[0, 1]])
+    mm(t1, [(8 * h, 8 * h + 8, 1, ap(vth, 256 + H * h, 256 + H * h + H, p1=8), ap(ib, 0, 8, p1=8), True, True) for h in range(NH)], 128, [vth, ib])
+    op("S", lambda: [S.activation(ap(thl), ps(t1, 0, 16), AF.Identity, bias=32768.0 - 15, scale=16.0)], sc(16), [], [thl], [t1])
+    op("S", lambda: [S.activation(ap(ea), ap(lpq), AF.Relu, scale=-2048.0)], sc(512), [lpq], [ea])
+    lin("eb", ap(eb), ap(lpq), 512, [lpq], [eb], bias=-2048.0)
     for h in range(NH):
-        tl = tile()
-        mm(tl, [(128 * m, 128 * m + 128, 1, ap(e, 256 * m + H * h, 256 * m + H * h + H), ap(ib), e is ea, e is eb) for m in range(2) for e in (ea, eb)],
-           512, [ea, eb, ib])
-        op("V", lambda h=h, tl=tl: [V.tensor_copy(ap(pm[0, h]), ps(tl, 0, 256))], vc(256), [], [pm[0, h]], [tl])
+        tl = tile(5 + h)
+        mm(tl, [(128 * m, 128 * m + 128, 1, ap(e, 256 * m + H * h, 256 * m + H * h + H), ap(ineg if e is ea else ib), e is ea, e is eb)
+                for m in range(2) for e in (ea, eb)], 512, [ea, eb, ib, ineg])
+        lin("pm0", ap(pm[0, h]), lambda tl=tl: ps(tl, 0, 256), 256, [], subs(pm[0, h], 2), [tl])
+    SNR = ["snr"]
 
     mask = {(u, h): al("ab", 2048) for u in range(2) for h in range(NH)}
     gm = {h: al("ah", 2048) for h in range(NH)}
@@ -285,314 +316,326 @@ def build(g, core, T, topo):
     sg = {h: al("ab", 2048) for h in range(NH)}
     fb = {h: al("ab", 2048) for h in range(NH)}
 
-    def spread(o, src, r, cols, lst):
-        def fn(e, _):
-            if e == "V":
-                return [V.tensor_tensor(ap(o), ap(src).indirect(ap(lst, 0, len(cols))), ap(diag, 0, o[2]), OP.mult)]
-            return [S.activation(ap(o, 16 * c, 16 * c + 16), ap(diag, 0, 16), AF.Identity, scale=ap(src, x, x + 1)) for c, x in enumerate(cols)]
-        flex(fn, len(cols) * sc(16), 60 + o[2] * GA, r + [lst, diag], [o])
-
-    def members(dst, win, rw, lst, mk, tab, MEM):
+    def members(name, dst, win, rw, lst, mk, tab, MEM):
         a = al("au", H)
-        op("V", lambda: [ts(ap(a), win.indirect(ap(lst)), 1.0 / 4096, -0.5 + 1.0 / 8192, OP.mult, OP.add)], 60 + H * GA, rw + [lst], [a])
-        for q in range(2):
-            op("V", lambda q=q: [V.tensor_tensor(ap(dst, 1024 * q, 1024 * q + 1024), tab[:, MEM0:MEM0 + 2048].indirect(ap(a, 64 * q, 64 * q + 64)),
-                                                 ap(mk, 1024 * q, 1024 * q + 1024), OP.mult)],
-               60 + 1024 * GA, MEM + [a, sub(mk, q)], [sub(dst, q)])
+        flex(name + "l", lambda e, _: [act(e, ap(a), win.indirect(ap(lst)), AF.Identity, -0.5 + 1.0 / 8192, 1.0 / 4096)], 75 + H * GA, 60 + H * GA, rw + [lst], [a])
+        for q in range(NC):
+            gat(name + "abcd"[q], lambda q=q: V.tensor_tensor(ap(dst, CW * q, CW * q + CW), tab[:, MEM0:MEM0 + 2048].indirect(ap(a, CW // 16 * q, CW // 16 * (q + 1))),
+                                                  ap(mk, CW * q, CW * q + CW), OP.mult), CW, MEM + [a] + subs(mk, 4), [sub(dst, q)])
 
-    def compare(src, other, okey, h, after):
+    def compare(name, src, other, okey, h, after):
         for b in range(4):
-            tl = tile()
+            tl = tile(1 + b % 2)
             calls = []
             for u in range(4):
                 calls.append((128 * u, 128 * u + 128, 1, ap(bo), ap(src, 4 * b + u, 2048, 16), True, False))
                 calls.append((128 * u, 128 * u + 128, 1, other, ap(ineg), False, True))
-            mm(tl, calls, 1024, [bo, ineg, okey, sub(src, 0), sub(src, 1)])
-            flex(lambda e, _, b=b, tl=tl: [act(e, ap(sg[h], 512 * b, 512 * b + 512), ps(tl, 0, 512), AF.Sigmoid, -math.log(63.0), 64.0)],
+            mm(tl, calls, 1024, [bo, ineg, okey] + subs(src, NC))
+            flex(name + "abcd"[b], lambda e, _, b=b, tl=tl: [act(e, ap(sg[h], 512 * b, 512 * b + 512), ps(tl, 0, 512), AF.Sigmoid, -math.log(63.0), 64.0)],
                  sc(512), vc(512), [], [sub(sg[h], b)], [tl])
             after(b)
 
-    def settle(tl, w, o, rr, other, h):
-        rounded(ap(rr), rr, tl, w, MAGIC, tmp("r1%d" % w, h, w))
-        if FOLD:
-            mm(tl, [(0, w, 1, ap(ineg), ap(rr), False, True)], w, [ineg, rr])
-            op("V", lambda: [V.tensor_tensor(ap(o), ps(tl, 0, w), ap(other), OP.max)], vc(w), [other], [o], [tl])
-        else:
-            op("V", lambda: [V.tensor_tensor(ap(other), ps(tl, 0, w), ap(rr), OP.subtract)], vc(w), [rr], [other], [tl])
-            op("V", lambda: [V.tensor_tensor(ap(o), ps(tl, w, 2 * w), ap(other), OP.max)], vc(w), [other], [o], [tl])
+    def settle(name, tl, lo, o, okey, other, r, h):
+        rr, left = tmp(name + "r", h, H), tmp(name + "l", h, H)
+        rounded(name + "r", ap(rr), rr, tl, H, MAGIC, tmp(name + "1", h, H), lo)
+        v1(name, lambda: V.tensor_tensor(ap(left), ps(tl, lo, lo + H), ap(rr), OP.subtract), H, [rr], [left], [tl])
+        v1(name, lambda: V.tensor_tensor(ap(o), other(), ap(left), OP.max), H, [left] + r, [okey], [] if r else [tl], 2.0 if r else 1.0)
 
-    def half(t, h, tab, MEM, REC, PAD, thr, xout):
+    def half(t, h, tab, MEM, REC, thr, xout):
         last = t == RO - 1
         mk, db, xk, x, s_ = mask[t % 2, h], sg[h], "x%d%d" % (t, h), xap(t, h), sv[t, h]
-        both = lambda b: [sub(b, 0), sub(b, 1)]
-        tj = tile()
-        mm(tj, [(0, H, 1, ap(bo), x, True, True)], 128, [bo, xk])
-        ji = al("au", H)
-        op("V", lambda: [ts(ap(ji), ps(tj, 0, H), ap(colr[t]), None, OP.add)], vc(H), [colr[t]], [ji], [tj])
-        for q in range(2):
-            pick(mk, 1024 * q, 1024 * q + 1024, ap(ring), ji, 64 * q, 64 * q + 64, [ring], [sub(mk, q)])
-        su = al("au", 8)
-        op("V", lambda: [V.tensor_copy(ap(su), ap(s_, 0, 8))], vc(8), [s_], [su])
-        if t == 0:
-            members(gm[h], T.lmi[:, :], ["lmi0", "lmi1"], su, mk, tab, MEM)
+        if not last:
+            send(h, ap(vb[t + 1, h]), ap(vb[t, h]), [vb[t, h]], [vb[t + 1, h]], 32768)
+        tj = tile(3)
+        mm(tj, [(0, H, 1, ap(bo_16), x, True, True)], 128, [bo_16, xk])
+        jq, jw = tmp("jq", h, H, "ai"), tmp("jw", h, H, "ab")
+        lin("jq", ap(jq), lambda: ps(tj, 0, H), H, [], [jq], [tj], bias=-15.0 / 32)
+        v1("j", lambda: V.tensor_tensor(ap(jw), ps(tj, 0, H), ap(jq), OP.subtract), H, [jq], [jw], [tj])
+        if engine("mask") == "V":
+            for q in range(4):
+                op("V", lambda q=q: [ts(ap(mk, k, 2048, 16), ap(jw), ap(cols, k + t, k + t + 1), None, OP.is_equal) for k in range(4 * q, 4 * q + 4)],
+                   4 * vc(H, 0.5), [jw, cols], [sub(mk, q)], name="mask")
         else:
-            members(gm[h], tab[:, 0:2048], REC, su, mk, tab, MEM)
-        ty = tile()
-        mm(ty, [(H, 2 * H, 1, ap(ib), ap(pm[t, h], 0, H), True, False), (H, 2 * H, 1, ap(mk, 0, 2048, 16), ap(par), False, True)], 256,
-           [ib, par, pm[t, h], sub(gm[h], 0)] + both(mk))
-        val, pf = tmp("val", h, H, "ab"), tmp("pf", h, H)
-        flex(lambda e, _: [act(e, ap(val), ps(ty, H, 2 * H), AF.Relu, 3000.0)], sc(H), vc(H), [], [val], [ty])
-        if FOLD:
-            flex(lambda e, _: [act(e, ap(pf), ps(ty, H, 2 * H))], sc(H), vc(H), [], [pf], [ty])
-        mm(ty, [(0, H, 1, ap(i16n), ap(val), True, False)] + [(k, H, 16, ap(gm[h], k, 2048, 16), ap(bo, 0, 128, 16), False, False) for k in range(16)],
-           128 + 1024, [i16n, val, bo] + both(gm[h]))
-        compare(gm[h], ap(pm[t, h], H, 2 * H), pm[t, h], h, lambda b: mm(
-            ty, [(k, H, 16, ap(sg[h], H * k, H * k + H), ap(bow, 0, 128, 16), False, k == 15 and not FOLD) for k in range(4 * b, 4 * b + 4)], 256, [bow, sub(sg[h], b)]))
-        nl, nu = al("ah", H), al("au", H)
-        settle(ty, H, nl, tmp("rr", h, H, "ab" if FOLD else "af"), pf, h)
-        tn = tile()
-        mm(tn, [(0, H, 1, ap(nl), ap(ib), True, True)], 128, [nl, ib])
-        op("V", lambda: [ts(ap(nu), ps(tn, 0, H), 2064.0, 0.0, OP.add, OP.max)], vc(H), [], [nu], [tn])
-        for q in range(2):
-            pick(fb[h], 1024 * q, 1024 * q + 1024, T.fw[:, VOID0:FEAT0 + 4096], nu, 64 * q, 64 * q + 64, ["void", "feat"], [sub(fb[h], q)])
-        td = tile()
-        mm(td, [(H, 2 * H, 1, ap(ib), ap(nl), True, True)], 128, [nl, ib])
-        if BY_MAX[h]:
-            txp = tile()
+            ji = al("au", H)
+            sact(ji, jw, scale=16.0, bias=ap(colr[t]), r=[colr[t]])
+            for q in range(4):
+                pick("mask", mk, 512 * q, 512 * q + 512, ap(diag), ji, 32 * q, 32 * q + 32, [diag], [sub(mk, q)])
+        oh = ap(mk, 0, 2048, 16)
+        su = al("au", 8)
+        lin("su", ap(su), ap(s_), 8, [s_], [su])
+        if t == 0:
+            members("mem1", gm[h], T.lmi[:, :], ["lmi%d" % q for q in range(4)], su, mk, tab, MEM)
+        else:
+            members("mem1", gm[h], tab[:, 0:2048], REC, su, mk, tab, MEM)
+        ty, tp = tile(0), tile(3)
+        pe, n0, nl, nu = tmp("pe", h, H, "ah"), tmp("n0", h, H, "ah"), tmp("nl", h, H, "ah"), al("au", H)
+        mm(tp, [(0, H, 1, oh, ap(par), True, False), (0, H, 1, ap(ib), ap(pm[t, h], 0, H), False, True)], 256, [ib, par, sub(pm[t, h], 0)] + subs(mk, 4))
+        v1("pe", lambda: ts(ap(pe), ps(tp, 0, H), -4096.0, None, OP.max), H, [], [pe], [tp])
+        mm(ty, [(0, H, 1, ap(i64k), ap(ones, 0, H), True, False)] + [(k, H, 16, ap(gm[h], k, 2048, 16), ap(bo, 0, 128, 16), False, False) for k in range(16)],
+           128 + 1024, [i64k, ones, bo] + subs(gm[h], NC))
+        mm(ty, [(0, H, 1, ap(i16n), ap(pe), False, True)], 128, [i16n, pe])
+        v1("n0", lambda: V.tensor_tensor(ap(n0), ps(ty, 0, H), ap(pe), OP.max), H, [pe], [n0], [ty])
+        tn = tile(3)
+        mm(tn, [(0, H, 1, ap(n0), ap(ib), True, True)], 128, [n0, ib])
+        lin("nu", ap(nu), lambda: ps(tn, 0, H), H, [], [nu], [tn], bias=2048.0)
+        for q in range(NC):
+            pick("feat" + "abcd"[q], fb[h], CW * q, CW * q + CW, T.fw[:, FEAT0:FEAT0 + 4096], nu, CW // 16 * q, CW // 16 * (q + 1), ["feat"], [sub(fb[h], q)])
+        mm(ty, [(H, 2 * H, 1, ap(ib), ap(pe), True, True), (0, H, 1, ap(ib), ap(n0), True, False)], 256, [ib, n0, pe])
+        compare("cmp1", gm[h], ap(pm[t, h], H, 2 * H), sub(pm[t, h], 1), h, lambda b: mm(
+            ty, [(k, H, 16, ap(sg[h], H * k, H * k + H), ap(bow, 0, 128, 16), False, k == 15) for k in range(4 * b, 4 * b + 4)], 256, [bow, sub(sg[h], b)]))
+        settle("set1", ty, 0, nl, nl, lambda: ps(ty, H, 2 * H), [], h)
+        td = tile(0)
+        mm(td, [(H, 2 * H, 1, ap(ib), ap(nl), True, False), (H, 2 * H - 1, 1, ap(ineg), ap(nl, 1, H), False, False),
+                (H + 15, 2 * H - 16, 16, ap(ib), ap(nl, 16, H, 16), False, True),
+                (0, H, 1, ap(i128), ap(n0), True, False), (0, H, 1, ap(i128n), ap(nl), False, False)], 576, [nl, n0, ib, ineg, i128, i128n])
+        by_max = [engine("dist" + "abcd"[b]) == "V" for b in range(4)]
+        if any(by_max):
+            txp = tile(3)
             mm(txp, [(0, H, 1, ap(ib), x, True, True)], 128, [ib, xk, sub(fb[h], 0)])
-            mm(td, [(0, H, 1, x, ap(bo16n), True, False)] + [(k, H, 16, ap(fb[h], k, 2048, 16), ap(bo16n, 0, 128, 16), False, False) for k in range(16)],
-               128 + 1024, [bo16n, xk] + both(fb[h]))
         for b in range(4):
             ks = range(4 * b, 4 * b + 4)
-            if BY_MAX[h]:
+            if by_max[b]:
                 op("V", lambda ks=ks: [V.tensor_tensor(ap(db, H * k, H * k + H), ps(txp, 0, H), ap(fb[h], k, 2048, 16), OP.max) for k in ks],
-                   4 * vc(H), both(fb[h]), [sub(db, b)], [txp])
-                mm(td, [(k, H, 16, ap(db, H * k, H * k + H), ap(bo32b, 0, 128, 16), False, k == 15) for k in ks], 256, [bo32b, sub(db, b)])
+                   4 * vc(H), subs(fb[h], NC), [sub(db, b)], [txp], name="dist" + "abcd"[b])
+                mm(td, [(k, H, 16, l, ap(r, 0, 128, 16), False, k == 15 and r is bo32b) for k in ks
+                        for l, r in ((x, bo16n), (ap(fb[h], k, 2048, 16), bo16n), (ap(db, H * k, H * k + H), bo32b))], 768,
+                   [bo32b, bo16n, xk, sub(db, b)] + subs(fb[h], NC))
             else:
-                tl = tile()
+                tl = tile(1 + b % 2)
                 calls = []
                 for u in range(4):
                     calls.append((128 * u, 128 * u + 128, 1, ap(ib), ap(fb[h], 4 * b + u, 2048, 16), True, False))
                     calls.append((128 * u, 128 * u + 128, 1, ap(ineg), x, False, True))
-                mm(tl, calls, 1024, [ib, ineg, xk] + both(fb[h]))
-                op("S", lambda b=b, tl=tl: [S.activation(ap(db, 512 * b, 512 * b + 512), ps(tl, 0, 512), AF.Abs)], sc(512), [], [sub(db, b)], [tl])
-                mm(td, [(k, H, 16, ap(db, H * k, H * k + H), ap(bo16, 0, 128, 16), True, True) for k in ks], 256, [bo16, sub(db, b)])
-        sp2, tk, nt, z, lo = tmp("sp2", h, 256), tmp("tk", h, H), tmp("nt", h, H), tmp("z", h, H), tmp("lo", h, 256)
-        op("V", lambda: [V.tensor_tensor_scan(ap(sp2, 0, H), ap(d0), ps(td, 0, H), 0.0, OP.add, OP.min)], vc(H), [d0], [sub(sp2, 0)], [td])
-        op("V", lambda: [V.tensor_tensor(ap(tk), ps(td, 0, H), ap(sp2, 0, H), OP.is_equal)], vc(H), [sub(sp2, 0)], [tk], [td])
-        sact(nt, tk, bias=1.0, scale=-1.0)
-        op("V", lambda: [V.tensor_tensor(ap(z), ps(td, H, 2 * H), ap(tk), OP.mult)], vc(H), [tk], [z], [td])
-        op("V", lambda: [V.tensor_tensor_scan(ap(sp2, H, 2 * H), ap(nt), ap(z), 0.0, OP.mult, OP.add)], vc(H), [nt, z], [sub(sp2, 1)])
-        spread(lo, sp2, both(sp2), [16 * c + 15 for c in range(16)], l_end)
-        to = tile()
-        mm(to, [(8 * m, 8 * m + 8, 1, ap(lo, H * m, H * m + H), ap(bo32, 0, 128, 16), True, True) for m in range(2)], 512, [lo, bo32])
-        o1, of, osn, far = al("af", 8), al("au", 8), al("au", 8), al("af", 8)
-        op("V", lambda: [ts(ap(osn), ps(to, 8, 16), 2048.0, 0.0, OP.add, OP.max),
-                         V.tensor_tensor(ap(o1), ps(to, 8, 16), ap(xc[t, h]), OP.max),
-                         V.tensor_tensor(ap(far), ps(to, 0, 8), ap(thr, 8 * h, 8 * h + 8), OP.is_ge)], 3 * vc(8), [xc[t, h], thr], [osn, o1, far], [to])
-        vts(of, o1, float(FEAT0 - strip(t, h) + 2048), None, OP.add)
+                mm(tl, calls, 1024, [ib, ineg, xk] + subs(fb[h], NC))
+                op("S", lambda b=b, tl=tl: [S.activation(ap(db, 512 * b, 512 * b + 512), ps(tl, 0, 512), AF.Abs)], sc(512), [], [sub(db, b)], [tl], name="dist" + "abcd"[b])
+                mm(td, [(k, H, 16, ap(db, H * k, H * k + H), ap(bo16, 0, 128, 16), False, k == 15) for k in ks], 256, [bo16, sub(db, b)])
+        old, new = tmp("old", h, 256), tmp("new", h, 256)
+        sb, tv = tmp("sb", h, H, "ah"), tile(1)
+        pick("sb", sb, 0, H, T.ramp[:, :], su, 0, 8, ["ramp"], [sb])
+        mm(tv, [(0, H, 1, ap(ilow), oh, True, False), (0, H, 1, ap(ib), ap(vb[t, h]), False, False), (0, H, 1, ap(i4k), ap(sb), False, True),
+                (H, 2 * H, 1, ap(ilow), oh, True, False), (H, 2 * H, 1, ap(ib), ap(vb[t, h]), False, True)][:3 if last else 5],
+           384 if last else 640, [ilow, ib, i4k, sb, vb[t, h]] + subs(mk, 4))
+        flex("vo", lambda e, _: [act(e, ap(new, m, 256, 2), ps(tv, H * m, H * m + H), AF.Identity, 2048.0 * (1 - m) - LOW) for m in range(2 - last)],
+             (2 - last) * sc(H), (2 - last) * vc(H), [], subs(new, 2), [tv])
+        kk, nt, sp2, ls = tmp("kk", h, H), tmp("nt", h, H), tmp("sp2", h, 256, "ah"), tmp("ls", h, H)
+        v1("arg", lambda: V.tensor_tensor_scan(ap(kk), ap(d0), ps(td, 0, H), 0.0, OP.add, OP.min), H, [d0], [kk], [td])
+        v1("arg", lambda: V.tensor_tensor(ap(nt), ps(td, 0, H), ap(kk), OP.not_equal), H, [kk], [nt], [td])
+        v1("arg", lambda: V.tensor_tensor_scan(ap(sp2, 0, H), ap(nt), ps(td, H, 2 * H), 0.0, OP.mult, OP.add), H, [nt], [sub(sp2, 0)], [td])
+        v1("arg", lambda: V.tensor_tensor(ap(sp2, H + 15, 2 * H, 16), ap(kk, 15, H, 16), ap(thr, 8 * h, 8 * h + 8), OP.is_lt), 8, [kk, thr], [sub(sp2, 1)])
+        to = tile(3)
+        mm(to, [(0, H, 1, ap(ib), ap(offm), True, False)] + [(16 * c, 16 * c + 16, 1, ap(shift, c, 1024, 8), ap(sp2, 15, 256, 16), False, c == 7) for c in range(8)],
+           128 + 512, [ib, offm, shift] + subs(sp2, 2))
+        v1("arg", lambda: V.tensor_tensor_scan(ap(ls), ap(rst8), ps(to, 0, H), 0.0, OP.add, OP.max), H, [rst8], [ls], [to])
+        win, near = ap(ls, 7, H, 16), ap(ls, 15, H, 16)
+        o1, of, osn = al("af", 8), al("au", 8), al("au", 8)
+        lin("osn", ap(osn), win, 8, [ls], [osn], func=AF.Relu, bias=2048.0)
+        v1("of", lambda: V.tensor_tensor(ap(o1), win, ap(xc[t, h]), OP.max), 8, [ls, xc[t, h]], [o1])
+        lin("ofu", ap(of), ap(o1), 8, [o1], [of], bias=float(FEAT0 - strip(t, h) + 2048))
         fs = tmp("fs", h, H, "ab")
-        pick(fs, 0, H, T.fw[:, strip(t, h):FEAT0 + 4096], of, 0, 8,
+        pick("fs", fs, 0, H, T.fw[:, strip(t, h):FEAT0 + 4096], of, 0, 8,
              ["void", "feat"] + ["x%d%d" % (u, v) for u in range(t + 1) for v in range(NH) if 2 * u + v <= 2 * t + h], [fs])
-        tx = tile()
+        tx = tile(2)
         mm(tx, [(0, H, 1, ap(ihalf), x, True, False), (0, H, 1, ap(iquar), ap(ones, 0, H), False, False), (0, H, 1, ap(ihalf), ap(fs), False, True)], 384,
            [ihalf, iquar, ones, xk, fs])
         if last:
-            rounded(ap(xout, H * h, H * h + H), sub(xout, h), tx, H, MAGIC1, tmp("x1", h, H))
+            rounded("x2", ap(xout, H * h, H * h + H), sub(xout, h), tx, H, MAGIC1, tmp("x1", h, H))
         else:
             x2 = al("ab", H)
-            rounded(ap(x2), x2, tx, H, MAGIC1, tmp("x1", h, H))
+            rounded("x2", ap(x2), x2, tx, H, MAGIC1, tmp("x1", h, H))
             send(h, xap(t + 1, h), ap(x2), [x2], ["x%d%d" % (t + 1, h)], 32768)
-        sr = al("ah", H)
-        op("V", lambda: [V.tensor_copy(ap(sr), T.snr[:, :].indirect(ap(osn)))], 60 + H * GA, ["snr", osn], [sr])
-        tq = tile()
-        mm(tq, [(0, 8, 1, ap(wone, 15 - p, 143 - p), ap(sr, p, H, 16), p == 0, p == 15) for p in range(16)], 1024, [wone, sr])
-        su2, il, sp, same, ngo = al("au", 8), al("au", 16), al("af", 8), al("af", 8), al("af", 8)
-        op("V", lambda: [V.tensor_copy(ap(su2), ps(tq, 0, 8)), V.tensor_tensor(ap(same), ps(tq, 0, 8), ap(s_, 0, 8), OP.is_equal), V.tensor_copy(ap(sp), ps(tq, 0, 8))],
-           3 * vc(8), [s_], [su2, sp, same], [tq])
-        members(gn[h], tab[:, 0:2048], REC, su2, mk, tab, MEM)
-        op("V", lambda: [ts(ap(il, 0, 16, 2), ap(sp), 0.0, None, OP.add), ts(ap(il, 1, 16, 2), ap(sp), float(MEM0), None, OP.add)], 2 * vc(8), [sp], [il])
-        vtt(ngo, same, far, OP.max)
-        so, kt, ko, u1, u2 = al("af", 16), al("af", 8), al("af", 8), al("af", 8), al("af", 8)
-        sact(kt, ngo, scale=-4096.0)
-        vtt(ko, kt, sp, OP.add)
-        sact(u1, ngo, bias=-4096.0, scale=4096.0)
-        op("V", lambda: [V.tensor_tensor(ap(u2), ap(u1), ap(s_, 0, 8), OP.add)], vc(8), [u1, s_], [u2])
-        op("V", lambda: [V.tensor_tensor(ap(so, 0, 8), ap(ko), ap(u2), OP.max)], vc(8), [ko, u2], [sub(so, 0)])
-        cnt = None
-        if not last:
-            flex(lambda e, _: [act(e, ap(so, 8, 16), ap(s_, 8, 16))], sc(8), vc(8), [s_], [sub(so, 1)])
-            send(h, ap(sv[t + 1, h], 0, 16), ap(so), both(so), [sv[t + 1, h]], 8192)
-            cnt, junk = al("af", 1), al("af", 8)
-            op("S", lambda: [S.activation(ap(junk), ap(ngo), AF.Identity, accum_out=ap(cnt))], sc(8) + 20, [ngo], [junk, cnt])
+        z, zs, sr = tmp("z", h, H, "ah"), tmp("zs", h, H, "ah"), tmp("sr", h, H, "ah")
+        sp = ap(zs, 15, H, 16)
+        su2, d, e, so, ngo, ko = al("au", 8), al("af", 8), al("af", 8), al("af", 8), al("ab", 8), al("af", 8)
+        pick("sr", sr, 0, H, T.snr[:, :], osn, 0, 8, SNR, [sr])
+        if engine("sn") == "V":
+            gat("sn", lambda: V.tensor_tensor(ap(z), T.snr[:, :].indirect(ap(osn)), ap(diag, 0, H), OP.mult), H, SNR + [osn, diag], [z])
+            v1("sn", lambda: V.tensor_tensor_scan(ap(zs), ap(keep), ap(z), 0.0, OP.mult, OP.add), H, [keep, z], [zs], rate=0.5)
+            lin("su2", ap(su2), sp, 8, [zs], [su2])
         else:
-            tys, ysb = tile(), al("af", H)
-            mm(tys, [(p, H, 16, ap(i32, p, 128, 16), ap(so, 0, 8), True, True, 8) for p in range(16)], 16 * 4 * 8, [i32, sub(so, 0)])
-            flex(lambda e, _: [act(e, ap(ysb, p1=8), ps(tys, 0, H, 1, 8))], sc(H), vc(H), [], [ysb], [tys])
+            tq = tile(3)
+            mm(tq, [(0, 8, 1, ap(wall, 15 - p, 143 - p), ap(sr, p, H, 16), p == 0, p == 15) for p in range(16)], 1024, [wall, sr])
+            lin("su2", ap(su2), lambda: ps(tq, 0, 8), 8, [], [su2], [tq], scale=1.0 / 16)
+            lin("sp", sp, lambda: ps(tq, 0, 8), 8, [], [zs], [tq], scale=1.0 / 16)
+        members("mem2", gn[h], tab[:, 0:2048], REC, su2, mk, tab, MEM)
+        v1("mv", lambda: V.tensor_tensor(ap(d), sp, ap(s_), OP.subtract), 8, [zs, s_], [d])
+        v1("mv", lambda: V.tensor_tensor(ap(e), ap(d), near, OP.mult), 8, [d, ls], [e])
+        v1("mv", lambda: V.tensor_tensor(ap(so), ap(e), ap(s_), OP.add), 8, [e, s_], [so])
+        v1("mv", lambda: ts(ap(ngo), ap(e), 0.0, 4096.0, OP.is_equal, OP.mult), 8, [e], [ngo])
+        v1("mv", lambda: V.tensor_tensor(ap(ko), sp, ap(ngo), OP.subtract), 8, [zs, ngo], [ko])
+        eqb = tmp("eqb", h, H, "ab")
+        gat("eqb", lambda: V.tensor_tensor(ap(eqb), ap(ko).indirect(ap(l_col)), ap(sr), OP.is_equal), H, [ko, sr, l_col], [eqb])
+        tw = tile(3)
+        calls = []
+        for m in range(2):
+            calls += [(m, 16, 2, ap(perm[m]), sp, True, False), (m, 16, 2, ap(perm[m]), ap(ngo), False, False)]
+            calls += [(m, 16, 2, ap(trip, p, 2048, 16), ap(eqb, p, H, 16), False, p % 8 == 7) for p in range(max(1, 8 * m), 8 * m + 8)]
+        mm(tw, calls, 64 * 19, perm + [zs, ngo, eqb] + subs(trip, 8))
+        wl = al("au", 16)
+        if last:
+            op("V", lambda: [ts(ap(wl, m, 16, 2), ps(tw, m, 16, 2), ap(dum2[m]), ap(least[m]), OP.min, OP.max) for m in range(2)], 2 * vc(8), dum2 + least, [wl], [tw], name="wl")
+        else:
+            op("V", lambda: [ts(ap(wl, m, 16, 2), ps(tw, m, 16, 2), ap(dum[m]), ap(memo), OP.min, OP.add) for m in range(2)], 2 * vc(8), dum + [memo], [wl], [tw], name="wl")
+        nm = 1 if last else 2
+        if engine("old") == "V":
+            up = tmp("up", h, H, "ab")
+            flex("up", lambda e, _: [act(e, ap(up), oh, AF.Identity, 2.0 ** 24, -2.0 ** 25)], sc(H), vc(H, 0.5), subs(mk, 4), [up])
+            for m, rw in enumerate((REC, MEM)[:nm]):
+                gat("old", lambda m=m: V.tensor_tensor(ap(old, m, 256, 2), tab[:, MEM0 * m:MEM0 * m + 2048].indirect(ap(su2)), ap(up), OP.min), H,
+                    rw + [su2, up], [sub(old, m)])
+        else:
+            orc, omc, tu = tmp("orc", h, H), tmp("omc", h, H, "ah"), tile(1)
+            pick("old", orc, 0, H, tab[:, 0:2048], su2, 0, 8, REC, [orc])
+            if not last:
+                pick("old", omc, 0, H, tab[:, MEM0:MEM0 + 2048], su2, 0, 8, MEM, [omc])
+            mm(tu, [(0, 256, 2, ap(i32), ap(orc), True, False), (0, 256, 2, ap(ihigh), oh, False, True),
+                    (1, 256, 2, ap(ib), ap(omc), True, False), (1, 256, 2, ap(ihigh), oh, False, True)][:2 * nm], 384 + 256 * nm, [i32, ib, ihigh, orc, omc] + subs(mk, 4))
+            lin("old", ap(old, 0, 256, 3 - nm), lambda: ps(tu, 0, 256, 3 - nm), H * nm, [], subs(old, 2), [tu])
+        cz = None
+        if not last:
+            send(h, ap(sv[t + 1, h]), ap(so), [so], [sv[t + 1, h]], 4096)
+            cnt, junk, cz = al("af", 1), al("af", 8), al("ab", 16)
+            op("S", lambda: [S.activation(ap(junk), ap(ngo), AF.Identity, accum_out=ap(cnt))], sc(8) + 20, [ngo], [junk, cnt])
+            sact(cz, bo8, scale=ap(cnt), r=[cnt])
+        else:
+            tys, ysb = tile(3), al("af", H)
+            mm(tys, [(p, H, 16, ap(i32, p, 128, 16), ap(so, 0, 8), True, True, 8) for p in range(16)], 16 * 4 * 8, [i32, so])
+            flex("ys", lambda e, _: [act(e, ap(ysb, p1=8), ps(tys, 0, H, 1, 8))], sc(H), vc(H), [], [ysb], [tys])
             dma("Y", [(T.ys[:, H * h:H * h + H], ap(ysb, p1=8))], 4096, r=[ysb])
-        zg, nv = tmp("zg", h, H, "ab"), tmp("nv", h, 256)
-        spread(zg, ngo, [ngo], list(range(8)), l_col)
-        tr = tile()
-        mm(tr, [(256, 512, 1, ap(ib), ap(pm[t, h]), True, False), (256, 512, 1, ap(i8n), ap(ones), False, False), (256, 512, 1, ap(zg), ap(bo8p), False, True)], 768,
-           [ib, i8n, ones, zg, bo8p, pm[t, h], sub(gn[h], 0)])
-        if FOLD:
-            flex(lambda e, _: [act(e, ap(nv), ps(tr, 256, 512))], sc(256), vc(256), [], [nv], [tr])
-        mm(tr, [(0, 256, 1, ap(zg), ap(bo8n), True, False), (0, H, 1, ap(ib), ap(nl), False, False)]
+        zg = tmp("zg", h, H, "ab")
+        gat("zg", lambda: V.tensor_tensor(ap(zg), ap(ngo).indirect(ap(l_col)), ap(diag, 0, H), OP.mult), H, [ngo, l_col, diag], [zg])
+        tr = tile(0)
+        mm(tr, [(256, 512, 1, ap(ib), ap(pm[t, h]), True, False), (256, 512, 1, ap(i8n), ap(ones), False, False),
+                (256, 384, 1, ap(zg), ap(bo2p), False, False), (384, 512, 1, ap(zg), ap(bo2p), False, True)], 768,
+           [ib, i8n, ones, zg, bo2p] + subs(pm[t, h], 2))
+        mm(tr, [(0, 256, 1, ap(zg), ap(bo2n), True, False), (0, H, 1, ap(ib), ap(nl), False, False)]
            + [(H + k, 2 * H, 16, ap(gn[h], k, 2048, 16), ap(bo, 0, 128, 16), False, False) for k in range(16)],
-           384 + 1024, [zg, bo8n, ib, nl, bo] + both(gn[h]))
+           384 + 1024, [zg, bo2n, ib, nl, bo] + subs(gn[h], NC))
 
         def after(b):
             calls = []
             for k in range(4 * b, 4 * b + 4):
                 calls.append((H + k, 2 * H, 16, ap(sg[h], H * k, H * k + H), ap(bow, 0, 128, 16), False, False))
-                calls.append((0, H, 1, ap(sg[h], H * k, H * k + H), ap(iw), False, k == 15 and not FOLD))
+                calls.append((0, H, 1, ap(sg[h], H * k, H * k + H), ap(iw), False, k == 15))
             mm(tr, calls, 768, [bow, iw, sub(sg[h], b)])
-        compare(gn[h], ap(nl), nl, h, after)
+        compare("cmp2", gn[h], ap(nl), nl, h, after)
         po = al("ah", 256)
-        settle(tr, 256, po, tmp("r2", h, 256, "ab" if FOLD else "af"), nv, h)
-        if not last:
-            send(h, ap(pm[t + 1, h]), ap(po), [po], [pm[t + 1, h]], 65536)
-        else:
-            tf, yo = tile(), al("af", 256)
-            mm(tf, [(H * m, H * m + H, 1, ap(po, H * m, H * m + H), ap(ib), True, True) for m in range(2)], 256, [po, ib])
-            op("V", lambda: [ts(ap(yo), ps(tf, 0, 256), 2048.0, -1.0, OP.add, OP.max)], vc(256), [], [yo], [tf])
+        for m in range(2):
+            settle("set" + "pm"[m], tr, H * m, part(po, H * m, H), sub(po, m), lambda m=m: ps(tr, 256 + H * m, 256 + H * m + H), [], h)
+            if not last:
+                send(h, ap(pm[t + 1, h], H * m, H * m + H), ap(po, H * m, H * m + H), [sub(po, m)], [sub(pm[t + 1, h], m)], 32768)
+        if last:
+            tf, yo = tile(3), al("af", 256)
+            mm(tf, [(H * m, H * m + H, 1, ap(po, H * m, H * m + H), ap(ib), True, True) for m in range(2)], 256, subs(po, 2) + [ib])
+            v1("yo", lambda: ts(ap(yo), ps(tf, 0, 256), 2048.0, -1.0, OP.add, OP.max), 256, [], [yo], [tf])
             dma("Y", [(T.yp[:, H * h:H * h + H], ap(yo, 0, H)), (T.yq[:, H * h:H * h + H], ap(yo, H, 2 * H))], 131072, r=[yo])
-        eqb = tmp("eqb", h, H, "ab")
-        op("V", lambda: [V.tensor_tensor(ap(eqb), ap(ko).indirect(ap(l_col, 0, 8)), ap(sr), OP.is_equal)], 60 + H * GA, [ko, sr, l_col], [eqb])
-        tw = tile()
-        mm(tw, [(0, 8, 1, ap(i32), ap(ngo), True, False)] + [(0, 8, 1, T.trip[:, 128 * p:128 * p + 128], ap(eqb, p, H, 16), False, p == 15) for p in range(1, 16)],
-           256 + 960, [i32, ngo, "trip", eqb])
-        w1, w2, wl, ra = al("af", 8), al("af", 8), al("au", 16), al("af", 8)
-        op("V", lambda: [ts(ap(w1), ps(tw, 0, 8), 0.5, ap(dum), OP.is_gt, OP.mult)], vc(8), [dum], [w1], [tw])
-        vtt(w2, w1, sp, OP.max)
-        op("V", lambda: [ts(ap(wl, 0, 16, 2), ap(w2), 0.0, None, OP.add), ts(ap(wl, 1, 16, 2), ap(w2), float(MEM0), None, OP.add)], 2 * vc(8), [w2], [wl])
-        sact(ra, s_, bias=2048.0, scale=4096.0)
-        op("V", lambda: [V.tensor_tensor(ap(s_, 16, 24), ap(ra), ap(s_, 8, 16), OP.add)], vc(8), [ra, s_], [sub(s_, 2)])
-        zr, old, oh, dl = tmp("zr", h, 256), tmp("old", h, 256), tmp("oh", h, 256, "ab"), tmp("dl", h, 256)
-        spread(zr, s_, [s_, sub(s_, 2)], [16 - 8 * (c % 2) + c // 2 for c in range(16)], l_rec)
-        pick(old, 0, 256, tab[:, :], il, 0, 16, REC + MEM + PAD, [old])
-        pick(oh, 0, 256, ap(mk), l_oh, 0, 16, both(mk), [oh])
-        tu = tile()
-        mm(tu, [(0, 256, 1, ap(bo32, 0, 128), ap(zr), True, False)], 1024, [bo32, zr, osn])
-        mm(tu, [(0, 256, 1, ap(i32n), ap(old), False, True)], 1024, [i32n, old])
-        op("V", lambda: [V.tensor_tensor(ap(dl), ps(tu, 0, 256), ap(oh), OP.mult)], vc(256), [oh], [dl], [tu])
-        return wl, old, dl, cnt
+        return wl, old, new, cz
 
-    thr = th16
+    thr = thl
     xout = al("af", 256)
     for t in range(RO):
         last = t == RO - 1
-        u, w = t % 2, 1 - t % 2
-        tab, nxt = T["tab%d" % u], T["tab%d" % w]
-        MEM, REC, PAD = ["mem%d0" % u, "mem%d1" % u], ["rec%d0" % u, "rec%d1" % u], ["pad%d" % u]
-        MEMN, RECN, PADN = ["mem%d0" % w, "mem%d1" % w], ["rec%d0" % w, "rec%d1" % w], ["pad%d" % w]
-        dma("Y", [(nxt[:, a:a + 1032], tab[:, a:a + 1032]) for a in (0, 1032)], 1056768, r=REC + PAD, w=RECN + PADN)
-        if not last:
-            dma("Y", [(nxt[:, a:a + 1032], tab[:, a:a + 1032]) for a in (MEM0, MEM0 + 1032)], 1056768, r=MEM + PAD, w=MEMN + ["padm%d" % w])
-        PAD, PADN = PAD + ["padm%d" % u], PADN + ["padm%d" % w]
         upd = {}
+        u, w = (t % 2, 1 - t % 2) if CFG["double"] else (0, 0)
+        tab, nxt = T[("tab", "tab1")[u]], T[("tab", "tab1")[w]]
+        MEM, REC = ["mem%d" % (q + 4 * u) for q in range(4)], ["rec%d" % (q + 4 * u) for q in range(4)]
+        MEMN, RECN = ["mem%d" % (q + 4 * w) for q in range(4)], ["rec%d" % (q + 4 * w) for q in range(4)]
+        if u != w:
+            dma("Y", [(nxt[:, 0:MEM0], tab[:, 0:MEM0])], 1064960, r=REC + ["pad%d" % u], w=RECN + ["pad%d" % w])
+            if not last:
+                dma("Y", [(nxt[:, MEM0:2 * MEM0], tab[:, MEM0:2 * MEM0])], 1064960, r=MEM + ["padm%d" % u], w=MEMN + ["padm%d" % w])
         for h in range(NH):
             cur[0] = (t, h)
-            upd[h] = half(t, h, tab, MEM, REC, PAD, thr, xout)
-        cur[0] = (t, 2)
+            upd[h] = half(t, h, tab, MEM, REC, thr, xout)
+        win = nxt[:, 0:MEM0] if last else nxt[:, :]
         for h in (1, 0):
-            wl, old, dl, _ = upd[h]
-            m = 1 if last else 2
+            wl, old, new, _ = upd[h]
+            cur[0] = (t, h)
             for c in range(7, -1, -1):
-                op("V", lambda wl=wl, old=old, dl=dl, c=c, m=m, nxt=nxt: [
-                    V.tensor_tensor(nxt[:, 0:m * MEM0].indirect(ap(wl, 2 * c, 2 * c + m)), ap(old, 32 * c, 32 * c + 16 * m), ap(dl, 32 * c, 32 * c + 16 * m), OP.add)],
-                   60 + 16 * m * SC, [wl, old, dl], RECN + (PADN[:1] if last else MEMN + PADN))
+                op("V", lambda wl=wl, old=old, new=new, c=c, win=win: [
+                    V.tensor_tensor(win.indirect(ap(wl, 2 * c, 2 * c + 2)), ap(old, 32 * c, 32 * c + 32), ap(new, 32 * c, 32 * c + 32), OP.max)],
+                   50 + 32 * SC, [wl] + subs(old, 2) + subs(new, 2), RECN + ["pad%d" % w] + ([] if last else MEMN + ["padm%d" % w]), name="scat")
         if not last:
-            ta = tile()
-            mm(ta, [(0, 1, 1, ap(bo32, 0, 128), ap(upd[h][3]), h == 0, h == 1) for h in range(NH)], 512, [bo32, upd[0][3], upd[1][3]])
-            a1, a2, a3, nthr = al("ai", 1), al("ai", 1), al("af", 1), al("af", 16)
-            op("V", lambda ta=ta, a1=a1: [ts(ap(a1), ps(ta, 0, 1), -1.0, 256.0, OP.mult, OP.add)], vc(1), [], [a1], [ta])
-            vts(a2, a1, 31, None, OP.bitwise_and)
-            vts(a3, a2, 16.0, None, OP.mult)
-            op("S", lambda a3=a3, nthr=nthr: [S.activation(ap(nthr), ap(th16), AF.Identity, bias=ap(a3))], sc(16), [th16, a3], [nthr])
+            ta = tile(3)
+            mm(ta, [(0, 16, 1, ap(ones, 0, 128), ap(upd[h][3]), h == 0, h == 1) for h in range(NH)], 128, [ones, upd[0][3], upd[1][3]])
+            a1, a2, nthr = al("ai", 16), al("ai", 16), al("af", 16)
+            lin("cnt", ap(a1), lambda ta=ta: ps(ta, 0, 16), 16, [], [a1], [ta], bias=4096.0, scale=-1.0 / 256)
+            vts(a2, a1, 496, None, OP.bitwise_and)
+            v1("thr", lambda a2=a2, nthr=nthr: V.tensor_tensor(ap(nthr), ap(a2), ap(thl), OP.add), 16, [a2, thl], [nthr])
             thr = nthr
-    dma("Y", [(T.yx[:, :], ap(xout))], 131072, r=[sub(xout, 0), sub(xout, 1)])
-    dma("Y", [(T.ylm[:, a:a + 1024], nxt[:, a:a + 1024]) for a in (0, 1024)], 1048576, r=RECN)
+    dma("Y", [(T.yx[:, :], ap(xout))], 131072, r=subs(xout, 2))
+    dma("Y", [(T.ylm[:, :], nxt[:, 0:2048])], 1048576, r=RECN)
     return ops
 
 
 def links(ops):
     lastw, readers = {}, {}
-    succ = [[] for _ in ops]
     for i, o in enumerate(ops):
         d = set(lastw[k] for k in o["r"] + o["w"] if k in lastw)
         for k in o["w"]:
             d.update(readers.get(k, []))
-        for t in o["t"]:
-            d.update(t["ops"][-1:])
-            t["ops"].append(i)
         d.discard(i)
         o["d"] = d
-        for j in d:
-            succ[j].append(i)
         for k in o["r"]:
             readers.setdefault(k, []).append(i)
         for k in o["w"]:
             lastw[k] = i
             readers[k] = []
-    return succ
 
 
-def plan(ops, order):
+def lay(ops):
     n = len(ops)
-    succ = links(ops)
-    assert len(order) == 2 * n
-    rank = [62 * LETTERS.index(order[2 * i]) + LETTERS.index(order[2 * i + 1]) for i in range(n)]
+    succ = [[] for _ in ops]
     for i, o in enumerate(ops):
-        o["flex"] = o["e"] == "F"
-        if o["flex"]:
-            o["e"] = "V" if rank[i] % 2 else "S"
-            o["c"] = o["cost"][o["e"]]
-        if o["k"] == "d" and not o["r"]:
-            rank[i] = i - 10 ** 9
-    left = [len(o["d"]) for o in ops]
-    rdy = [0.0] * n
-    busy = {e: [] for e in "VSPGY"}
-    ready = [i for i in range(n) if left[i] == 0]
-    while ready:
-        i = min(ready, key=lambda j: (rank[j], j))
-        ready.remove(i)
-        o = ops[i]
-        b, st = busy[o["e"]], rdy[i]
-        k = len(b)
-        while k > 0 and b[k - 1][1] > st:
-            k -= 1
-        while k < len(b) and b[k][0] < st + o["c"]:
-            st = max(st, b[k][1])
-            k += 1
-        b.insert(k, (st, st + o["c"]))
-        o["st"] = st
-        for j in succ[i]:
-            e = ops[j]["e"]
-            hop = 0.0 if o["e"] == e == "P" else o["lat"] + (SAME if o["e"] == e else OTHER)
-            rdy[j] = max(rdy[j], st + o["c"] + hop)
-            left[j] -= 1
-            if left[j] == 0:
-                ready.append(j)
-    seq = sorted(range(n), key=lambda i: (ops[i]["st"], i))
-    bank = [None] * 8
-    for i in seq:
-        for t in ops[i]["t"]:
-            if t["bank"] is None:
-                tb, b = min((-1e9 if bank[b] is None else ops[bank[b]]["st"] + ops[bank[b]]["c"], b) for b in range(8))
-                assert tb <= ops[i]["st"]
-                if bank[b] is not None:
-                    ops[i]["d"].add(bank[b])
-                t["bank"] = b
-                bank[b] = t["ops"][-1]
-    return seq, max(o["st"] + o["c"] + o["lat"] for o in ops)
+        for j in o["d"]:
+            succ[j].append(i)
+
+    def hop(i, j):
+        a, b = ops[i], ops[j]
+        return 0.0 if a["e"] == b["e"] == "P" else a["lat"] + CFG["same" if a["e"] == b["e"] else "psum" if a["e"] == "P" else "other"]
+    key = [-99.0 if o["k"] == "d" and not o["r"] else o["tv"][0] + CFG["pos"].get((o["name"], o["tv"][1]), 99.0) for o in ops]
+    for i in reversed(range(n)):
+        key[i] = min([key[i]] + [key[j] for j in succ[i]])
+
+    def sweep(order, back):
+        rdy = [o["lat"] if back else 0.0 for o in ops]
+        end = [0.0] * n
+        busy = {e: [] for e in "VSPGY"}
+        for i in order:
+            o = ops[i]
+            b, st = busy[o["e"]], rdy[i]
+            k = len(b)
+            while k > 0 and b[k - 1][1] > st:
+                k -= 1
+            while k < len(b) and b[k][0] < st + o["c"]:
+                st = max(st, b[k][1])
+                k += 1
+            end[i] = st + o["c"]
+            b.insert(k, (st, end[i]))
+            for j in o["d"] if back else succ[i]:
+                rdy[j] = max(rdy[j], end[i] + (hop(j, i) if back else hop(i, j)))
+        return end
+    end = sweep(sorted(range(n), key=lambda i: (key[i], i)), False)
+    tries = [end]
+    for _ in range(CFG["turns"]):
+        late = sweep(sorted(range(n), key=lambda i: (-end[i], -i)), True)
+        end = sweep(sorted(range(n), key=lambda i: (-1e9 if key[i] < -90 else -late[i], i)), False)
+        tries.append(end)
+    end = min(tries, key=lambda x: max(x[i] + ops[i]["lat"] for i in range(n)))
+    for i, o in enumerate(ops):
+        o["st"] = end[i] - o["c"]
+    return sorted(range(n), key=lambda i: (ops[i]["st"], i))
+
+
+def plan(ops):
+    links(ops)
+    return lay(ops)
 
 
 def rank_program(g, core, T, topo):
     if T.rank_of(core) is None:
         return
     ops = build(g, core, T, topo)
-    seq, _ = plan(ops, ORDER)
+    seq = plan(ops)
     queue = {"V": g.vector, "S": g.scalar, "P": g.tensor, "G": g, "Y": g.sync}
     count, waited, nd = {}, {}, [0]
     for i in seq:

@@ -4,43 +4,52 @@ from concourse.mybir import AluOpType, ActivationFunctionType
 OP = AluOpType
 AF = ActivationFunctionType
 RO, NH, H = 4, 2, 128
-VOID0, FEAT0 = 1024, 1040
+FEAT0 = 1024
 MEM0 = 2080
 W19 = float(2 ** 19)
 MAGIC = 1.5 * 2.0 ** 42
 MAGIC1 = 1.5 * 2.0 ** 23
 LOW = 2.0 ** 23
 CFG = {
-    "pos": {},
-    "on_v": [],
-    "chunks": 2,
-    "same": 90.0, "other": 260.0, "psum": 440.0, "remote": 1200.0,
-    "pe": 0.45, "turns": 1, "rate": 400.0, "double": True,
+    "on_v": set(),
+    "chunks": {"mem1": 2, "feat": 4, "mem2": 4},
+    "stack1": False, "stack2": False,
+    "same": 85.0, "other": 180.0, "psum": 360.0, "far": 120.0, "row": 30.0,
+    "pe": 0.44, "rate": 400.0, "slack": 0.3, "pos": {}, "period": 27.0,
+    "rounds": 80000, "warm": 200.0, "cool": 40.0, "seed": 3, "early": 2, "late": 0, "mean": 0.1, "onpath": 0.95, "jump": 0.5,
 }
-
-ORDER = """pe1 pe0- set1r1- setm0 ofu1 jq1- mem1l0 mv0++ distc0+ mem2l1 sp0 x20 cmp1b0- mem1b1 feata1++ cmp1d1- yo0+++ ys1+ mem2a1- mem2l0 thr0 cmp2d1- setpr1+ ofu0 setm1 fs0+ wl0 distb1- sb1 feata0 su1 mem2b0+ mem1b0- distd0+ cmp2b0 up1 mem2b1- set11- x21 sn0 mask0- old0- n00- set10- setp0 su21 osn1- fs1 distd1 wl1 cmp2c1- mem1a1- cmp2a1- cmp1b1- j1-- sr0+ cmp1a0 dista0+ up0+ cmp1c0- of0+ mv1 su0- zg0 vo0 cmp1d0+ cmp1c1- cmp2d0 nu0 scat0+ n01- old1- sr1- scat1- cmp2c0- set1r0- osn0- featb1- setmr0- setp1 distc1 mem1l1- distb0 eqb1 sp1+ mem1a0- cmp2a0- arg1 featb0- cnt0- sb0- su20- ys0++ cmp2b1 setmr1- of1 j0-- nu1- eqb0 jq0-- yo1- mask1-- arg0- mem2a0- setpr0- zg1 dista1- cmp1a1 vo1- sn1-""".split()
-ON_V = """cmp1b0 cmp1c0 cmp1d1 cmp1d3 cmp2b1 cnt2 dista0 dista2 dista3 distb1 distc1 distc3 distd3 eb0 feata2 featb0 fs2 jq1 jq2 jq3 k00 k10 k20 k30 mask1 mem00 mem1l0 nu0 nu2 osn1 osn3 pm00 rec00 sb1 sb3 set1r0 set1r1 set1r2 set1r3 setmr0 setmr2 setmr3 setpr0 setpr2 sh0 sn0 sn1 sn3 sp0 sp3 sr2 sr3 su0 su1 up0 vo2 x22 x23""".split()
+ORDER = """and0 mem00 su1 jq1 j1 mask1 jq0 j0 su0 mask0 mem1l1 mem11 mem1l0 pe1 n01 nu1 mem10 cmp1d1 cmp1b1 copy0 cmp1c1 cmp1a1 featd1 pe0 featc1
+feata1 n00 cmp1a0 featb1 cmp1d0 cmp1c0 set1r1 cmp1b0 nu0 dista1 featc0 set11 distc1 distd1 feata0 distb1 featd0 featb0 xc1 arg1 set1r0 dista0 ls1 of1 fs1 sn1
+set10 distb0 su21 mv1 mem2l1 zg1 x21 eqb1 distd0 distc0 xc0 mem21 newm1 newr1 oth1 old1 ys1 arg0 wl1 cmp2b1 ls0 scat1 of0 cmp2a1 sn0 fs0 su20 mem2l0 mv0 cmp2c1 zg0 eqb0 x20
+newm0 newr0 mem20 old0 cmp2d1 ys0 wl0 scat0 cmp2a0 set2r1 cmp2b0 cmp2d0 set21 cmp2c0 oth0 yo1 set2r0 cnt0 yo0 set20 thr0""".split()
+ON_V = "jq0 of set1r1 set2r1 su2 dista1 distb1 distc1 distd1 maskS1 newrS oldS cmp1LS cmp2LS".split()
 for _i, _x in enumerate(ORDER):
-    CFG["pos"][_x.strip("+-")[:-1], int(_x.strip("+-")[-1])] = _x.count("+") - _x.count("-") + _i / len(ORDER)
-CFG["on_v"] = [(_x[:-1], int(_x[-1])) for _x in ON_V]
+    if _x != "|":
+        CFG["pos"][_x[:-1], int(_x[-1])] = (_i - 8) * 0.36
+for _x in ON_V:
+    CFG["on_v"].update([(_x[:-1], int(_x[-1]) + _h) for _h in (0, 2)] if _x[-1] in "01" else [(_x, _h) for _h in range(4)])
+CFG["on_v"] -= {("maskS", 3), ("cmp1LS", 2), ("cmp1LS", 3)}
 
 SCRATCH = {
     "fw": ("sbuf", [128, FEAT0 + 4096], "bfloat16"),
+    "snr": ("sbuf", [128, FEAT0 + 4096], "int32"),
     "tab": ("sbuf", [128, 2 * MEM0], "float32"),
+    "tab1": ("sbuf", [128, 2 * MEM0], "float32"),
     "lmi": ("sbuf", [128, 2048], "int32"),
     "lmt": ("sbuf", [128, 2048], "int32"),
-    "snr": ("sbuf", [128, 4096], "int32"),
-    "tab1": ("sbuf", [128, 2 * MEM0], "float32"),
     "ramp": ("sbuf", [128, 2048], "float32"),
-    "af": ("sbuf", [128, 8704], "float32"),
-    "ab": ("sbuf", [128, 29696], "bfloat16"),
-    "ah": ("sbuf", [128, 18944], "float16"),
-    "ai": ("sbuf", [128, 3072], "int32"),
-    "au": ("sbuf", [128, 5120], "uint16"),
+    "af": ("sbuf", [128, 5760], "float32"),
+    "ab": ("sbuf", [128, 36864], "bfloat16"),
+    "ah": ("sbuf", [128, 18432], "float16"),
+    "ai": ("sbuf", [128, 2048], "int32"),
+    "au": ("sbuf", [128, 4480], "uint16"),
 }
+for _b in range(NH):
+    SCRATCH["old%d" % _b] = ("sbuf", [128, 8, 32], "float32")
+    SCRATCH["new%d" % _b] = ("sbuf", [128, 8, 32], "float32")
 for _b in range(8):
     SCRATCH["ps%d" % _b] = ("psum", [128, 512], "float32")
-SEMAPHORES = ["cV", "cS", "cP", "cG", "left"] + ["d%d" % i for i in range(40)] + ["a%d" % i for i in range(30)]
+SEMAPHORES = ["cV", "cS", "cP", "cG", "left"] + ["d%d" % i for i in range(40)] + ["a%d" % i for i in range(24)]
 
 CY, GA, SC = 0.85, 1.28, 3.1
 
@@ -53,8 +62,6 @@ def build(g, core, T, topo):
     kept = {}
     cur = [(-1, 0)]
     V, S, P = g.vector, g.scalar, g.tensor
-    NC = CFG["chunks"]
-    CW = 2048 // NC
 
     def al(arena, w):
         a = used[arena]
@@ -67,17 +74,15 @@ def build(g, core, T, topo):
             kept[name, h] = al(arena, w)
         return kept[name, h]
 
-    def part(b, lo, w):
-        return [b[0], b[1] + lo, w, b[3]]
-
     def ap(b, lo=0, hi=None, step=1, p1=128):
         hi = b[2] if hi is None else hi
+        p0, p1 = p1 if isinstance(p1, tuple) else (0, p1)
         if step == 1:
-            return T[b[0]][0:p1, b[1] + lo:b[1] + hi]
-        return T[b[0]][0:p1, b[1] + lo:b[1] + hi:step]
+            return T[b[0]][p0:p1, b[1] + lo:b[1] + hi]
+        return T[b[0]][p0:p1, b[1] + lo:b[1] + hi:step]
 
     def sub(b, q):
-        return "%s/%d" % (b[3], q)
+        return "%s/%s" % (b[3], q)
 
     def subs(b, m):
         return [sub(b, q) for q in range(m)]
@@ -85,16 +90,26 @@ def build(g, core, T, topo):
     def keys(xs):
         return [x if isinstance(x, str) else x[3] for x in xs]
 
-    def op(eng, fn, cost, r=(), w=(), t=(), lat=0.0, kind="c", name=""):
-        ops.append({"e": eng, "fn": fn, "c": float(cost), "r": keys(r), "w": keys(w) + list(t), "lat": lat, "k": kind, "tv": cur[0], "name": name, "flex": False, "free": False})
+    def op(eng, fn, cost, r=(), w=(), t=None, lat=0.0, kind="c", name=""):
+        ops.append({"e": eng, "fn": fn, "c": float(cost), "r": keys(r), "w": keys(w), "t": t, "lat": lat, "k": kind, "tv": cur[0], "name": name, "flex": False})
+        if t is not None:
+            t["n"] += 1
 
-    def tile(kind):
-        return "ps%d" % (4 * (cur[0][1] % 2) + kind)
+    tiles = [0]
+
+    def tile(own=None):
+        tiles[0] += 1
+        return {"id": "t%d" % tiles[0], "own": own, "n": 0, "b": None, "open": False, "shut": False, "due": 0, "keys": []}
 
     def ps(t, lo, hi, step=1, p1=128):
+        p0, p1 = p1 if isinstance(p1, tuple) else (0, p1)
         if step == 1:
-            return T[t][0:p1, lo:hi]
-        return T[t][0:p1, lo:hi:step]
+            return T["ps%d" % t["b"]][p0:p1, lo:hi]
+        return T["ps%d" % t["b"]][p0:p1, lo:hi:step]
+
+    def got(t):
+        t["shut"] = True
+        return list(t["keys"])
 
     def vc(w, rate=1.0):
         return 5 + max(64, w * rate) * CY
@@ -110,7 +125,7 @@ def build(g, core, T, topo):
     def vts(o, i, s1, s2, o0, o1=None, r=()):
         op("V", lambda: [ts(ap(o), ap(i), s1, s2, o0, o1)], vc(o[2]), [i] + list(r), [o])
 
-    def v1(name, fn, w, r, wr, t=(), rate=1.0):
+    def v1(name, fn, w, r, wr, t=None, rate=1.0):
         op("V", lambda: [fn()], vc(w, rate), r, wr, t, name=name)
 
     def gat(name, fn, w, r, wr):
@@ -125,16 +140,20 @@ def build(g, core, T, topo):
             return ts(o, i, bias, 0.0, OP.add, OP.max)
         return ts(o, i, scale, bias, OP.mult, OP.add)
 
-    def engine(name, h=None):
-        return "V" if (name, cur[0][1] + 2 * (cur[0][0] == 0) if h is None else h) in CFG["on_v"] else "S"
+    def engine(name):
+        return "V" if (name, cur[0][1] + 2 * (cur[0][0] <= 0)) in CFG["on_v"] else "S"
 
-    def flex(name, fn, cs, cv, r=(), w=(), t=()):
+    def other(name):
+        return engine(name + "S") == "V"
+
+    def flex(name, fn, cs, cv, r=(), w=(), t=None):
         e = engine(name)
         op(e, fn, cs if e == "S" else cv, r, w, t, name=name)
         ops[-1]["flex"] = True
+        ops[-1]["alt"] = [("S", cs), ("V", cv)]
 
-    def lin(name, o, i, n_, r, w, t=(), func=AF.Identity, bias=0.0, scale=1.0):
-        flex(name, lambda e, _: [act(e, o, i() if t else i, func, bias, scale)], sc(n_), vc(n_), r, w, t)
+    def lin(name, o, i, n_, r, w, t=None, func=AF.Identity, bias=0.0, scale=1.0, rate=1.0):
+        flex(name, lambda e, _: [act(e, o, i() if t else i, func, bias, scale)], sc(n_), vc(n_, rate), r, w, t)
 
     def sact(o, i, bias=0.0, scale=1.0, r=()):
         op("S", lambda: [S.activation(ap(o), ap(i, 0, o[2]), AF.Identity, bias=bias, scale=scale)], sc(o[2]), [i] + list(r), [o])
@@ -142,28 +161,30 @@ def build(g, core, T, topo):
     def pick(name, o, lo, hi, win, lst, a, b, r, w):
         flex(name, lambda e, _: [act(e, ap(o, lo, hi), win.indirect(ap(lst, a, b)))], 75 + (hi - lo) * GA, 60 + (hi - lo) * GA, r + [lst], w)
 
-    def rounded(name, o, okey, tl, w, magic, r1, lo=0):
+    def rounded(name, o, okey, tl, lo, w, magic, r1, r):
         def fn(e, chain):
             if e == "V":
                 return [ts(o, ps(tl, lo, lo + w), magic, -magic, OP.add, OP.add)]
             chain(S.activation(ap(r1), ps(tl, lo, lo + w), AF.Identity, bias=magic))
             return [S.activation(o, ap(r1), AF.Identity, bias=-magic)]
-        flex(name, fn, 2 * sc(w) + 60, vc(w), [], [okey, r1], [tl])
+        flex(name, fn, 2 * sc(w) + 60, vc(w), r, [okey, r1], tl)
 
-    def mm(t, calls, cyc, r, name=""):
+    def mm(t, calls, cyc, r):
         def fn():
             last = None
             for c in calls:
-                last = P.matmul(ps(t, c[0], c[1], c[2], c[7] if len(c) > 7 else 128), c[3], c[4], c[5], c[6])
+                t["due"] -= 1
+                last = P.matmul(ps(t, c[0], c[1], c[2], c[5] if len(c) > 5 else 128), c[3], c[4], not t["open"], t["due"] == 0)
+                t["open"] = True
             return [last]
-        op("P", fn, 10 + cyc * CFG["pe"], r, [], [t], name=name)
+        t["due"] += len(calls)
+        assert not t["shut"]
+        t["keys"].append("%s/%d" % (t["id"], len(ops)))
+        op("P", fn, 10 + cyc * CFG["pe"], r, t["keys"][-1:], t)
 
-    clock = [1500.0]
-
-    def dma(q, pairs, nbytes, r=(), w=()):
-        clock[0] += nbytes / CFG["rate"] if not r else 0.0
+    def dma(q, pairs, nbytes, r=(), w=(), name="dma", rows=128):
         eng = g.sync if q == "Y" else g.scalar
-        op(q, lambda: [eng.dma_start(o, i) for o, i in pairs], 60 * len(pairs), r, w, lat=(clock[0] if not r else 1500 + nbytes / CFG["rate"]), kind="d")
+        op(q, lambda: [eng.dma_start(o, i) for o, i in pairs], 60 * len(pairs), r, w, lat=nbytes / CFG["rate"] + rows / 16 * CFG["row"], kind="d", name=name)
 
     arr = [0]
 
@@ -174,7 +195,7 @@ def build(g, core, T, topo):
         m = sum(1 << e for e in eng)
         sem = "a%d" % arr[0]
         arr[0] += 1
-        op("G", lambda: [g.remote_dma(out, in_, T.sem[sem], T.sem.left, pid, rid, m)], 400, r, w, lat=CFG["remote"] + nbytes / 50.0, kind="r", name="send")
+        op("G", lambda: [g.remote_dma(out, in_, T.sem[sem], T.sem.left, pid, rid, m)], 400, r, w, lat=nbytes / CFG["far"] + 16 * CFG["row"], kind="r", name="send")
         ops[-1]["sem"] = sem
         ops[-1]["n"] = len(eng)
 
@@ -185,27 +206,27 @@ def build(g, core, T, topo):
         return T.fw[:, strip(t, h):strip(t, h) + H]
 
     s0, vt0, lpq = al("ai", 256), al("ai", 512), al("ai", 512)
-    dma("Y", [(ap(s0, p1=8), T.ls[:, :])], 8192, w=[s0])
-    dma("S", [(xap(0, h), T.lx[:, H * h:H * h + H]) for h in range(NH)], 65536, w=["x00", "x01"])
+    dma("Y", [(ap(s0, p1=8), T.ls[:, :])], 8192, w=[s0], name="load")
+    dma("S", [(xap(0, h), T.lx[:, H * h:H * h + H]) for h in range(NH)], 65536, w=["x00", "x01"], name="load")
     for q in range(4):
-        dma("YS"[q % 2], [(T.lmi[:, 512 * q:512 * q + 512], T.lm[:, 512 * q:512 * q + 512])], 262144, w=["lmi%d" % q])
-    dma("Y", [(ap(lpq, 0, 256), T.lp[:, :]), (ap(lpq, 256, 512), T.lq[:, :])], 262144, w=[lpq])
-    dma("Y", [(T.fw[:, FEAT0:FEAT0 + 4096], T.feat[:, :])], 1048576, w=["feat"])
-    dma("Y", [(ap(vt0, 0, 256, p1=8), T.lv[:, :]), (ap(vt0, 256, 512, p1=8), T.th[:, :])], 16384, w=[vt0])
-    dma("Y", [(T.snr[i:128:16, :], T.sn[:, :]) for i in range(16)], 2097152, w=["snr"])
+        dma("YS"[q % 2], [(T.lmi[:, 512 * q:512 * q + 512], T.lm[:, 512 * q:512 * q + 512])], 262144, w=["lmi%d" % q], name="load")
+    dma("Y", [(ap(lpq, 0, 256), T.lp[:, :]), (ap(lpq, 256, 512), T.lq[:, :])], 262144, w=[lpq], name="load")
+    dma("Y", [(T.fw[:, FEAT0:FEAT0 + 4096], T.feat[:, :])], 1048576, w=["feat"], name="load")
+    dma("Y", [(ap(vt0, 0, 256, p1=8), T.lv[:, :]), (ap(vt0, 256, 512, p1=8), T.th[:, :])], 16384, w=[vt0], name="load")
+    dma("Y", [(T.snr[i:128:16, FEAT0:FEAT0 + 4096], T.sn[:, :]) for i in range(16)], 2097152, w=["snr"], name="load")
 
     def iota(arena, pat, base, cm):
         b = al(arena, math.prod(c for _, c in pat))
         if arena == "ai":
-            op("G", lambda: [g.iota(ap(b), pat, base, cm)], 130 + 2 * b[2], [], [b])
+            op("G", lambda: [g.iota(ap(b), pat, base, cm)], 130 + 1.7 * b[2], [], [b])
         else:
-            op("G", lambda: [g.iota(ap(b), pat, base, cm, allow_small_or_imprecise_dtypes=True)], 130 + 2 * b[2], [], [b])
+            op("G", lambda: [g.iota(ap(b), pat, base, cm, allow_small_or_imprecise_dtypes=True)], 130 + 1.7 * b[2], [], [b])
         return b
 
     def where(src, pat, cmp, base, cm, arena="ab", w=None):
         m = math.prod(c for _, c in pat)
         b = al(arena, w or m)
-        op("G", lambda: [g.affine_select(ap(b, 0, m), ap(src, 0, m), pat, cmp, 0.0, base, cm)], 170 + 2 * m, [src], [b])
+        op("G", lambda: [g.affine_select(ap(b, 0, m), ap(src, 0, m), pat, cmp, 0.0, base, cm)], 170 + 1.7 * m, [src], [b])
         return b
 
     def in_group(src, pat):
@@ -219,351 +240,434 @@ def build(g, core, T, topo):
 
     ones = al("ab", 256)
     op("V", lambda: [V.memset(ap(ones), 1.0)], vc(256, 0.5), [], [ones])
-    op("V", lambda: [V.memset(T.fw[:, VOID0:FEAT0], 16384.0), V.memset(T.tab[:, 2048:MEM0], 0.0), V.memset(T.tab[:, MEM0 + 2048:2 * MEM0], 0.0)],
-       3 * vc(16), [], ["void", "pad0", "padm0"])
+    op("V", lambda: [V.memset(T.tab[:, MEM0 + 2048:2 * MEM0], 0.0), V.memset(T.tab1[:, 2048:MEM0], 0.0)], 2 * vc(16), [], ["padm0", "pad1"])
     bo = in_group(ones, [[-16, 8], [0, 16]])
     ib = where(ones, [[-1, 128]], OP.is_equal, 0, 1)
     wsel = where(ones, [[1, 144]], OP.is_equal, -15, -16)
     keep = where(ones, [[0, 8], [1, 16]], OP.not_equal, 0, 0)
-    keep8 = where(ones, [[0, 16], [1, 8]], OP.not_equal, 0, 0)
     bo8 = in_group(ones, [[0, 16], [-16, 8]])
-    perm = [where(ones, [[-16, 8], [-1, 8], [0, 2]], OP.is_equal, -8 * m, 1) for m in range(2)]
-    shift = where(ones, [[-1, 16], [-16, 8]], OP.is_equal, 0, 1, w=1024)
-    for a in (128, 256, 512):
-        op("S", lambda a=a: [S.activation(ap(shift, a, 2 * a), ap(shift, 0, a), AF.Identity)], sc(a), [shift], [shift])
-    ioq, ion, pc, ioa = iota("ai", [[0, 1]], 0, 1), iota("ai", [[-1, 20]], 32, 1), iota("af", [[0, 16], [1, 16]], 0, 0), iota("ai", [[1, 128]], 0, 1)
+    shift = al("ab", 1024)
+    for a in range(4):
+        op("G", lambda a=a: [g.affine_select(ap(shift, 256 * a, 256 * a + 256), ap(ones), [[0, 2], [-1, 16], [-16, 8]], OP.is_equal, 0.0, 0, 1)], 170 + 1.7 * 256, [ones], [sub(shift, a)])
+    zeros = al("ab", H)
+    op("V", lambda: [V.memset(ap(zeros), 0.0)], vc(H, 0.5), [], [zeros])
+
+    def eye(k):
+        b = al("ab", H)
+        op("G", lambda: [g.affine_select(ap(b), ap(zeros), [[-1, H]], OP.not_equal, float(k), 0, 1)], 170 + 1.7 * H, [zeros], [b])
+        return b
+    wall = scaled(in_group(where(ones, [[0, 9], [1, 16]], OP.is_equal, -15, 0), [[-16, 9], [0, 16]]), 4096)
+    ioq, ion, pc, ioa = iota("ai", [[0, 1]], 0, 1), iota("ai", [[-1, 20]], 32, 1), iota("af", [[0, 8], [1, 16]], 0, 0), iota("ai", [[1, 128]], 0, 1)
     c8, c16 = iota("ai", [[1, 8]], 0, 0), iota("af", [[16, 8]], 0, 0)
-    op("G", lambda: [g.iota(T.ramp[:, :], [[1, 2048]], 0, 0, allow_small_or_imprecise_dtypes=True)], 4300, [], ["ramp"], name="late")
-    pqi, pui, ni, pa = al("ai", 1), al("ai", 1), al("ai", 20), al("ai", 128)
-    pq, pu, odd, memo = [al("af", 1) for _ in range(4)]
-    cols, diag, paf, tra, l_col, lane8 = al("ab", 20), al("ab", 256), al("ab", 128), al("ab", 256), al("au", 8), al("af", 8)
+    for q in range(4):
+        op("G", lambda q=q: [g.iota(T.ramp[:, 512 * q:512 * q + 512], [[4096, 512]], 2048 + 4096 * 512 * q, 0, allow_small_or_imprecise_dtypes=True)], 1000, [ib], ["ramp%d" % q])
+    RAMP = ["ramp%d" % q for q in range(4)]
+    op("G", lambda: [g.iota(T.snr[:, 0:FEAT0], [[0, FEAT0]], 0, 0)], 130 + 1.7 * FEAT0, [ib], ["snpad"])
+    pqi, ni, pa, pq = al("ai", 1), al("ai", 20), al("ai", 128), al("af", 1)
+    cols, diag, paf, l_col, lane8 = al("ab", 20), al("ab", H), al("ab", 128), al("au", 8), al("af", 8)
+    pen0, pen1, pen = al("ab", H), al("ab", H), al("ab", H)
     vts(pqi, ioq, 15, None, OP.bitwise_and)
     vts(pq, pqi, 1.0, None, OP.mult)
-    vts(pui, pqi, 1, None, OP.logical_shift_right)
-    vts(pu, pui, 1.0, None, OP.mult)
     vts(ni, ion, 15, None, OP.bitwise_and)
     vts(cols, ni, 1.0 / 16, None, OP.mult)
     vts(diag, pc, ap(pq), None, OP.is_equal, r=[pq])
+    vts(pen0, pc, ap(pq), -2048.0, OP.not_equal, OP.mult, r=[pq])
+    vts(pen1, pc, ap(pq), -4096.0, OP.is_lt, OP.mult, r=[pq])
+    v1("", lambda: V.tensor_tensor(ap(pen), ap(pen0), ap(pen1), OP.add), H, [pen0, pen1], [pen], rate=2.0)
     vts(pa, ioa, 1, None, OP.bitwise_and)
     vts(paf, pa, -1.0, 8192.0, OP.add, OP.mult)
     par = in_group(paf, [[-16, 8], [0, 16]])
-    vts(tra, pc, ap(pq), 4096.0, OP.is_gt, OP.mult, r=[pq])
-    trb, trip = where(tra, [[1, 8], [0, 4], [-1, 8]], OP.is_equal, 0, 0), al("ab", 2048)
-    bo32 = scaled(bo8, 1, "af")
-
-    def spread(name, o, src):
-        for k in range(8):
-            flex(name, lambda e, _, k=k: [act(e, ap(o, 256 * k, 256 * k + 256), ap(src), AF.Identity, 0.0, ap(bo32, k, k + 1))], sc(256), vc(256, 0.5),
-                 [src, bo32], [sub(o, k)])
-    spread("trip", trip, trb)
     vts(l_col, c8, 1.0, None, OP.mult)
     vts(lane8, c16, ap(pq), None, OP.add, r=[pq])
-    dum = [scaled(pu, 1, "af", 2048.0 + 8 * m) for m in range(2)]
-    sact(odd, pu, scale=-2.0, bias=ap(pq), r=[pq])
-    sact(memo, odd, scale=float(MEM0))
-    dum2, least = [al("af", 1) for _ in range(2)], [al("af", 1) for _ in range(2)]
-    for m in range(2):
-        sact(dum2[m], odd, scale=16.0, bias=ap(dum[m]), r=[dum[m]])
-        sact(least[m], dum2[m], scale=ap(odd), r=[odd])
-    bo_16, bow, bo16, bo16n, bo32b, bo2p = [scaled(bo, k) for k in (1.0 / 16, -W19, 16, -16, 32, 2)]
-    bo2n = al("ab", 256)
-    op("S", lambda: [S.activation(ap(bo2n, a, a + H), ap(bo), AF.Identity, scale=-2.0) for a in (0, H)], 2 * sc(H), [bo], [bo2n])
-    ineg, i16n, ihalf, iquar, i8n, iw, ilow, i64k, i128, i128n, i4k = [scaled(ib, k) for k in (-1, -16, 0.5, -0.25, -8192, -W19, LOW, -65536, 128, -128, 4096)]
-    if {engine("old", h) for h in range(4)} != {"V"}:
-        ihigh = scaled(ib, -2.0 ** 24)
-    if {engine("mask", h) for h in range(4)} != {"V"}:
-        colr = [scaled(pq, 1, "af", float(t)) for t in range(RO)]
-    if {engine("sn", h) for h in range(4)} != {"V"}:
-        wall = in_group(where(ones, [[0, 9], [1, 16]], OP.is_equal, -15, 0), [[-16, 9], [0, 16]])
+    dum = scaled(pq, 1, "af", 2048.0)
+    bo_16, bo16 = scaled(bo, 1.0 / 16), scaled(bo, 16)
+    bo32 = in_group(ones, [[-16, 8], [0, 32]])
+    bo4p, bo4n = scaled(bo32, 4), scaled(bo32, -4)
+    ineg, i16n, ihalf, iquar, i8n, ilow, i64k, i128, i128n = [eye(k) for k in (-1, -16, 0.5, -0.25, -8192, LOW, -65536, 128, -128)]
+    if any(x[0][:4] == "dist" for x in CFG["on_v"]):
+        bo16n, bo32b = scaled(bo, -16), scaled(bo, 32)
+    if not (CFG["stack1"] and CFG["stack2"]):
+        bow, iw = scaled(bo, -W19), eye(-W19)
     i32 = scaled(ib, 1, "af")
+    forms = set(x[0] for x in CFG["on_v"])
+    if "maskS" in forms:
+        colr = [scaled(pq, 1, "af", float(t)) for t in range(RO)]
+    if "oldS" in forms:
+        ihigh = eye(-2.0 ** 24)
+    if forms & {"cmp1LS", "cmp2LS"}:
+        wide, minus = al("ab", 2048), al("ab", 512)
+        op("V", lambda: [V.memset(ap(minus), -1.0)], vc(512, 0.5), [], [minus])
+        for q in range(4):
+            op("G", lambda q=q: [g.affine_select(ap(wide, 512 * q, 512 * q + 512), ap(minus), [[-1, 32], [0, 16]], OP.is_equal, 0.0, -32 * q, 1)], 170 + 1.7 * 512, [minus], [sub(wide, q)])
+    if "newrS" in forms:
+        i4k = eye(4096)
     d0 = scaled(keep, -2.0 ** 23 - 1, "af", 2.0 ** 23)
-    rst8, offm = scaled(keep8, 2.0 ** 21, "af", -2.0 ** 21), scaled(bo8, 2.0 ** 20, "ab", -2.0 ** 20)
-    xc = {}
-    for t in range(RO):
-        for h in range(NH):
-            xc[t, h] = scaled(lane8, 1, "af", -float(FEAT0 - strip(t, h) + 2048))
+    rst16 = scaled(keep, 8192, "ab", -8192.0)
+    offm = scaled(bo8, 2.0 ** 20, "ab", -2.0 ** 20)
+    rst = {h: al("af", H) for h in range(NH)}
+    for h in range(NH):
+        op("V", lambda h=h: [V.memset(ap(rst[h]), 2.0 ** 21)], vc(H), [], [rst[h], sub(rst[h], 0)])
+        op("V", lambda h=h: [V.memset(ap(rst[h], 8, H, 16), -2.0 ** 21)], vc(8), [], [rst[h]])
+    if CFG["stack1"] or CFG["stack2"]:
+        dif, red = al("ab", 1024), al("ab", 256)
+        for q in range(4):
+            op("G", lambda q=q: [g.affine_select(ap(dif, 256 * q, 256 * q + 256), ap(ones), [[0, 16], [-32, 2], [-2, 8]], OP.is_equal, 0.0, -64 * (q // 2) - 16 * (q % 2) - 1, 1)],
+               170 + 1.7 * 256, [ones], [sub(dif, q)])
+            op("G", lambda q=q: [g.affine_select(ap(dif, 256 * q, 256 * q + 256), ap(dif, 256 * q, 256 * q + 256), [[-2, 16], [-32, 2], [0, 8]], OP.not_equal, -1.0, -64 * (q // 2), 1)],
+               170 + 1.7 * 256, [sub(dif, q)], [sub(dif, q)])
+        tl = tile()
+        mm(tl, [(64 * u, 64 * u + 64, 1, ap(dif, 128 * u, 128 * u + 128), ap(ib, 0, 64)) for u in range(4)], 256, [ib] + subs(dif, 2))
+        v1("", lambda tl=tl: ts(ap(red), ps(tl, 0, 256), 0.0, -W19, OP.not_equal, OP.mult), 256, got(tl), [red], tl)
 
     for q in range(4):
         a, b = 512 * q, 512 * q + 512
-        op("V", lambda a=a, b=b: [ts(T.lmt[:, a:b], T.lmi[:, a:b], 4095, None, OP.bitwise_and)], vc(512), ["lmi%d" % q], ["lmt%d" % q])
+        op("V", lambda a=a, b=b: [ts(T.lmt[:, a:b], T.lmi[:, a:b], 4095, None, OP.bitwise_and)], vc(512), ["lmi%d" % q], ["lmt%d" % q], name="and")
         lin("mem0", T.tab[:, MEM0 + a:MEM0 + b], T.lmt[:, a:b], 512, ["lmt%d" % q], ["mem%d" % q], bias=-2048.0)
-        lin("rec0", T.tab[:, a:b], T.lmi[:, a:b], 512, ["lmi%d" % q], ["rec%d" % q])
+    for q in range(4):
+        a, b = 512 * q, 512 * q + 512
+        lin("rec0", T.tab1[:, a:b], T.lmi[:, a:b], 512, ["lmi%d" % q, "mem3"], ["rec%d" % (q + 4)])
     sh, vth, thl, ea, eb = al("ah", 256), al("ah", 512), al("af", 16), al("ah", 512), al("ah", 512)
     lin("sh", ap(sh, p1=8), ap(s0, p1=8), 256, [s0], [sh])
     lin("vth", ap(vth, p1=8), ap(vt0, p1=8), 512, [vt0], [vth], bias=-2048.0)
-    t0, t1 = tile(1), tile(2)
-    mm(t0, [(0, 16, 1, ap(wsel, 15 - p, 143 - p, p1=8), ap(sh, p, 256, 16, p1=8), p == 0, p == 15) for p in range(16)], 16 * 64, [wsel, sh])
+    t0, t1 = tile(), tile()
+    mm(t0, [(0, 16, 1, ap(wsel, 15 - p, 143 - p, p1=8), ap(sh, p, 256, 16, p1=8)) for p in range(16)], 16 * 64, [wsel, sh])
     sv = {(t, h): al("af", 8) for t in range(RO) for h in range(NH)}
     vb = {(t, h): al("ah", H) for t in range(RO) for h in range(NH)}
     pm = {(t, h): al("ah", 256) for t in range(RO) for h in range(NH)}
     for h in range(NH):
-        op("S", lambda h=h: [S.activation(ap(sv[0, h]), ps(t0, 8 * h, 8 * h + 8), AF.Identity)], sc(8), [], [sv[0, h]], [t0])
+        lin("sv", ap(sv[0, h]), lambda h=h: ps(t0, 8 * h, 8 * h + 8), 8, got(t0), [sv[0, h]], t0)
     dma("Y", [(T.ah[i:128:16, vb[0, 0][1]:vb[0, 0][1] + 256], ap(vth, 0, 256, p1=8)) for i in range(16)], 65536, r=[vth], w=[vb[0, 0], vb[0, 1]])
-    mm(t1, [(8 * h, 8 * h + 8, 1, ap(vth, 256 + H * h, 256 + H * h + H, p1=8), ap(ib, 0, 8, p1=8), True, True) for h in range(NH)], 128, [vth, ib])
-    op("S", lambda: [S.activation(ap(thl), ps(t1, 0, 16), AF.Identity, bias=32768.0 - 15, scale=16.0)], sc(16), [], [thl], [t1])
+    mm(t1, [(8 * h, 8 * h + 8, 1, ap(vth, 256 + H * h, 256 + H * h + H, p1=8), ap(ib, 0, 8, p1=8)) for h in range(NH)], 128, [vth, ib])
+    lin("thl", ap(thl), lambda: ps(t1, 0, 16), 16, got(t1), [thl], t1, bias=32768.0 - 15, scale=16.0)
     op("S", lambda: [S.activation(ap(ea), ap(lpq), AF.Relu, scale=-2048.0)], sc(512), [lpq], [ea])
     lin("eb", ap(eb), ap(lpq), 512, [lpq], [eb], bias=-2048.0)
     for h in range(NH):
-        tl = tile(5 + h)
-        mm(tl, [(128 * m, 128 * m + 128, 1, ap(e, 256 * m + H * h, 256 * m + H * h + H), ap(ineg if e is ea else ib), e is ea, e is eb)
-                for m in range(2) for e in (ea, eb)], 512, [ea, eb, ib, ineg])
-        lin("pm0", ap(pm[0, h]), lambda tl=tl: ps(tl, 0, 256), 256, [], subs(pm[0, h], 2), [tl])
-    SNR = ["snr"]
+        tl = tile()
+        mm(tl, [(m, 256, 2, ap(e, 256 * m + H * h, 256 * m + H * h + H), ap(ineg if e is ea else ib)) for m in range(2) for e in (ea, eb)], 512, [ea, eb, ib, ineg])
+        lin("pm0", ap(pm[0, h]), lambda tl=tl: ps(tl, 0, 256), 256, got(tl), subs(pm[0, h], 2), tl)
 
     mask = {(u, h): al("ab", 2048) for u in range(2) for h in range(NH)}
-    gm = {h: al("ah", 2048) for h in range(NH)}
-    gn = {h: al("ah", 2048) for h in range(NH)}
-    sg = {h: al("ab", 2048) for h in range(NH)}
-    fb = {h: al("ab", 2048) for h in range(NH)}
+    gm, gn = [{h: al("ah", 2048) for h in range(NH)} for _ in range(2)]
+    sg1, sg2, fb, db = [{h: al("ab", 2048) for h in range(NH)} for _ in range(4)]
+    g2 = al("ab", 32 * RO)
+    op("V", lambda: [V.memset(ap(g2), 0.0)], vc(32 * RO, 0.5), [], subs(g2, NH * RO))
 
-    def members(name, dst, win, rw, lst, mk, tab, MEM):
-        a = al("au", H)
+    def members(name, dst, win, rw, lst, mk, tab, MEM, behind=()):
+        a, nc = al("au", H), CFG["chunks"][name]
+        cw = 2048 // nc
         flex(name + "l", lambda e, _: [act(e, ap(a), win.indirect(ap(lst)), AF.Identity, -0.5 + 1.0 / 8192, 1.0 / 4096)], 75 + H * GA, 60 + H * GA, rw + [lst], [a])
-        for q in range(NC):
-            gat(name + "abcd"[q], lambda q=q: V.tensor_tensor(ap(dst, CW * q, CW * q + CW), tab[:, MEM0:MEM0 + 2048].indirect(ap(a, CW // 16 * q, CW // 16 * (q + 1))),
-                                                  ap(mk, CW * q, CW * q + CW), OP.mult), CW, MEM + [a] + subs(mk, 4), [sub(dst, q)])
+        for q in range(nc):
+            out, col = ap(dst, cw * q, cw * q + cw), tab[:, MEM0:MEM0 + 2048].indirect(ap(a, cw // 16 * q, cw // 16 * (q + 1)))
+            if other(name + "abcd"[q]):
+                tl = tile()
+                op("S", lambda out=out, col=col: [act("S", out, col)], 75 + cw * GA, MEM + [a], [sub(dst, q)], name=name)
+                mm(tl, [(0, cw, 1, ap(ib), ap(mk, cw * q, cw * q + cw))], cw, [ib, sub(dst, q)] + subs(mk, 4))
+                v1(name + "m", lambda out=out, tl=tl: V.tensor_tensor(out, ps(tl, 0, cw), out, OP.mult), cw, got(tl), [sub(dst, q)], tl)
+            else:
+                gat(name, lambda out=out, col=col, q=q: V.tensor_tensor(out, col, ap(mk, cw * q, cw * q + cw), OP.mult), cw,
+                    MEM + [a] + subs(mk, 4) + (list(behind) if q >= nc - CFG["late"] else []), [sub(dst, q)])
+        return subs(dst, nc)
 
-    def compare(name, src, other, okey, h, after):
+    def steps(name, sg, b, tl):
+        if other(name):
+            v1(name + "abcd"[b], lambda: act("V", ap(sg, 512 * b, 512 * b + 512), ps(tl, 0, 512), AF.Sigmoid), 512, got(tl), [sub(sg, b)], tl)
+            return
+        flex(name + "abcd"[b], lambda e, _: [act(e, ap(sg, 512 * b, 512 * b + 512), ps(tl, 0, 512), AF.Sigmoid, -math.log(63.0), 64.0)],
+             sc(512), vc(512), got(tl), [sub(sg, b)], tl)
+
+    def compare(name, sg, src, skeys, other, okey, after):
+        if engine(name + "LS") == "V":
+            for b in range(4):
+                tl = tile()
+                mm(tl, [(0, 512, 1, other, ap(wide, 512 * b, 512 * b + 512)), (0, 512, 1, ap(bo), ap(src, 512 * b, 512 * b + 512))], 1024,
+                   [bo, sub(wide, b), okey, skeys[b * len(skeys) // 4]])
+                steps(name, sg, b, tl)
+            for b in range(4):
+                after(b, lambda k: ap(sg, k, 2048, 16), subs(sg, 4))
+            return
         for b in range(4):
-            tl = tile(1 + b % 2)
+            tl = tile()
             calls = []
             for u in range(4):
-                calls.append((128 * u, 128 * u + 128, 1, ap(bo), ap(src, 4 * b + u, 2048, 16), True, False))
-                calls.append((128 * u, 128 * u + 128, 1, other, ap(ineg), False, True))
-            mm(tl, calls, 1024, [bo, ineg, okey] + subs(src, NC))
-            flex(name + "abcd"[b], lambda e, _, b=b, tl=tl: [act(e, ap(sg[h], 512 * b, 512 * b + 512), ps(tl, 0, 512), AF.Sigmoid, -math.log(63.0), 64.0)],
-                 sc(512), vc(512), [], [sub(sg[h], b)], [tl])
-            after(b)
+                calls.append((128 * u, 128 * u + 128, 1, ap(bo), ap(src, 4 * b + u, 2048, 16)))
+                calls.append((128 * u, 128 * u + 128, 1, other, ap(ineg)))
+            mm(tl, calls, 1024, [bo, ineg, okey] + skeys)
+            steps(name, sg, b, tl)
+            after(b, lambda k: ap(sg, H * k, H * k + H), [sub(sg, b)])
 
-    def settle(name, tl, lo, o, okey, other, r, h):
-        rr, left = tmp(name + "r", h, H), tmp(name + "l", h, H)
-        rounded(name + "r", ap(rr), rr, tl, H, MAGIC, tmp(name + "1", h, H), lo)
-        v1(name, lambda: V.tensor_tensor(ap(left), ps(tl, lo, lo + H), ap(rr), OP.subtract), H, [rr], [left], [tl])
-        v1(name, lambda: V.tensor_tensor(ap(o), other(), ap(left), OP.max), H, [left] + r, [okey], [] if r else [tl], 2.0 if r else 1.0)
+    def stacked(name, sg, u_, h, into, lo, w):
+        tt, st, first = tile(), tmp(name + "t", h, 256, "ah"), into["keys"][-1]
+        mm(tt, [(H * m, H * m + H, 1, ap(u_, H * m, H * m + H), ap(ib)) for m in range(2)], 256, [ib] + subs(u_, 2))
+        lin(name + "t", ap(st), lambda: ps(tt, 0, 256), 256, got(tt), [st], tt)
+        for b in range(4):
+            tl = tile()
+            mm(tl, [(128 * u, 128 * u + 128, 1, ap(dif, 512 * (b % 2) + 128 * u, 512 * (b % 2) + 128 * u + 128), ap(st, H * (b // 2), H * (b // 2) + H)) for u in range(4)],
+               512, [st] + subs(dif, 4))
+            steps(name, sg, b, tl)
+            mm(into, [(lo + 32 * w * b, lo + 32 * w * (b + 1), 1, ap(sg, 512 * b + 128 * u, 512 * b + 128 * u + 128), ap(red, 64 * u, 64 * u + 64, 3 - w)) for u in range(4)],
+               256, [red, sub(sg, b), first])
 
-    def half(t, h, tab, MEM, REC, thr, xout):
+    def settle(name, tl, w, o, okeys, h, kept_=None):
+        if kept_ is not None:
+            v1(name, lambda: V.tensor_tensor(o, ps(tl, 0, w), ap(kept_), OP.max), w, got(tl) + [kept_], okeys, tl)
+            return
+        rr, left = tmp(name + "r", h, w), tmp(name + "l", h, w)
+        rounded(name + "r", ap(rr), rr, tl, 0, w, MAGIC, left, got(tl))
+        v1(name, lambda: V.tensor_tensor(ap(left), ps(tl, 0, w), ap(rr), OP.subtract), w, [rr], [left], tl)
+        v1(name, lambda: V.tensor_tensor(o, ps(tl, w, 2 * w), ap(left), OP.max), w, [left], okeys, tl)
+
+    def half(t, h, tab, rec, MEM, REC, thr, xout):
         last = t == RO - 1
-        mk, db, xk, x, s_ = mask[t % 2, h], sg[h], "x%d%d" % (t, h), xap(t, h), sv[t, h]
-        if not last:
-            send(h, ap(vb[t + 1, h]), ap(vb[t, h]), [vb[t, h]], [vb[t + 1, h]], 32768)
-        tj = tile(3)
-        mm(tj, [(0, H, 1, ap(bo_16), x, True, True)], 128, [bo_16, xk])
-        jq, jw = tmp("jq", h, H, "ai"), tmp("jw", h, H, "ab")
-        lin("jq", ap(jq), lambda: ps(tj, 0, H), H, [], [jq], [tj], bias=-15.0 / 32)
-        v1("j", lambda: V.tensor_tensor(ap(jw), ps(tj, 0, H), ap(jq), OP.subtract), H, [jq], [jw], [tj])
-        if engine("mask") == "V":
-            for q in range(4):
-                op("V", lambda q=q: [ts(ap(mk, k, 2048, 16), ap(jw), ap(cols, k + t, k + t + 1), None, OP.is_equal) for k in range(4 * q, 4 * q + 4)],
-                   4 * vc(H, 0.5), [jw, cols], [sub(mk, q)], name="mask")
-        else:
+        mk, xk, x, s_, lane = mask[t % 2, h], "x%d%d" % (t, h), xap(t, h), sv[t, h], pm[t, h]
+        old, new = T["old%d" % h], T["new%d" % h]
+        shift0 = float(FEAT0 - strip(t, h) + 2048)
+        tj = tile()
+        mm(tj, [(0, H, 1, ap(bo_16), x)], 128, [bo_16, xk])
+        jq, jw, up = tmp("jq", h, H, "ai"), tmp("jw", h, H, "ab"), tmp("up", h, H, "ab")
+        lin("jq", ap(jq), lambda: ps(tj, 0, H), H, got(tj), [jq], tj, bias=-15.0 / 32)
+        v1("j", lambda: V.tensor_tensor(ap(jw), ps(tj, 0, H), ap(jq), OP.subtract), H, [jq], [jw], tj)
+        if other("mask"):
             ji = al("au", H)
             sact(ji, jw, scale=16.0, bias=ap(colr[t]), r=[colr[t]])
             for q in range(4):
-                pick("mask", mk, 512 * q, 512 * q + 512, ap(diag), ji, 32 * q, 32 * q + 32, [diag], [sub(mk, q)])
+                op("S", lambda q=q: [act("S", ap(mk, 512 * q, 512 * q + 512), ap(diag).indirect(ap(ji, 32 * q, 32 * q + 32)))], 75 + 512 * GA, [diag, ji], [sub(mk, q)], name="mask")
+            ohk = subs(mk, 4)
+        else:
+            for q in range(4):
+                op("V", lambda q=q: [ts(ap(mk, k, 2048, 16), ap(jw), ap(cols, k + t, k + t + 1), None, OP.is_equal) for k in range(4 * q, 4 * q + 4)],
+                   4 * vc(H, 0.5), [jw, cols], [sub(mk, q)], name="mask")
+            ohk = subs(mk, 1)
         oh = ap(mk, 0, 2048, 16)
+        if not other("old"):
+            lin("up", ap(up), oh, H, ohk, [up], scale=-2.0 ** 24, rate=0.5)
         su = al("au", 8)
         lin("su", ap(su), ap(s_), 8, [s_], [su])
-        if t == 0:
-            members("mem1", gm[h], T.lmi[:, :], ["lmi%d" % q for q in range(4)], su, mk, tab, MEM)
+        GM = members("mem1", gm[h], rec, REC, su, mk, tab, MEM)
+        yield GM
+        ty, tp = tile(h), tile()
+        pe, pc_, u2, nu = tmp("pe", h, H, "ah"), tmp("pc", h, H, "ah"), tmp("u2", h, 256, "ah"), al("au", H)
+        mm(tp, [(0, H, 1, oh, ap(par)), (0, H, 1, ap(ib), ap(lane, 0, 256, 2))], 256, [ib, par, sub(lane, 0)] + ohk)
+        v1("pe", lambda: ts(ap(pe), ps(tp, 0, H), -4096.0, None, OP.max), H, got(tp), [pe], tp)
+        if CFG["stack1"]:
+            lin("pc", ap(pc_), ap(lane, 0, 256, 2), H, [sub(lane, 0)], [pc_], rate=0.5)
+            n0, n0k, pold, poldk = ap(lane, 0, 256, 2), sub(lane, 0), ap(pc_), pc_
         else:
-            members("mem1", gm[h], tab[:, 0:2048], REC, su, mk, tab, MEM)
-        ty, tp = tile(0), tile(3)
-        pe, n0, nl, nu = tmp("pe", h, H, "ah"), tmp("n0", h, H, "ah"), tmp("nl", h, H, "ah"), al("au", H)
-        mm(tp, [(0, H, 1, oh, ap(par), True, False), (0, H, 1, ap(ib), ap(pm[t, h], 0, H), False, True)], 256, [ib, par, sub(pm[t, h], 0)] + subs(mk, 4))
-        v1("pe", lambda: ts(ap(pe), ps(tp, 0, H), -4096.0, None, OP.max), H, [], [pe], [tp])
-        mm(ty, [(0, H, 1, ap(i64k), ap(ones, 0, H), True, False)] + [(k, H, 16, ap(gm[h], k, 2048, 16), ap(bo, 0, 128, 16), False, False) for k in range(16)],
-           128 + 1024, [i64k, ones, bo] + subs(gm[h], NC))
-        mm(ty, [(0, H, 1, ap(i16n), ap(pe), False, True)], 128, [i16n, pe])
-        v1("n0", lambda: V.tensor_tensor(ap(n0), ps(ty, 0, H), ap(pe), OP.max), H, [pe], [n0], [ty])
-        tn = tile(3)
-        mm(tn, [(0, H, 1, ap(n0), ap(ib), True, True)], 128, [n0, ib])
-        lin("nu", ap(nu), lambda: ps(tn, 0, H), H, [], [nu], [tn], bias=2048.0)
-        for q in range(NC):
-            pick("feat" + "abcd"[q], fb[h], CW * q, CW * q + CW, T.fw[:, FEAT0:FEAT0 + 4096], nu, CW // 16 * q, CW // 16 * (q + 1), ["feat"], [sub(fb[h], q)])
-        mm(ty, [(H, 2 * H, 1, ap(ib), ap(pe), True, True), (0, H, 1, ap(ib), ap(n0), True, False)], 256, [ib, n0, pe])
-        compare("cmp1", gm[h], ap(pm[t, h], H, 2 * H), sub(pm[t, h], 1), h, lambda b: mm(
-            ty, [(k, H, 16, ap(sg[h], H * k, H * k + H), ap(bow, 0, 128, 16), False, k == 15) for k in range(4 * b, 4 * b + 4)], 256, [bow, sub(sg[h], b)]))
-        settle("set1", ty, 0, nl, nl, lambda: ps(ty, H, 2 * H), [], h)
-        td = tile(0)
-        mm(td, [(H, 2 * H, 1, ap(ib), ap(nl), True, False), (H, 2 * H - 1, 1, ap(ineg), ap(nl, 1, H), False, False),
-                (H + 15, 2 * H - 16, 16, ap(ib), ap(nl, 16, H, 16), False, True),
-                (0, H, 1, ap(i128), ap(n0), True, False), (0, H, 1, ap(i128n), ap(nl), False, False)], 576, [nl, n0, ib, ineg, i128, i128n])
+            n0k = tmp("n0", h, H, "ah")
+            n0, pold, poldk = ap(n0k), ap(lane, 0, 256, 2), sub(lane, 0)
+        nl, nlk = ap(u2, 0, 256, 2), sub(u2, 0)
+        mm(ty, [(0, H, 1, ap(i64k), ap(ones, 0, H)), (0, H, 1, ap(i16n), ap(pe))], 256, [i64k, ones, i16n, pe])
+        nc = CFG["chunks"]["feat"]
+        cw = 2048 // nc
+        mm(ty, [(k, H, 16, ap(gm[h], k, 2048, 16), ap(bo, 0, 128, 16)) for k in range(16)], 1024, [bo] + GM)
+        v1("n0", lambda: V.tensor_tensor(n0, ps(ty, 0, H), ap(pe), OP.max), H, [pe] + got(ty), [n0k], ty)
+        tn = tile()
+        mm(tn, [(0, H, 1, n0, ap(ib))], 128, [n0k, ib])
+        lin("nu", ap(nu), lambda: ps(tn, 0, H), H, got(tn), [nu], tn, bias=2048.0)
+        for q in range(nc):
+            pick("feat" + "abcd"[q], fb[h], cw * q, cw * q + cw, T.fw[:, FEAT0:FEAT0 + 4096], nu, cw // 16 * q, cw // 16 * (q + 1), ["feat"], [sub(fb[h], q)])
+        FB = subs(fb[h], nc)
+        if not last:
+            send(h, ap(vb[t + 1, h]), ap(vb[t, h]), [vb[t, h], nu], [vb[t + 1, h]], 32768)
+        tz, td = tile(), tile(h)
+        mm(tz, [(0, H, 1, ap(ib), n0), (H, 2 * H, 1, ap(ib), ap(pe))][:1 if other("cmp1") else 2], 128 if other("cmp1") else 256, [ib, pe, n0k])
+        if CFG["stack1"]:
+            stacked("cmp1", sg1[h], lane, h, tz, 0, 1)
+        else:
+            compare("cmp1", sg1[h], gm[h], GM, ap(lane, 1, 256, 2), sub(lane, 1), lambda b, col, ck: mm(
+                tz, [(k, H, 16, col(k), ap(bow, 0, 128, 16)) for k in range(4 * b, 4 * b + 4)], 256, [bow, tz["keys"][0]] + ck))
+        settle("set1", tz, H, nl, [nlk], h, pe if other("cmp1") else None)
         by_max = [engine("dist" + "abcd"[b]) == "V" for b in range(4)]
+        if all(by_max):
+            mm(td, [(0, H, 1, ap(i128), n0), (0, H, 1, x, ap(bo16n))], 256, [i128, n0k, xk, bo16n])
+        else:
+            mm(td, [(0, H, 1, ap(i128), n0)], 128, [i128, n0k])
         if any(by_max):
-            txp = tile(3)
-            mm(txp, [(0, H, 1, ap(ib), x, True, True)], 128, [ib, xk, sub(fb[h], 0)])
+            txp = tile()
+            mm(txp, [(0, H, 1, ap(ib), x)], 128, [ib, xk] + FB)
         for b in range(4):
             ks = range(4 * b, 4 * b + 4)
             if by_max[b]:
-                op("V", lambda ks=ks: [V.tensor_tensor(ap(db, H * k, H * k + H), ps(txp, 0, H), ap(fb[h], k, 2048, 16), OP.max) for k in ks],
-                   4 * vc(H), subs(fb[h], NC), [sub(db, b)], [txp], name="dist" + "abcd"[b])
-                mm(td, [(k, H, 16, l, ap(r, 0, 128, 16), False, k == 15 and r is bo32b) for k in ks
-                        for l, r in ((x, bo16n), (ap(fb[h], k, 2048, 16), bo16n), (ap(db, H * k, H * k + H), bo32b))], 768,
-                   [bo32b, bo16n, xk, sub(db, b)] + subs(fb[h], NC))
+                op("V", lambda ks=ks: [V.tensor_tensor(ap(db[h], H * k, H * k + H), ps(txp, 0, H), ap(fb[h], k, 2048, 16), OP.max) for k in ks],
+                   4 * vc(H), FB + got(txp), [sub(db[h], b)], txp, name="dist" + "abcd"[b])
+                if all(by_max):
+                    mm(td, [(k, H, 16, ap(fb[h], k, 2048, 16), ap(bo16n, 0, 128, 16)) for k in ks], 256, [bo16n, td["keys"][0]] + FB)
+                else:
+                    mm(td, [(k, H, 16, l, ap(bo16n, 0, 128, 16)) for k in ks for l in (x, ap(fb[h], k, 2048, 16))], 512, [bo16n, xk, td["keys"][0]] + FB)
+                mm(td, [(k, H, 16, ap(db[h], H * k, H * k + H), ap(bo32b, 0, 128, 16)) for k in ks], 256, [bo32b, sub(db[h], b), td["keys"][0]])
             else:
-                tl = tile(1 + b % 2)
+                tl = tile()
                 calls = []
                 for u in range(4):
-                    calls.append((128 * u, 128 * u + 128, 1, ap(ib), ap(fb[h], 4 * b + u, 2048, 16), True, False))
-                    calls.append((128 * u, 128 * u + 128, 1, ap(ineg), x, False, True))
-                mm(tl, calls, 1024, [ib, ineg, xk] + subs(fb[h], NC))
-                op("S", lambda b=b, tl=tl: [S.activation(ap(db, 512 * b, 512 * b + 512), ps(tl, 0, 512), AF.Abs)], sc(512), [], [sub(db, b)], [tl], name="dist" + "abcd"[b])
-                mm(td, [(k, H, 16, ap(db, H * k, H * k + H), ap(bo16, 0, 128, 16), False, k == 15) for k in ks], 256, [bo16, sub(db, b)])
-        old, new = tmp("old", h, 256), tmp("new", h, 256)
-        sb, tv = tmp("sb", h, H, "ah"), tile(1)
-        pick("sb", sb, 0, H, T.ramp[:, :], su, 0, 8, ["ramp"], [sb])
-        mm(tv, [(0, H, 1, ap(ilow), oh, True, False), (0, H, 1, ap(ib), ap(vb[t, h]), False, False), (0, H, 1, ap(i4k), ap(sb), False, True),
-                (H, 2 * H, 1, ap(ilow), oh, True, False), (H, 2 * H, 1, ap(ib), ap(vb[t, h]), False, True)][:3 if last else 5],
-           384 if last else 640, [ilow, ib, i4k, sb, vb[t, h]] + subs(mk, 4))
-        flex("vo", lambda e, _: [act(e, ap(new, m, 256, 2), ps(tv, H * m, H * m + H), AF.Identity, 2048.0 * (1 - m) - LOW) for m in range(2 - last)],
-             (2 - last) * sc(H), (2 - last) * vc(H), [], subs(new, 2), [tv])
+                    calls.append((128 * u, 128 * u + 128, 1, ap(ib), ap(fb[h], 4 * b + u, 2048, 16)))
+                    calls.append((128 * u, 128 * u + 128, 1, ap(ineg), x))
+                mm(tl, calls, 1024, [ib, ineg, xk] + FB)
+                op("S", lambda b=b, tl=tl: [S.activation(ap(db[h], 512 * b, 512 * b + 512), ps(tl, 0, 512), AF.Abs)], sc(512), got(tl), [sub(db[h], b)], tl, name="dist" + "abcd"[b])
+                mm(td, [(k, H, 16, ap(db[h], H * k, H * k + H), ap(bo16, 0, 128, 16)) for k in ks], 256, [bo16, sub(db[h], b), td["keys"][0]])
+        mm(td, [(0, H, 1, ap(i128n), nl), (H, 2 * H, 1, ap(ib), nl), (H, 2 * H - 1, 1, ap(ineg), ap(u2, 2, 256, 2)), (H + 15, 2 * H - 16, 16, ap(ib), ap(u2, 32, 256, 32))], 448,
+           [nlk, ib, ineg, i128n])
+        tv = tile()
+        if other("newr"):
+            sb = tmp("sb", h, H, "ah")
+            op("S", lambda: [act("S", ap(sb), T.ramp[:, :].indirect(ap(su)), AF.Identity, -0.5, 1.0 / 4096)], 75 + H * GA, RAMP + [su], [sb], name="newr")
+            mm(tv, [(H, 2 * H, 1, ap(ilow), oh), (H, 2 * H, 1, ap(ib), ap(vb[t, h])), (H, 2 * H, 1, ap(i4k), ap(sb))], 384, [ilow, ib, vb[t, h], i4k, sb] + ohk)
+        if not (last and other("newr")):
+            mm(tv, [(0, H, 1, ap(ilow), oh), (0, H, 1, ap(ib), ap(vb[t, h]))], 256, [ilow, ib, vb[t, h]] + ohk)
+            lin("newm", new[:, :, 16:32], lambda: ps(tv, 0, H), H, got(tv), ["newm%d" % h], tv, bias=-LOW)
+        if other("newr"):
+            op("S", lambda: [act("S", new[:, :, 0:16], ps(tv, H, 2 * H), AF.Identity, 2048.0 - LOW)], sc(H), got(tv), ["newr%d" % h], tv, name="newr")
+        else:
+            gat("newr", lambda: V.tensor_tensor(new[:, :, 0:16], T.ramp[:, :].indirect(ap(su)), new[:, :, 16:32], OP.add), H, RAMP + [su, "newm%d" % h], ["newr%d" % h])
         kk, nt, sp2, ls = tmp("kk", h, H), tmp("nt", h, H), tmp("sp2", h, 256, "ah"), tmp("ls", h, H)
-        v1("arg", lambda: V.tensor_tensor_scan(ap(kk), ap(d0), ps(td, 0, H), 0.0, OP.add, OP.min), H, [d0], [kk], [td])
-        v1("arg", lambda: V.tensor_tensor(ap(nt), ps(td, 0, H), ap(kk), OP.not_equal), H, [kk], [nt], [td])
-        v1("arg", lambda: V.tensor_tensor_scan(ap(sp2, 0, H), ap(nt), ps(td, H, 2 * H), 0.0, OP.mult, OP.add), H, [nt], [sub(sp2, 0)], [td])
+        lin("xc", ap(rst[h], 0, H, 16), ap(lane8), 8, [lane8, rst[h]], [sub(rst[h], 0)], bias=-shift0)
+        v1("arg", lambda: V.tensor_tensor_scan(ap(kk), ap(d0), ps(td, 0, H), 0.0, OP.add, OP.min), H, [d0] + got(td), [kk], td)
+        v1("arg", lambda: V.tensor_tensor(ap(nt), ps(td, 0, H), ap(kk), OP.not_equal), H, [kk], [nt], td)
         v1("arg", lambda: V.tensor_tensor(ap(sp2, H + 15, 2 * H, 16), ap(kk, 15, H, 16), ap(thr, 8 * h, 8 * h + 8), OP.is_lt), 8, [kk, thr], [sub(sp2, 1)])
-        to = tile(3)
-        mm(to, [(0, H, 1, ap(ib), ap(offm), True, False)] + [(16 * c, 16 * c + 16, 1, ap(shift, c, 1024, 8), ap(sp2, 15, 256, 16), False, c == 7) for c in range(8)],
-           128 + 512, [ib, offm, shift] + subs(sp2, 2))
-        v1("arg", lambda: V.tensor_tensor_scan(ap(ls), ap(rst8), ps(to, 0, H), 0.0, OP.add, OP.max), H, [rst8], [ls], [to])
-        win, near = ap(ls, 7, H, 16), ap(ls, 15, H, 16)
-        o1, of, osn = al("af", 8), al("au", 8), al("au", 8)
-        lin("osn", ap(osn), win, 8, [ls], [osn], func=AF.Relu, bias=2048.0)
-        v1("of", lambda: V.tensor_tensor(ap(o1), win, ap(xc[t, h]), OP.max), 8, [ls, xc[t, h]], [o1])
-        lin("ofu", ap(of), ap(o1), 8, [o1], [of], bias=float(FEAT0 - strip(t, h) + 2048))
+        v1("arg", lambda: V.tensor_tensor_scan(ap(sp2, 0, H), ap(nt), ps(td, H, 2 * H), 0.0, OP.mult, OP.add), H, [nt], [sub(sp2, 0)], td)
+        to = tile()
+        mm(to, [(0, H, 1, ap(ib), ap(offm))] + [(16 * c, 16 * c + 16, 1, ap(shift, c, 1024, 8), ap(sp2, 15, 256, 16)) for c in range(8)],
+           128 + 512, [ib, offm] + subs(shift, 4) + subs(sp2, 2))
+        v1("ls", lambda: V.tensor_tensor_scan(ap(ls), ap(rst[h]), ps(to, 0, H), 0.0, OP.min, OP.max), H, [rst[h], sub(rst[h], 0)] + got(to), [ls], to)
+        near = ap(ls, 15, H, 16)
+        of = al("au", 8)
+        lin("of", ap(of), ap(ls, 7, H, 16), 8, [ls], [of], bias=shift0)
         fs = tmp("fs", h, H, "ab")
         pick("fs", fs, 0, H, T.fw[:, strip(t, h):FEAT0 + 4096], of, 0, 8,
-             ["void", "feat"] + ["x%d%d" % (u, v) for u in range(t + 1) for v in range(NH) if 2 * u + v <= 2 * t + h], [fs])
-        tx = tile(2)
-        mm(tx, [(0, H, 1, ap(ihalf), x, True, False), (0, H, 1, ap(iquar), ap(ones, 0, H), False, False), (0, H, 1, ap(ihalf), ap(fs), False, True)], 384,
-           [ihalf, iquar, ones, xk, fs])
+             ["feat"] + ["x%d%d" % (u, v) for u in range(t + 1) for v in range(NH) if 2 * u + v <= 2 * t + h], [fs])
+        tx = tile()
+        mm(tx, [(0, H, 1, ap(ihalf), x), (0, H, 1, ap(iquar), ap(ones, 0, H)), (0, H, 1, ap(ihalf), ap(fs))], 384, [ihalf, iquar, ones, xk, fs])
         if last:
-            rounded("x2", ap(xout, H * h, H * h + H), sub(xout, h), tx, H, MAGIC1, tmp("x1", h, H))
+            rounded("x2", ap(xout, H * h, H * h + H), sub(xout, h), tx, 0, H, MAGIC1, tmp("x1", h, H), got(tx))
         else:
             x2 = al("ab", H)
-            rounded("x2", ap(x2), x2, tx, H, MAGIC1, tmp("x1", h, H))
+            rounded("x2", ap(x2), x2, tx, 0, H, MAGIC1, tmp("x1", h, H), got(tx))
             send(h, xap(t + 1, h), ap(x2), [x2], ["x%d%d" % (t + 1, h)], 32768)
-        z, zs, sr = tmp("z", h, H, "ah"), tmp("zs", h, H, "ah"), tmp("sr", h, H, "ah")
-        sp = ap(zs, 15, H, 16)
-        su2, d, e, so, ngo, ko = al("au", 8), al("af", 8), al("af", 8), al("af", 8), al("ab", 8), al("af", 8)
-        pick("sr", sr, 0, H, T.snr[:, :], osn, 0, 8, SNR, [sr])
-        if engine("sn") == "V":
-            gat("sn", lambda: V.tensor_tensor(ap(z), T.snr[:, :].indirect(ap(osn)), ap(diag, 0, H), OP.mult), H, SNR + [osn, diag], [z])
-            v1("sn", lambda: V.tensor_tensor_scan(ap(zs), ap(keep), ap(z), 0.0, OP.mult, OP.add), H, [keep, z], [zs], rate=0.5)
-            lin("su2", ap(su2), sp, 8, [zs], [su2])
-        else:
-            tq = tile(3)
-            mm(tq, [(0, 8, 1, ap(wall, 15 - p, 143 - p), ap(sr, p, H, 16), p == 0, p == 15) for p in range(16)], 1024, [wall, sr])
-            lin("su2", ap(su2), lambda: ps(tq, 0, 8), 8, [], [su2], [tq], scale=1.0 / 16)
-            lin("sp", sp, lambda: ps(tq, 0, 8), 8, [], [zs], [tq], scale=1.0 / 16)
-        members("mem2", gn[h], tab[:, 0:2048], REC, su2, mk, tab, MEM)
+        zs, sr = tmp("zs", h, H, "ah"), tmp("sr", h, H, "ah")
+        sp, go = ap(zs, 15, H, 16), ap(g2, 32 * t + 16 * h, 32 * t + 16 * h + 8)
+        su2, d, e, so, ko, gk = al("au", 8), al("af", 8), al("af", 8), al("af", 8), al("af", 8), sub(g2, NH * t + h)
+        gat("sn", lambda: V.tensor_tensor(ap(sr), T.snr[:, strip(t, h):FEAT0 + 4096].indirect(ap(of)), ap(pen), OP.add), H, ["snr", "snpad", of, pen], [sr])
+        v1("sn", lambda: V.tensor_tensor_scan(ap(zs), ap(rst16), ap(sr), 0.0, OP.add, OP.max), H, [rst16, sr], [zs], rate=0.5)
+        lin("su2", ap(su2), sp, 8, [zs], [su2])
         v1("mv", lambda: V.tensor_tensor(ap(d), sp, ap(s_), OP.subtract), 8, [zs, s_], [d])
         v1("mv", lambda: V.tensor_tensor(ap(e), ap(d), near, OP.mult), 8, [d, ls], [e])
+        v1("mv", lambda: ts(go, ap(e), 0.0, 2048.0, OP.not_equal, OP.mult), 8, [e], [gk])
+        v1("mv", lambda: V.tensor_tensor(ap(ko), sp, go, OP.subtract), 8, [zs, gk], [ko])
         v1("mv", lambda: V.tensor_tensor(ap(so), ap(e), ap(s_), OP.add), 8, [e, s_], [so])
-        v1("mv", lambda: ts(ap(ngo), ap(e), 0.0, 4096.0, OP.is_equal, OP.mult), 8, [e], [ngo])
-        v1("mv", lambda: V.tensor_tensor(ap(ko), sp, ap(ngo), OP.subtract), 8, [zs, ngo], [ko])
         eqb = tmp("eqb", h, H, "ab")
         gat("eqb", lambda: V.tensor_tensor(ap(eqb), ap(ko).indirect(ap(l_col)), ap(sr), OP.is_equal), H, [ko, sr, l_col], [eqb])
-        tw = tile(3)
-        calls = []
-        for m in range(2):
-            calls += [(m, 16, 2, ap(perm[m]), sp, True, False), (m, 16, 2, ap(perm[m]), ap(ngo), False, False)]
-            calls += [(m, 16, 2, ap(trip, p, 2048, 16), ap(eqb, p, H, 16), False, p % 8 == 7) for p in range(max(1, 8 * m), 8 * m + 8)]
-        mm(tw, calls, 64 * 19, perm + [zs, ngo, eqb] + subs(trip, 8))
+        tw = tile()
+        mm(tw, [(0, 8, 1, ap(ib), sp)] + [(0, 8, 1, ap(wall, 15 - p, 143 - p), ap(eqb, p, H, 16)) for p in range(16)], 64 * 17, [ib, wall, zs, eqb])
         wl = al("au", 16)
-        if last:
-            op("V", lambda: [ts(ap(wl, m, 16, 2), ps(tw, m, 16, 2), ap(dum2[m]), ap(least[m]), OP.min, OP.max) for m in range(2)], 2 * vc(8), dum2 + least, [wl], [tw], name="wl")
-        else:
-            op("V", lambda: [ts(ap(wl, m, 16, 2), ps(tw, m, 16, 2), ap(dum[m]), ap(memo), OP.min, OP.add) for m in range(2)], 2 * vc(8), dum + [memo], [wl], [tw], name="wl")
         nm = 1 if last else 2
-        if engine("old") == "V":
-            up = tmp("up", h, H, "ab")
-            flex("up", lambda e, _: [act(e, ap(up), oh, AF.Identity, 2.0 ** 24, -2.0 ** 25)], sc(H), vc(H, 0.5), subs(mk, 4), [up])
-            for m, rw in enumerate((REC, MEM)[:nm]):
-                gat("old", lambda m=m: V.tensor_tensor(ap(old, m, 256, 2), tab[:, MEM0 * m:MEM0 * m + 2048].indirect(ap(su2)), ap(up), OP.min), H,
-                    rw + [su2, up], [sub(old, m)])
-        else:
-            orc, omc, tu = tmp("orc", h, H), tmp("omc", h, H, "ah"), tile(1)
-            pick("old", orc, 0, H, tab[:, 0:2048], su2, 0, 8, REC, [orc])
-            if not last:
-                pick("old", omc, 0, H, tab[:, MEM0:MEM0 + 2048], su2, 0, 8, MEM, [omc])
-            mm(tu, [(0, 256, 2, ap(i32), ap(orc), True, False), (0, 256, 2, ap(ihigh), oh, False, True),
-                    (1, 256, 2, ap(ib), ap(omc), True, False), (1, 256, 2, ap(ihigh), oh, False, True)][:2 * nm], 384 + 256 * nm, [i32, ib, ihigh, orc, omc] + subs(mk, 4))
-            lin("old", ap(old, 0, 256, 3 - nm), lambda: ps(tu, 0, 256, 3 - nm), H * nm, [], subs(old, 2), [tu])
-        cz = None
+        op("V", lambda: [ts(ap(wl, m, 16, 2), ps(tw, 0, 8), ap(dum), float(MEM0 * m), OP.min, OP.add) for m in range(nm)], nm * vc(8), [dum] + got(tw), [wl], tw, name="wl")
+        for m, (win, rw) in enumerate(((rec, REC), (tab[:, MEM0:MEM0 + 2048], MEM))[:nm]):
+            if other("old"):
+                raw, tu = tmp("raw%d" % m, h, H, "ah" if m else "af"), tile()
+                op("S", lambda win=win, raw=raw: [act("S", ap(raw), win.indirect(ap(su2)))], 75 + H * GA, rw + [su2], [raw], name="old")
+                mm(tu, [(0, H, 1, ap(ib if m else i32), ap(raw)), (0, H, 1, ap(ihigh), oh)], 256 if m else 640, [ib, i32, ihigh, raw] + ohk)
+                op("S", lambda m=m, tu=tu: [act("S", old[:, :, 16 * m:16 * m + 16], ps(tu, 0, H))], sc(H), got(tu), ["old%d%d" % (h, m)], tu, name="old")
+            else:
+                gat("old", lambda m=m, win=win: V.tensor_tensor(old[:, :, 16 * m:16 * m + 16], win.indirect(ap(su2)), ap(up), OP.add), H, rw + [su2, up], ["old%d%d" % (h, m)])
         if not last:
             send(h, ap(sv[t + 1, h]), ap(so), [so], [sv[t + 1, h]], 4096)
-            cnt, junk, cz = al("af", 1), al("af", 8), al("ab", 16)
-            op("S", lambda: [S.activation(ap(junk), ap(ngo), AF.Identity, accum_out=ap(cnt))], sc(8) + 20, [ngo], [junk, cnt])
-            sact(cz, bo8, scale=ap(cnt), r=[cnt])
         else:
-            tys, ysb = tile(3), al("af", H)
-            mm(tys, [(p, H, 16, ap(i32, p, 128, 16), ap(so, 0, 8), True, True, 8) for p in range(16)], 16 * 4 * 8, [i32, so])
-            flex("ys", lambda e, _: [act(e, ap(ysb, p1=8), ps(tys, 0, H, 1, 8))], sc(H), vc(H), [], [ysb], [tys])
+            tys, ysb = tile(), al("af", H)
+            mm(tys, [(p, H, 16, ap(i32, p, 128, 16), ap(so, 0, 8), 8) for p in range(16)], 16 * 4 * 8, [i32, so])
+            lin("ys", ap(ysb, p1=8), lambda: ps(tys, 0, H, 1, 8), H, got(tys), [ysb], tys)
             dma("Y", [(T.ys[:, H * h:H * h + H], ap(ysb, p1=8))], 4096, r=[ysb])
+        behind = yield wl
+        GN = members("mem2", gn[h], rec, REC, su2, mk, tab, MEM, behind)
         zg = tmp("zg", h, H, "ab")
-        gat("zg", lambda: V.tensor_tensor(ap(zg), ap(ngo).indirect(ap(l_col)), ap(diag, 0, H), OP.mult), H, [ngo, l_col, diag], [zg])
-        tr = tile(0)
-        mm(tr, [(256, 512, 1, ap(ib), ap(pm[t, h]), True, False), (256, 512, 1, ap(i8n), ap(ones), False, False),
-                (256, 384, 1, ap(zg), ap(bo2p), False, False), (384, 512, 1, ap(zg), ap(bo2p), False, True)], 768,
-           [ib, i8n, ones, zg, bo2p] + subs(pm[t, h], 2))
-        mm(tr, [(0, 256, 1, ap(zg), ap(bo2n), True, False), (0, H, 1, ap(ib), ap(nl), False, False)]
-           + [(H + k, 2 * H, 16, ap(gn[h], k, 2048, 16), ap(bo, 0, 128, 16), False, False) for k in range(16)],
-           384 + 1024, [zg, bo2n, ib, nl, bo] + subs(gn[h], NC))
-
-        def after(b):
-            calls = []
-            for k in range(4 * b, 4 * b + 4):
-                calls.append((H + k, 2 * H, 16, ap(sg[h], H * k, H * k + H), ap(bow, 0, 128, 16), False, False))
-                calls.append((0, H, 1, ap(sg[h], H * k, H * k + H), ap(iw), False, k == 15))
-            mm(tr, calls, 768, [bow, iw, sub(sg[h], b)])
-        compare("cmp2", gn[h], ap(nl), nl, h, after)
+        gat("zg", lambda: V.tensor_tensor(ap(zg), go.indirect(ap(l_col)), ap(diag), OP.mult), H, [gk, l_col, diag], [zg])
+        tr = tile()
+        keepers = [(256, 512, 2, ap(ib), pold), (257, 512, 2, ap(ib), ap(lane, 1, 256, 2)), (256, 512, 1, ap(zg), ap(bo4n))]
         po = al("ah", 256)
-        for m in range(2):
-            settle("set" + "pm"[m], tr, H * m, part(po, H * m, H), sub(po, m), lambda m=m: ps(tr, 256 + H * m, 256 + H * m + H), [], h)
-            if not last:
-                send(h, ap(pm[t + 1, h], H * m, H * m + H), ap(po, H * m, H * m + H), [sub(po, m)], [sub(pm[t + 1, h], m)], 32768)
-        if last:
-            tf, yo = tile(3), al("af", 256)
-            mm(tf, [(H * m, H * m + H, 1, ap(po, H * m, H * m + H), ap(ib), True, True) for m in range(2)], 256, subs(po, 2) + [ib])
-            v1("yo", lambda: ts(ap(yo), ps(tf, 0, 256), 2048.0, -1.0, OP.add, OP.max), 256, [], [yo], [tf])
+        tk, oth = (tile(), tmp("oth", h, 256, "ah")) if other("cmp2") else (tr, None)
+        mm(tk, keepers, 512, [ib, poldk, sub(lane, 1), zg, bo4n])
+        if oth:
+            lin("oth", ap(oth), lambda: ps(tk, 256, 512), 256, got(tk), [oth], tk)
+        if CFG["stack2"]:
+            tm = tile()
+            mm(tm, [(k, H, 16, ap(gn[h], k, 2048, 16), ap(bo, 0, 128, 16)) for k in range(16)], 1024, [bo] + GN)
+            lin("m2", ap(u2, 1, 256, 2), lambda: ps(tm, 0, H), H, got(tm), [sub(u2, 1)], tm)
+            mm(tr, [(0, 256, 1, ap(i8n), ap(ones)), (0, 256, 1, ap(zg), ap(bo4p)), (0, 256, 1, ap(ib), ap(u2))], 768, [i8n, ones, zg, bo4p, ib] + subs(u2, 2))
+            stacked("cmp2", sg2[h], u2, h, tr, 0, 2)
+        else:
+            mm(tr, [(0, 256, 1, ap(i8n), ap(ones)), (0, 256, 1, ap(zg), ap(bo4p)), (0, 256, 2, ap(ib), nl)], 640, [i8n, ones, zg, bo4p, ib, nlk])
+            first = tr["keys"][-1]
+            mm(tr, [(2 * k + 1, 256, 32, ap(gn[h], k, 2048, 16), ap(bo, 0, 128, 16)) for k in range(16)], 1024, [bo, first] + GN)
+
+            def after(b, col, ck):
+                calls = []
+                for k in range(4 * b, 4 * b + 4):
+                    calls.append((2 * k + 1, 256, 32, col(k), ap(bow, 0, 128, 16)))
+                    calls.append((0, 256, 2, col(k), ap(iw)))
+                mm(tr, calls, 768, [bow, iw, first] + ck)
+            compare("cmp2", sg2[h], gn[h], GN, nl, nlk, after)
+        settle("set2", tr, 256, ap(po), [po], h, oth)
+        if not last:
+            send(h, ap(pm[t + 1, h]), ap(po), [po], subs(pm[t + 1, h], 2), 65536)
+        else:
+            tf, yo = tile(), al("af", 256)
+            mm(tf, [(H * m, H * m + H, 1, ap(po, m, 256, 2), ap(ib)) for m in range(2)], 256, [po, ib])
+            v1("yo", lambda: ts(ap(yo), ps(tf, 0, 256), 2048.0, -1.0, OP.add, OP.max), 256, got(tf), [yo], tf)
             dma("Y", [(T.yp[:, H * h:H * h + H], ap(yo, 0, H)), (T.yq[:, H * h:H * h + H], ap(yo, H, 2 * H))], 131072, r=[yo])
-        return wl, old, new, cz
+        yield None
 
     thr = thl
     xout = al("af", 256)
     for t in range(RO):
         last = t == RO - 1
-        upd = {}
-        u, w = (t % 2, 1 - t % 2) if CFG["double"] else (0, 0)
+        wls = {}
+        u, w = t % 2, 1 - t % 2
         tab, nxt = T[("tab", "tab1")[u]], T[("tab", "tab1")[w]]
         MEM, REC = ["mem%d" % (q + 4 * u) for q in range(4)], ["rec%d" % (q + 4 * u) for q in range(4)]
         MEMN, RECN = ["mem%d" % (q + 4 * w) for q in range(4)], ["rec%d" % (q + 4 * w) for q in range(4)]
-        if u != w:
-            dma("Y", [(nxt[:, 0:MEM0], tab[:, 0:MEM0])], 1064960, r=REC + ["pad%d" % u], w=RECN + ["pad%d" % w])
-            if not last:
-                dma("Y", [(nxt[:, MEM0:2 * MEM0], tab[:, MEM0:2 * MEM0])], 1064960, r=MEM + ["padm%d" % u], w=MEMN + ["padm%d" % w])
-        for h in range(NH):
-            cur[0] = (t, h)
-            upd[h] = half(t, h, tab, MEM, REC, thr, xout)
+        rec, RECR = (T.lmi[:, :], ["lmi%d" % q for q in range(4)]) if t == 0 else (tab[:, 0:2048], REC)
+        cur[0] = (t, 1)
+        upper = half(t, 1, tab, rec, MEM, RECR, thr, xout)
+        first = next(upper)
+        if t > 0:
+            cur[0] = (t - 1, 0)
+            lower.send(first)
+        cur[0] = (t, 0)
+        lists = [sub(pm[t, h], 1) for h in range(NH)]
+        if t > 0:
+            dma("Y", [(nxt[:, 0:MEM0], tab[:, 0:MEM0])], 1064960, r=REC + ["pad%d" % u] + lists[CFG["early"]:], w=RECN + ["pad%d" % w], name="copy")
+        if not last:
+            dma("Y", [(nxt[:, MEM0:2 * MEM0], tab[:, MEM0:2 * MEM0])], 1064960, r=MEM + ["padm%d" % u] + lists, w=MEMN + ["padm%d" % w], name="copy")
+        cur[0] = (t, 1)
+        wls[1] = next(upper)
+        upper.send([])
+        cur[0] = (t, 0)
+        lower = half(t, 0, tab, rec, MEM, RECR, thr, xout)
+        next(lower)
+        wls[0] = next(lower)
+        if last:
+            lower.send([])
         win = nxt[:, 0:MEM0] if last else nxt[:, :]
         for h in (1, 0):
-            wl, old, new, _ = upd[h]
             cur[0] = (t, h)
+            old, new = T["old%d" % h], T["new%d" % h]
             for c in range(7, -1, -1):
-                op("V", lambda wl=wl, old=old, new=new, c=c, win=win: [
-                    V.tensor_tensor(win.indirect(ap(wl, 2 * c, 2 * c + 2)), ap(old, 32 * c, 32 * c + 32), ap(new, 32 * c, 32 * c + 32), OP.max)],
-                   50 + 32 * SC, [wl] + subs(old, 2) + subs(new, 2), RECN + ["pad%d" % w] + ([] if last else MEMN + ["padm%d" % w]), name="scat")
+                if last:
+                    op("V", lambda wl=wls[h], old=old, new=new, c=c, win=win: [V.tensor_tensor(win.indirect(ap(wl, 2 * c, 2 * c + 1)), old[:, c, 0:16], new[:, c, 0:16], OP.max)],
+                       50 + 16 * SC, [wls[h], "old%d0" % h, "newr%d" % h], RECN + ["pad%d" % w], name="scat")
+                else:
+                    op("V", lambda wl=wls[h], old=old, new=new, c=c, win=win: [V.tensor_tensor(win.indirect(ap(wl, 2 * c, 2 * c + 2)), old[:, c, :], new[:, c, :], OP.max)],
+                       50 + 32 * SC, [wls[h], "old%d0" % h, "old%d1" % h, "newr%d" % h, "newm%d" % h], RECN + MEMN + ["pad%d" % w, "padm%d" % w], name="scat")
         if not last:
-            ta = tile(3)
-            mm(ta, [(0, 16, 1, ap(ones, 0, 128), ap(upd[h][3]), h == 0, h == 1) for h in range(NH)], 128, [ones, upd[0][3], upd[1][3]])
-            a1, a2, nthr = al("ai", 16), al("ai", 16), al("af", 16)
-            lin("cnt", ap(a1), lambda ta=ta: ps(ta, 0, 16), 16, [], [a1], [ta], bias=4096.0, scale=-1.0 / 256)
+            cnt, junk, cz, a1, a2, nthr, ta = al("af", 1), al("af", 32), al("ab", 16), al("ai", 16), al("ai", 16), al("af", 16), tile()
+            op("S", lambda t=t, junk=junk, cnt=cnt: [S.activation(ap(junk), ap(g2, 32 * t, 32 * t + 32), AF.Identity, accum_out=ap(cnt))], sc(32) + 20,
+               [sub(g2, NH * t + h) for h in range(NH)], [junk, cnt])
+            sact(cz, bo8, scale=ap(cnt), r=[cnt])
+            mm(ta, [(0, 16, 1, ap(ones, 0, 128), ap(cz))], 64, [ones, cz])
+            lin("cnt", ap(a1), lambda ta=ta: ps(ta, 0, 16), 16, got(ta), [a1], ta, scale=1.0 / 128)
             vts(a2, a1, 496, None, OP.bitwise_and)
             v1("thr", lambda a2=a2, nthr=nthr: V.tensor_tensor(ap(nthr), ap(a2), ap(thl), OP.add), 16, [a2, thl], [nthr])
             thr = nthr
     dma("Y", [(T.yx[:, :], ap(xout))], 131072, r=subs(xout, 2))
     dma("Y", [(T.ylm[:, :], nxt[:, 0:2048])], 1048576, r=RECN)
+    CFG["used"] = used
     return ops
 
 
@@ -589,46 +693,247 @@ def lay(ops):
         for j in o["d"]:
             succ[j].append(i)
 
-    def hop(i, j):
-        a, b = ops[i], ops[j]
-        return 0.0 if a["e"] == b["e"] == "P" else a["lat"] + CFG["same" if a["e"] == b["e"] else "psum" if a["e"] == "P" else "other"]
-    key = [-99.0 if o["k"] == "d" and not o["r"] else o["tv"][0] + CFG["pos"].get((o["name"], o["tv"][1]), 99.0) for o in ops]
+    def hop(i, e):
+        a = ops[i]
+        return 0.0 if a["e"] == e == "P" else 0.0 if a["k"] != "c" else CFG["same" if a["e"] == e else "psum" if a["e"] == "P" else "other"]
+    way = [0.0] * n
     for i in reversed(range(n)):
-        key[i] = min([key[i]] + [key[j] for j in succ[i]])
-
-    def sweep(order, back):
-        rdy = [o["lat"] if back else 0.0 for o in ops]
-        end = [0.0] * n
-        busy = {e: [] for e in "VSPGY"}
-        for i in order:
-            o = ops[i]
-            b, st = busy[o["e"]], rdy[i]
-            k = len(b)
-            while k > 0 and b[k - 1][1] > st:
-                k -= 1
-            while k < len(b) and b[k][0] < st + o["c"]:
-                st = max(st, b[k][1])
-                k += 1
-            end[i] = st + o["c"]
-            b.insert(k, (st, end[i]))
-            for j in o["d"] if back else succ[i]:
-                rdy[j] = max(rdy[j], end[i] + (hop(j, i) if back else hop(i, j)))
-        return end
-    end = sweep(sorted(range(n), key=lambda i: (key[i], i)), False)
-    tries = [end]
-    for _ in range(CFG["turns"]):
-        late = sweep(sorted(range(n), key=lambda i: (-end[i], -i)), True)
-        end = sweep(sorted(range(n), key=lambda i: (-1e9 if key[i] < -90 else -late[i], i)), False)
-        tries.append(end)
-    end = min(tries, key=lambda x: max(x[i] + ops[i]["lat"] for i in range(n)))
+        o = ops[i]
+        due = CFG["pos"].get((o["name"], o["tv"][1]))
+        way[i] = 1e9 - i if o["name"] == "load" else max([-1e6 if due is None else -due - CFG["period"] * o["tv"][0]] + [way[j] + 1e-3 * o["c"] for j in succ[i]])
+    left = [len(o["d"]) for o in ops]
+    rdy = [0.0] * n
+    end = [0.0] * n
+    free = {e: 0.0 for e in "VSPGY"}
+    cand = {e: [] for e in "VSPGY"}
     for i, o in enumerate(ops):
-        o["st"] = end[i] - o["c"]
-    return sorted(range(n), key=lambda i: (ops[i]["st"], i))
+        if not left[i]:
+            cand[o["e"]].append(i)
+    touch = [{} for _ in range(8)]
+    holder = [None] * 8
+    dmas = [0.0]
+    seq = []
+
+    def start(i):
+        o = ops[i]
+        st, t = max(rdy[i], free[o["e"]]), o["t"]
+        if t is None:
+            return st, None
+        banks = [t["b"]] if t["b"] is not None else [b for b in ([t["own"]] if t["own"] is not None else range(NH, 8)) if holder[b] is None]
+        if not banks:
+            return None, None
+        return min((max([st] + [end[j] + hop(j, o["e"]) for e, j in touch[b].items() if e != o["e"]]), b) for b in banks)
+    while len(seq) < n:
+        best = None
+        table = {}
+        for e in cand:
+            table[e] = [(i,) + start(i) for i in cand[e]]
+            table[e] = [x for x in table[e] if x[1] is not None]
+            for i, st, b in table[e]:
+                if best is None or st + CFG["slack"] * ops[i]["c"] < best[0]:
+                    best = (st + CFG["slack"] * ops[i]["c"], e)
+        i, st, b = max((x for x in table[best[1]] if x[1] <= best[0]), key=lambda x: (way[x[0]], -x[0]))
+        o = ops[i]
+        t = o["t"]
+        if t is not None:
+            o["d"] = o["d"] | set(j for e, j in touch[b].items() if e != o["e"])
+            t["b"] = b
+            touch[b][o["e"]] = i
+            t["n"] -= 1
+            holder[b] = t if t["n"] else None
+        o["st"] = st
+        free[o["e"]] = end[i] = st + o["c"]
+        if o["k"] != "c":
+            dmas[0] = max(dmas[0], end[i] + 900) + o["lat"]
+            end[i] = dmas[0] + 800
+        cand[o["e"]].remove(i)
+        seq.append(i)
+        for j in succ[i]:
+            rdy[j] = max(rdy[j], end[i] + hop(i, ops[j]["e"]))
+            left[j] -= 1
+            if not left[j]:
+                cand[ops[j]["e"]].append(j)
+    CFG["span"] = max(end)
+    return seq
+
+
+def polish(ops, waits, seq, rounds):
+    n = len(ops)
+    above, dep = [], []
+    for d in waits:
+        far = 0
+        for j in d:
+            far |= above[j]
+        dep.append(sorted(j for j in d if not far >> j & 1))
+        above.append(far | sum(1 << j for j in d if not far >> j & 1))
+    succ = [[] for _ in ops]
+    for i, d in enumerate(dep):
+        for j in d:
+            succ[j].append(i)
+    eng = ["VSPGY".index(o["e"]) for o in ops]
+    cost = [o["c"] for o in ops]
+    alt = [{"VSPGY".index(e): c for e, c in o["alt"]} if o["flex"] else None for o in ops]
+    kind = ["cdr".index(o["k"]) for o in ops]
+    extra = [o["lat"] for o in ops]
+    ids = {}
+    tile = [-1 if o["t"] is None else ids.setdefault(o["t"]["id"], len(ids)) for o in ops]
+    uses, own = [0] * len(ids), [None] * len(ids)
+    seen, sign, twin = {}, [], {}
+    for i, o in enumerate(ops):
+        if tile[i] >= 0:
+            uses[tile[i]] += 1
+            own[tile[i]] = o["t"]["own"]
+        k = (o["name"], "" if o["flex"] else o["e"], o["tv"])
+        seen[k] = seen.get(k, 0) + 1
+        sign.append((k[0], k[1], o["tv"][1], seen[k]))
+        twin[sign[i], o["tv"][0]] = i
+    visit = [o["tv"][0] for o in ops]
+    hop = [[CFG["same"] if a == b else CFG["other"] for b in range(5)] for a in range(5)]
+    hop[2] = [CFG["psum"], CFG["psum"], 0.0, CFG["psum"], CFG["psum"]]
+
+    def play(order):
+        end, pred, free, last, dmas, dlast = [0.0] * n, [-1] * n, [0.0] * 5, [-1] * 5, 0.0, -1
+        bank, left, held, touch = [-1] * len(uses), list(uses), [False] * 8, [[-1, -1, -1] for _ in range(8)]
+        for i in order:
+            e = eng[i]
+            st, p = free[e], last[e]
+            for j in dep[i]:
+                x = end[j] if kind[j] else end[j] + hop[eng[j]][e]
+                if x > st:
+                    st, p = x, j
+            t = tile[i]
+            if t >= 0:
+                b = bank[t]
+                if b < 0:
+                    soon = 1e18
+                    for c in (range(NH, 8) if own[t] is None else (own[t],)):
+                        if not held[c]:
+                            u, v = touch[c][:2]
+                            x = max(end[u] if u >= 0 else 0.0, end[v] if v >= 0 else 0.0)
+                            if x < soon:
+                                soon, b = x, c
+                    if b < 0:
+                        return 1e12, None, None, None, None
+                    bank[t] = b
+                tc = touch[b]
+                for f in (0, 1, 2):
+                    j = tc[f]
+                    if f != e and j >= 0 and end[j] + hop[f][e] > st:
+                        st, p = end[j] + hop[f][e], j
+                tc[e] = i
+                left[t] -= 1
+                held[b] = left[t] > 0
+            x = free[e] = st + cost[i]
+            last[e] = i
+            if kind[i]:
+                if dmas > x + 900:
+                    p = dlast
+                dmas, dlast = max(dmas, x + 900) + extra[i], i
+                x = dmas + 800
+            end[i], pred[i] = x, p
+        span = max(end)
+        i, path = end.index(span), []
+        while i >= 0:
+            path.append(i)
+            i = pred[i]
+        return span + CFG["mean"] * sum(end) / n, path, end, bank, pred
+
+    def move(order, pos, a, b, ahead):
+        pa, pb = pos[a], pos[b]
+        if pa >= pb:
+            return False
+        grp, todo = ({b}, [b]) if ahead else ({a}, [a])
+        while todo:
+            for j in (dep if ahead else succ)[todo.pop()]:
+                if pa <= pos[j] <= pb and j not in grp:
+                    if j in (a, b) or len(grp) > 11:
+                        return False
+                    grp.add(j)
+                    todo.append(j)
+        seg = order[pa:pb + 1]
+        order[pa:pb + 1] = [x for x in seg if (x in grp) == ahead] + [x for x in seg if (x in grp) != ahead]
+        for q in range(pa, pb + 1):
+            pos[order[q]] = q
+        return True
+    seed = [CFG["seed"]]
+
+    def draw():
+        seed[0] = (seed[0] * 6364136223846793005 + 1442695040888963407) % 2 ** 64
+        return (seed[0] >> 11) / 2.0 ** 53
+    loads = len([o for o in ops if o["name"] == "load"])
+    order = list(range(loads)) + [i for i in seq if i >= loads]
+    span, path, end, _, pred = play(order)
+    best = (span, order, list(eng), list(cost))
+    for r in range(rounds):
+        if r % 500 == 499:
+            timed = sorted(order, key=lambda i: i - 1e9 if i < loads else end[i] - cost[i] - (extra[i] + 1700 if kind[i] else 0))
+            at = {x: q for q, x in enumerate(timed)}
+            if all(at[j] < at[i] for i in range(n) for j in dep[i]):
+                res = play(timed)
+                if res[0] <= span + 50:
+                    order, (span, path, end, _, pred) = timed, res
+        b = path[int(draw() * (len(path) - 1))] if draw() < CFG["onpath"] else int(draw() * n)
+        a = pred[b]
+        if a < 0:
+            continue
+        u, alike, trial, flips = draw(), draw() < (0.9 if r < 0.75 * rounds else 0.4), order, []
+        if a in waits[b] or u < 0.2:
+            x = b if draw() < 0.5 else a
+            if alt[x] is None:
+                continue
+            to = 1 - eng[x]
+            for y in ([twin[sign[x], t] for t in range(RO) if (sign[x], t) in twin] if alike and visit[x] >= 0 else [x]):
+                if eng[y] != to:
+                    flips.append((y, eng[y], cost[y]))
+                    eng[y], cost[y] = to, alt[y][to]
+        else:
+            ahead = draw() < 0.5
+            while ahead and pred[a] >= 0 and eng[pred[a]] == eng[b] and pred[a] not in waits[b] and draw() < CFG["jump"]:
+                a = pred[a]
+            pairs = [(a, b)]
+            if alike and min(visit[a], visit[b]) >= 0:
+                pairs = [(twin[sign[a], visit[a] + d], twin[sign[b], visit[b] + d]) for d in range(1 - RO, RO)
+                         if min(visit[a], visit[b]) + d >= 0 and (sign[a], visit[a] + d) in twin and (sign[b], visit[b] + d) in twin]
+            trial, pos = list(order), [0] * n
+            for k, x in enumerate(trial):
+                pos[x] = k
+            if not [1 for x, y in pairs if move(trial, pos, x, y, ahead)] or trial[:loads] != order[:loads]:
+                continue
+        res = play(trial)
+        if res[0] <= span or draw() < math.exp((span - res[0]) / (CFG["warm"] * (CFG["cool"] / CFG["warm"]) ** (r / rounds))):
+            order, (span, path, end, _, pred) = trial, res
+            if span < best[0]:
+                best = (span, order, list(eng), list(cost))
+        else:
+            for y, e, c in flips:
+                eng[y], cost[y] = e, c
+    span, order, eng[:], cost[:] = best
+    end, bank = play(order)[2:4]
+    return max(end), order, ["VSPGY"[e] for e in eng], [None if t < 0 else bank[t] for t in tile]
+
+
+PLAN = []
 
 
 def plan(ops):
     links(ops)
-    return lay(ops)
+    waits = [o["d"] for o in ops]
+    if not PLAN:
+        PLAN.append(polish(ops, waits, lay(ops), CFG["rounds"]))
+    _, seq, eng, bank = PLAN[0]
+    touch, sent = [{} for _ in range(8)], set()
+    for i in seq:
+        o = ops[i]
+        o["e"], o["d"] = eng[i], waits[i]
+        if o["k"] == "r":
+            sent = {i}
+        elif o["name"] == "copy":
+            o["d"] = o["d"] | sent
+        if bank[i] is not None:
+            o["t"]["b"] = bank[i]
+            o["d"] = o["d"] | set(j for e, j in touch[bank[i]].items() if e != o["e"])
+            touch[bank[i]][o["e"]] = i
+    return seq
 
 
 def rank_program(g, core, T, topo):

import math
from concourse.mybir import AluOpType, ActivationFunctionType

OP = AluOpType
AF = ActivationFunctionType
RO, NH, H = 4, 2, 128
FEAT0 = 1024
MEM0 = 2080
W19 = float(2 ** 19)
MAGIC = 1.5 * 2.0 ** 42
MAGIC1 = 1.5 * 2.0 ** 23
LOW = 2.0 ** 23
CFG = {
    "on_v": set(),
    "chunks": {"mem1": 2, "feat": 4, "mem2": 4},
    "stack1": False, "stack2": False,
    "same": 85.0, "other": 180.0, "psum": 360.0, "far": 120.0, "row": 30.0,
    "pe": 0.44, "rate": 400.0, "slack": 0.3, "pos": {}, "period": 27.0,
    "rounds": 80000, "warm": 200.0, "cool": 40.0, "seed": 3, "early": 2, "late": 0, "mean": 0.1, "onpath": 0.95, "jump": 0.5,
}
ORDER = """and0 mem00 su1 jq1 j1 mask1 jq0 j0 su0 mask0 mem1l1 mem11 mem1l0 pe1 n01 nu1 mem10 cmp1d1 cmp1b1 copy0 cmp1c1 cmp1a1 featd1 pe0 featc1
feata1 n00 cmp1a0 featb1 cmp1d0 cmp1c0 set1r1 cmp1b0 nu0 dista1 featc0 set11 distc1 distd1 feata0 distb1 featd0 featb0 xc1 arg1 set1r0 dista0 ls1 of1 fs1 sn1
set10 distb0 su21 mv1 mem2l1 zg1 x21 eqb1 distd0 distc0 xc0 mem21 newm1 newr1 oth1 old1 ys1 arg0 wl1 cmp2b1 ls0 scat1 of0 cmp2a1 sn0 fs0 su20 mem2l0 mv0 cmp2c1 zg0 eqb0 x20
newm0 newr0 mem20 old0 cmp2d1 ys0 wl0 scat0 cmp2a0 set2r1 cmp2b0 cmp2d0 set21 cmp2c0 oth0 yo1 set2r0 cnt0 yo0 set20 thr0""".split()
ON_V = "jq0 of set1r1 set2r1 su2 dista1 distb1 distc1 distd1 maskS1 newrS oldS cmp1LS cmp2LS".split()
for _i, _x in enumerate(ORDER):
    if _x != "|":
        CFG["pos"][_x[:-1], int(_x[-1])] = (_i - 8) * 0.36
for _x in ON_V:
    CFG["on_v"].update([(_x[:-1], int(_x[-1]) + _h) for _h in (0, 2)] if _x[-1] in "01" else [(_x, _h) for _h in range(4)])
CFG["on_v"] -= {("maskS", 3), ("cmp1LS", 2), ("cmp1LS", 3)}

SCRATCH = {
    "fw": ("sbuf", [128, FEAT0 + 4096], "bfloat16"),
    "snr": ("sbuf", [128, FEAT0 + 4096], "int32"),
    "tab": ("sbuf", [128, 2 * MEM0], "float32"),
    "tab1": ("sbuf", [128, 2 * MEM0], "float32"),
    "lmi": ("sbuf", [128, 2048], "int32"),
    "lmt": ("sbuf", [128, 2048], "int32"),
    "ramp": ("sbuf", [128, 2048], "float32"),
    "af": ("sbuf", [128, 5760], "float32"),
    "ab": ("sbuf", [128, 36864], "bfloat16"),
    "ah": ("sbuf", [128, 18432], "float16"),
    "ai": ("sbuf", [128, 2048], "int32"),
    "au": ("sbuf", [128, 4480], "uint16"),
}
for _b in range(NH):
    SCRATCH["old%d" % _b] = ("sbuf", [128, 8, 32], "float32")
    SCRATCH["new%d" % _b] = ("sbuf", [128, 8, 32], "float32")
for _b in range(8):
    SCRATCH["ps%d" % _b] = ("psum", [128, 512], "float32")
SEMAPHORES = ["cV", "cS", "cP", "cG", "left"] + ["d%d" % i for i in range(40)] + ["a%d" % i for i in range(24)]

CY, GA, SC = 0.85, 1.28, 3.1


def build(g, core, T, topo):
    rank = T.rank_of(core)
    n = len(T.cores)
    ops = []
    used = {"af": 0, "ab": 0, "ah": 0, "ai": 0, "au": 0}
    kept = {}
    cur = [(-1, 0)]
    V, S, P = g.vector, g.scalar, g.tensor

    def al(arena, w):
        a = used[arena]
        used[arena] = a + (w + 15) // 16 * 16
        assert used[arena] <= SCRATCH[arena][1][1], arena
        return [arena, a, w, "%s@%d" % (arena, a)]

    def tmp(name, h, w, arena="af"):
        if (name, h) not in kept:
            kept[name, h] = al(arena, w)
        return kept[name, h]

    def ap(b, lo=0, hi=None, step=1, p1=128):
        hi = b[2] if hi is None else hi
        p0, p1 = p1 if isinstance(p1, tuple) else (0, p1)
        if step == 1:
            return T[b[0]][p0:p1, b[1] + lo:b[1] + hi]
        return T[b[0]][p0:p1, b[1] + lo:b[1] + hi:step]

    def sub(b, q):
        return "%s/%s" % (b[3], q)

    def subs(b, m):
        return [sub(b, q) for q in range(m)]

    def keys(xs):
        return [x if isinstance(x, str) else x[3] for x in xs]

    def op(eng, fn, cost, r=(), w=(), t=None, lat=0.0, kind="c", name=""):
        ops.append({"e": eng, "fn": fn, "c": float(cost), "r": keys(r), "w": keys(w), "t": t, "lat": lat, "k": kind, "tv": cur[0], "name": name, "flex": False})
        if t is not None:
            t["n"] += 1

    tiles = [0]

    def tile(own=None):
        tiles[0] += 1
        return {"id": "t%d" % tiles[0], "own": own, "n": 0, "b": None, "open": False, "shut": False, "due": 0, "keys": []}

    def ps(t, lo, hi, step=1, p1=128):
        p0, p1 = p1 if isinstance(p1, tuple) else (0, p1)
        if step == 1:
            return T["ps%d" % t["b"]][p0:p1, lo:hi]
        return T["ps%d" % t["b"]][p0:p1, lo:hi:step]

    def got(t):
        t["shut"] = True
        return list(t["keys"])

    def vc(w, rate=1.0):
        return 5 + max(64, w * rate) * CY

    def sc(w):
        return 50 + w * CY

    def ts(out, in0, s1, s2, o0, o1=None):
        if o1 is None:
            return V.tensor_scalar(out, in0, s1, None, o0)
        return V.tensor_scalar(out, in0, s1, s2, o0, o1)

    def vts(o, i, s1, s2, o0, o1=None, r=()):
        op("V", lambda: [ts(ap(o), ap(i), s1, s2, o0, o1)], vc(o[2]), [i] + list(r), [o])

    def v1(name, fn, w, r, wr, t=None, rate=1.0):
        op("V", lambda: [fn()], vc(w, rate), r, wr, t, name=name)

    def gat(name, fn, w, r, wr):
        op("V", lambda: [fn()], 60 + w * GA, r, wr, name=name)

    def act(e, o, i, func=AF.Identity, bias=0.0, scale=1.0):
        if e == "S":
            return S.activation(o, i, func, bias=bias, scale=scale)
        if func == AF.Sigmoid:
            return ts(o, i, 0.0, 1.0 / 64, OP.is_equal, OP.mult)
        if func == AF.Relu:
            return ts(o, i, bias, 0.0, OP.add, OP.max)
        return ts(o, i, scale, bias, OP.mult, OP.add)

    def engine(name):
        return "V" if (name, cur[0][1] + 2 * (cur[0][0] <= 0)) in CFG["on_v"] else "S"

    def other(name):
        return engine(name + "S") == "V"

    def flex(name, fn, cs, cv, r=(), w=(), t=None):
        e = engine(name)
        op(e, fn, cs if e == "S" else cv, r, w, t, name=name)
        ops[-1]["flex"] = True
        ops[-1]["alt"] = [("S", cs), ("V", cv)]

    def lin(name, o, i, n_, r, w, t=None, func=AF.Identity, bias=0.0, scale=1.0, rate=1.0):
        flex(name, lambda e, _: [act(e, o, i() if t else i, func, bias, scale)], sc(n_), vc(n_, rate), r, w, t)

    def sact(o, i, bias=0.0, scale=1.0, r=()):
        op("S", lambda: [S.activation(ap(o), ap(i, 0, o[2]), AF.Identity, bias=bias, scale=scale)], sc(o[2]), [i] + list(r), [o])

    def pick(name, o, lo, hi, win, lst, a, b, r, w):
        flex(name, lambda e, _: [act(e, ap(o, lo, hi), win.indirect(ap(lst, a, b)))], 75 + (hi - lo) * GA, 60 + (hi - lo) * GA, r + [lst], w)

    def rounded(name, o, okey, tl, lo, w, magic, r1, r):
        def fn(e, chain):
            if e == "V":
                return [ts(o, ps(tl, lo, lo + w), magic, -magic, OP.add, OP.add)]
            chain(S.activation(ap(r1), ps(tl, lo, lo + w), AF.Identity, bias=magic))
            return [S.activation(o, ap(r1), AF.Identity, bias=-magic)]
        flex(name, fn, 2 * sc(w) + 60, vc(w), r, [okey, r1], tl)

    def mm(t, calls, cyc, r):
        def fn():
            last = None
            for c in calls:
                t["due"] -= 1
                last = P.matmul(ps(t, c[0], c[1], c[2], c[5] if len(c) > 5 else 128), c[3], c[4], not t["open"], t["due"] == 0)
                t["open"] = True
            return [last]
        t["due"] += len(calls)
        assert not t["shut"]
        t["keys"].append("%s/%d" % (t["id"], len(ops)))
        op("P", fn, 10 + cyc * CFG["pe"], r, t["keys"][-1:], t)

    def dma(q, pairs, nbytes, r=(), w=(), name="dma", rows=128):
        eng = g.sync if q == "Y" else g.scalar
        op(q, lambda: [eng.dma_start(o, i) for o, i in pairs], 60 * len(pairs), r, w, lat=nbytes / CFG["rate"] + rows / 16 * CFG["row"], kind="d", name=name)

    arr = [0]

    def send(h, out, in_, r, w, nbytes):
        dst = T.cores[(rank + 1 + h) % n]
        rid, pid, _ = topo.addr(dst)
        eng = topo.engines(core, dst)[:8]
        m = sum(1 << e for e in eng)
        sem = "a%d" % arr[0]
        arr[0] += 1
        op("G", lambda: [g.remote_dma(out, in_, T.sem[sem], T.sem.left, pid, rid, m)], 400, r, w, lat=nbytes / CFG["far"] + 16 * CFG["row"], kind="r", name="send")
        ops[-1]["sem"] = sem
        ops[-1]["n"] = len(eng)

    def strip(t, h):
        return (7 - (2 * t + h)) * H

    def xap(t, h):
        return T.fw[:, strip(t, h):strip(t, h) + H]

    s0, vt0, lpq = al("ai", 256), al("ai", 512), al("ai", 512)
    dma("Y", [(ap(s0, p1=8), T.ls[:, :])], 8192, w=[s0], name="load")
    dma("S", [(xap(0, h), T.lx[:, H * h:H * h + H]) for h in range(NH)], 65536, w=["x00", "x01"], name="load")
    for q in range(4):
        dma("YS"[q % 2], [(T.lmi[:, 512 * q:512 * q + 512], T.lm[:, 512 * q:512 * q + 512])], 262144, w=["lmi%d" % q], name="load")
    dma("Y", [(ap(lpq, 0, 256), T.lp[:, :]), (ap(lpq, 256, 512), T.lq[:, :])], 262144, w=[lpq], name="load")
    dma("Y", [(T.fw[:, FEAT0:FEAT0 + 4096], T.feat[:, :])], 1048576, w=["feat"], name="load")
    dma("Y", [(ap(vt0, 0, 256, p1=8), T.lv[:, :]), (ap(vt0, 256, 512, p1=8), T.th[:, :])], 16384, w=[vt0], name="load")
    dma("Y", [(T.snr[i:128:16, FEAT0:FEAT0 + 4096], T.sn[:, :]) for i in range(16)], 2097152, w=["snr"], name="load")

    def iota(arena, pat, base, cm):
        b = al(arena, math.prod(c for _, c in pat))
        if arena == "ai":
            op("G", lambda: [g.iota(ap(b), pat, base, cm)], 130 + 1.7 * b[2], [], [b])
        else:
            op("G", lambda: [g.iota(ap(b), pat, base, cm, allow_small_or_imprecise_dtypes=True)], 130 + 1.7 * b[2], [], [b])
        return b

    def where(src, pat, cmp, base, cm, arena="ab", w=None):
        m = math.prod(c for _, c in pat)
        b = al(arena, w or m)
        op("G", lambda: [g.affine_select(ap(b, 0, m), ap(src, 0, m), pat, cmp, 0.0, base, cm)], 170 + 1.7 * m, [src], [b])
        return b

    def in_group(src, pat):
        neg = [[-s, c] for s, c in pat]
        return where(where(src, pat, OP.is_ge, 0, 1), neg, OP.is_ge, 15, -1)

    def scaled(src, k, arena="ab", bias=0.0):
        b = al(arena, src[2])
        flex("k%d" % (len(ops) % 4), lambda e, _: [act(e, ap(b), ap(src), AF.Identity, bias, float(k))], sc(src[2]), vc(src[2], 0.5), [src], [b])
        return b

    ones = al("ab", 256)
    op("V", lambda: [V.memset(ap(ones), 1.0)], vc(256, 0.5), [], [ones])
    op("V", lambda: [V.memset(T.tab[:, MEM0 + 2048:2 * MEM0], 0.0), V.memset(T.tab1[:, 2048:MEM0], 0.0)], 2 * vc(16), [], ["padm0", "pad1"])
    bo = in_group(ones, [[-16, 8], [0, 16]])
    ib = where(ones, [[-1, 128]], OP.is_equal, 0, 1)
    wsel = where(ones, [[1, 144]], OP.is_equal, -15, -16)
    keep = where(ones, [[0, 8], [1, 16]], OP.not_equal, 0, 0)
    bo8 = in_group(ones, [[0, 16], [-16, 8]])
    shift = al("ab", 1024)
    for a in range(4):
        op("G", lambda a=a: [g.affine_select(ap(shift, 256 * a, 256 * a + 256), ap(ones), [[0, 2], [-1, 16], [-16, 8]], OP.is_equal, 0.0, 0, 1)], 170 + 1.7 * 256, [ones], [sub(shift, a)])
    zeros = al("ab", H)
    op("V", lambda: [V.memset(ap(zeros), 0.0)], vc(H, 0.5), [], [zeros])

    def eye(k):
        b = al("ab", H)
        op("G", lambda: [g.affine_select(ap(b), ap(zeros), [[-1, H]], OP.not_equal, float(k), 0, 1)], 170 + 1.7 * H, [zeros], [b])
        return b
    wall = scaled(in_group(where(ones, [[0, 9], [1, 16]], OP.is_equal, -15, 0), [[-16, 9], [0, 16]]), 4096)
    ioq, ion, pc, ioa = iota("ai", [[0, 1]], 0, 1), iota("ai", [[-1, 20]], 32, 1), iota("af", [[0, 8], [1, 16]], 0, 0), iota("ai", [[1, 128]], 0, 1)
    c8, c16 = iota("ai", [[1, 8]], 0, 0), iota("af", [[16, 8]], 0, 0)
    for q in range(4):
        op("G", lambda q=q: [g.iota(T.ramp[:, 512 * q:512 * q + 512], [[4096, 512]], 2048 + 4096 * 512 * q, 0, allow_small_or_imprecise_dtypes=True)], 1000, [ib], ["ramp%d" % q])
    RAMP = ["ramp%d" % q for q in range(4)]
    op("G", lambda: [g.iota(T.snr[:, 0:FEAT0], [[0, FEAT0]], 0, 0)], 130 + 1.7 * FEAT0, [ib], ["snpad"])
    pqi, ni, pa, pq = al("ai", 1), al("ai", 20), al("ai", 128), al("af", 1)
    cols, diag, paf, l_col, lane8 = al("ab", 20), al("ab", H), al("ab", 128), al("au", 8), al("af", 8)
    pen0, pen1, pen = al("ab", H), al("ab", H), al("ab", H)
    vts(pqi, ioq, 15, None, OP.bitwise_and)
    vts(pq, pqi, 1.0, None, OP.mult)
    vts(ni, ion, 15, None, OP.bitwise_and)
    vts(cols, ni, 1.0 / 16, None, OP.mult)
    vts(diag, pc, ap(pq), None, OP.is_equal, r=[pq])
    vts(pen0, pc, ap(pq), -2048.0, OP.not_equal, OP.mult, r=[pq])
    vts(pen1, pc, ap(pq), -4096.0, OP.is_lt, OP.mult, r=[pq])
    v1("", lambda: V.tensor_tensor(ap(pen), ap(pen0), ap(pen1), OP.add), H, [pen0, pen1], [pen], rate=2.0)
    vts(pa, ioa, 1, None, OP.bitwise_and)
    vts(paf, pa, -1.0, 8192.0, OP.add, OP.mult)
    par = in_group(paf, [[-16, 8], [0, 16]])
    vts(l_col, c8, 1.0, None, OP.mult)
    vts(lane8, c16, ap(pq), None, OP.add, r=[pq])
    dum = scaled(pq, 1, "af", 2048.0)
    bo_16, bo16 = scaled(bo, 1.0 / 16), scaled(bo, 16)
    bo32 = in_group(ones, [[-16, 8], [0, 32]])
    bo4p, bo4n = scaled(bo32, 4), scaled(bo32, -4)
    ineg, i16n, ihalf, iquar, i8n, ilow, i64k, i128, i128n = [eye(k) for k in (-1, -16, 0.5, -0.25, -8192, LOW, -65536, 128, -128)]
    if any(x[0][:4] == "dist" for x in CFG["on_v"]):
        bo16n, bo32b = scaled(bo, -16), scaled(bo, 32)
    if not (CFG["stack1"] and CFG["stack2"]):
        bow, iw = scaled(bo, -W19), eye(-W19)
    i32 = scaled(ib, 1, "af")
    forms = set(x[0] for x in CFG["on_v"])
    if "maskS" in forms:
        colr = [scaled(pq, 1, "af", float(t)) for t in range(RO)]
    if "oldS" in forms:
        ihigh = eye(-2.0 ** 24)
    if forms & {"cmp1LS", "cmp2LS"}:
        wide, minus = al("ab", 2048), al("ab", 512)
        op("V", lambda: [V.memset(ap(minus), -1.0)], vc(512, 0.5), [], [minus])
        for q in range(4):
            op("G", lambda q=q: [g.affine_select(ap(wide, 512 * q, 512 * q + 512), ap(minus), [[-1, 32], [0, 16]], OP.is_equal, 0.0, -32 * q, 1)], 170 + 1.7 * 512, [minus], [sub(wide, q)])
    if "newrS" in forms:
        i4k = eye(4096)
    d0 = scaled(keep, -2.0 ** 23 - 1, "af", 2.0 ** 23)
    rst16 = scaled(keep, 8192, "ab", -8192.0)
    offm = scaled(bo8, 2.0 ** 20, "ab", -2.0 ** 20)
    rst = {h: al("af", H) for h in range(NH)}
    for h in range(NH):
        op("V", lambda h=h: [V.memset(ap(rst[h]), 2.0 ** 21)], vc(H), [], [rst[h], sub(rst[h], 0)])
        op("V", lambda h=h: [V.memset(ap(rst[h], 8, H, 16), -2.0 ** 21)], vc(8), [], [rst[h]])
    if CFG["stack1"] or CFG["stack2"]:
        dif, red = al("ab", 1024), al("ab", 256)
        for q in range(4):
            op("G", lambda q=q: [g.affine_select(ap(dif, 256 * q, 256 * q + 256), ap(ones), [[0, 16], [-32, 2], [-2, 8]], OP.is_equal, 0.0, -64 * (q // 2) - 16 * (q % 2) - 1, 1)],
               170 + 1.7 * 256, [ones], [sub(dif, q)])
            op("G", lambda q=q: [g.affine_select(ap(dif, 256 * q, 256 * q + 256), ap(dif, 256 * q, 256 * q + 256), [[-2, 16], [-32, 2], [0, 8]], OP.not_equal, -1.0, -64 * (q // 2), 1)],
               170 + 1.7 * 256, [sub(dif, q)], [sub(dif, q)])
        tl = tile()
        mm(tl, [(64 * u, 64 * u + 64, 1, ap(dif, 128 * u, 128 * u + 128), ap(ib, 0, 64)) for u in range(4)], 256, [ib] + subs(dif, 2))
        v1("", lambda tl=tl: ts(ap(red), ps(tl, 0, 256), 0.0, -W19, OP.not_equal, OP.mult), 256, got(tl), [red], tl)

    for q in range(4):
        a, b = 512 * q, 512 * q + 512
        op("V", lambda a=a, b=b: [ts(T.lmt[:, a:b], T.lmi[:, a:b], 4095, None, OP.bitwise_and)], vc(512), ["lmi%d" % q], ["lmt%d" % q], name="and")
        lin("mem0", T.tab[:, MEM0 + a:MEM0 + b], T.lmt[:, a:b], 512, ["lmt%d" % q], ["mem%d" % q], bias=-2048.0)
    for q in range(4):
        a, b = 512 * q, 512 * q + 512
        lin("rec0", T.tab1[:, a:b], T.lmi[:, a:b], 512, ["lmi%d" % q, "mem3"], ["rec%d" % (q + 4)])
    sh, vth, thl, ea, eb = al("ah", 256), al("ah", 512), al("af", 16), al("ah", 512), al("ah", 512)
    lin("sh", ap(sh, p1=8), ap(s0, p1=8), 256, [s0], [sh])
    lin("vth", ap(vth, p1=8), ap(vt0, p1=8), 512, [vt0], [vth], bias=-2048.0)
    t0, t1 = tile(), tile()
    mm(t0, [(0, 16, 1, ap(wsel, 15 - p, 143 - p, p1=8), ap(sh, p, 256, 16, p1=8)) for p in range(16)], 16 * 64, [wsel, sh])
    sv = {(t, h): al("af", 8) for t in range(RO) for h in range(NH)}
    vb = {(t, h): al("ah", H) for t in range(RO) for h in range(NH)}
    pm = {(t, h): al("ah", 256) for t in range(RO) for h in range(NH)}
    for h in range(NH):
        lin("sv", ap(sv[0, h]), lambda h=h: ps(t0, 8 * h, 8 * h + 8), 8, got(t0), [sv[0, h]], t0)
    dma("Y", [(T.ah[i:128:16, vb[0, 0][1]:vb[0, 0][1] + 256], ap(vth, 0, 256, p1=8)) for i in range(16)], 65536, r=[vth], w=[vb[0, 0], vb[0, 1]])
    mm(t1, [(8 * h, 8 * h + 8, 1, ap(vth, 256 + H * h, 256 + H * h + H, p1=8), ap(ib, 0, 8, p1=8)) for h in range(NH)], 128, [vth, ib])
    lin("thl", ap(thl), lambda: ps(t1, 0, 16), 16, got(t1), [thl], t1, bias=32768.0 - 15, scale=16.0)
    op("S", lambda: [S.activation(ap(ea), ap(lpq), AF.Relu, scale=-2048.0)], sc(512), [lpq], [ea])
    lin("eb", ap(eb), ap(lpq), 512, [lpq], [eb], bias=-2048.0)
    for h in range(NH):
        tl = tile()
        mm(tl, [(m, 256, 2, ap(e, 256 * m + H * h, 256 * m + H * h + H), ap(ineg if e is ea else ib)) for m in range(2) for e in (ea, eb)], 512, [ea, eb, ib, ineg])
        lin("pm0", ap(pm[0, h]), lambda tl=tl: ps(tl, 0, 256), 256, got(tl), subs(pm[0, h], 2), tl)

    mask = {(u, h): al("ab", 2048) for u in range(2) for h in range(NH)}
    gm, gn = [{h: al("ah", 2048) for h in range(NH)} for _ in range(2)]
    sg1, sg2, fb, db = [{h: al("ab", 2048) for h in range(NH)} for _ in range(4)]
    g2 = al("ab", 32 * RO)
    op("V", lambda: [V.memset(ap(g2), 0.0)], vc(32 * RO, 0.5), [], subs(g2, NH * RO))

    def members(name, dst, win, rw, lst, mk, tab, MEM, behind=()):
        a, nc = al("au", H), CFG["chunks"][name]
        cw = 2048 // nc
        flex(name + "l", lambda e, _: [act(e, ap(a), win.indirect(ap(lst)), AF.Identity, -0.5 + 1.0 / 8192, 1.0 / 4096)], 75 + H * GA, 60 + H * GA, rw + [lst], [a])
        for q in range(nc):
            out, col = ap(dst, cw * q, cw * q + cw), tab[:, MEM0:MEM0 + 2048].indirect(ap(a, cw // 16 * q, cw // 16 * (q + 1)))
            if other(name + "abcd"[q]):
                tl = tile()
                op("S", lambda out=out, col=col: [act("S", out, col)], 75 + cw * GA, MEM + [a], [sub(dst, q)], name=name)
                mm(tl, [(0, cw, 1, ap(ib), ap(mk, cw * q, cw * q + cw))], cw, [ib, sub(dst, q)] + subs(mk, 4))
                v1(name + "m", lambda out=out, tl=tl: V.tensor_tensor(out, ps(tl, 0, cw), out, OP.mult), cw, got(tl), [sub(dst, q)], tl)
            else:
                gat(name, lambda out=out, col=col, q=q: V.tensor_tensor(out, col, ap(mk, cw * q, cw * q + cw), OP.mult), cw,
                    MEM + [a] + subs(mk, 4) + (list(behind) if q >= nc - CFG["late"] else []), [sub(dst, q)])
        return subs(dst, nc)

    def steps(name, sg, b, tl):
        if other(name):
            v1(name + "abcd"[b], lambda: act("V", ap(sg, 512 * b, 512 * b + 512), ps(tl, 0, 512), AF.Sigmoid), 512, got(tl), [sub(sg, b)], tl)
            return
        flex(name + "abcd"[b], lambda e, _: [act(e, ap(sg, 512 * b, 512 * b + 512), ps(tl, 0, 512), AF.Sigmoid, -math.log(63.0), 64.0)],
             sc(512), vc(512), got(tl), [sub(sg, b)], tl)

    def compare(name, sg, src, skeys, other, okey, after):
        if engine(name + "LS") == "V":
            for b in range(4):
                tl = tile()
                mm(tl, [(0, 512, 1, other, ap(wide, 512 * b, 512 * b + 512)), (0, 512, 1, ap(bo), ap(src, 512 * b, 512 * b + 512))], 1024,
                   [bo, sub(wide, b), okey, skeys[b * len(skeys) // 4]])
                steps(name, sg, b, tl)
            for b in range(4):
                after(b, lambda k: ap(sg, k, 2048, 16), subs(sg, 4))
            return
        for b in range(4):
            tl = tile()
            calls = []
            for u in range(4):
                calls.append((128 * u, 128 * u + 128, 1, ap(bo), ap(src, 4 * b + u, 2048, 16)))
                calls.append((128 * u, 128 * u + 128, 1, other, ap(ineg)))
            mm(tl, calls, 1024, [bo, ineg, okey] + skeys)
            steps(name, sg, b, tl)
            after(b, lambda k: ap(sg, H * k, H * k + H), [sub(sg, b)])

    def stacked(name, sg, u_, h, into, lo, w):
        tt, st, first = tile(), tmp(name + "t", h, 256, "ah"), into["keys"][-1]
        mm(tt, [(H * m, H * m + H, 1, ap(u_, H * m, H * m + H), ap(ib)) for m in range(2)], 256, [ib] + subs(u_, 2))
        lin(name + "t", ap(st), lambda: ps(tt, 0, 256), 256, got(tt), [st], tt)
        for b in range(4):
            tl = tile()
            mm(tl, [(128 * u, 128 * u + 128, 1, ap(dif, 512 * (b % 2) + 128 * u, 512 * (b % 2) + 128 * u + 128), ap(st, H * (b // 2), H * (b // 2) + H)) for u in range(4)],
               512, [st] + subs(dif, 4))
            steps(name, sg, b, tl)
            mm(into, [(lo + 32 * w * b, lo + 32 * w * (b + 1), 1, ap(sg, 512 * b + 128 * u, 512 * b + 128 * u + 128), ap(red, 64 * u, 64 * u + 64, 3 - w)) for u in range(4)],
               256, [red, sub(sg, b), first])

    def settle(name, tl, w, o, okeys, h, kept_=None):
        if kept_ is not None:
            v1(name, lambda: V.tensor_tensor(o, ps(tl, 0, w), ap(kept_), OP.max), w, got(tl) + [kept_], okeys, tl)
            return
        rr, left = tmp(name + "r", h, w), tmp(name + "l", h, w)
        rounded(name + "r", ap(rr), rr, tl, 0, w, MAGIC, left, got(tl))
        v1(name, lambda: V.tensor_tensor(ap(left), ps(tl, 0, w), ap(rr), OP.subtract), w, [rr], [left], tl)
        v1(name, lambda: V.tensor_tensor(o, ps(tl, w, 2 * w), ap(left), OP.max), w, [left], okeys, tl)

    def half(t, h, tab, rec, MEM, REC, thr, xout):
        last = t == RO - 1
        mk, xk, x, s_, lane = mask[t % 2, h], "x%d%d" % (t, h), xap(t, h), sv[t, h], pm[t, h]
        old, new = T["old%d" % h], T["new%d" % h]
        shift0 = float(FEAT0 - strip(t, h) + 2048)
        tj = tile()
        mm(tj, [(0, H, 1, ap(bo_16), x)], 128, [bo_16, xk])
        jq, jw, up = tmp("jq", h, H, "ai"), tmp("jw", h, H, "ab"), tmp("up", h, H, "ab")
        lin("jq", ap(jq), lambda: ps(tj, 0, H), H, got(tj), [jq], tj, bias=-15.0 / 32)
        v1("j", lambda: V.tensor_tensor(ap(jw), ps(tj, 0, H), ap(jq), OP.subtract), H, [jq], [jw], tj)
        if other("mask"):
            ji = al("au", H)
            sact(ji, jw, scale=16.0, bias=ap(colr[t]), r=[colr[t]])
            for q in range(4):
                op("S", lambda q=q: [act("S", ap(mk, 512 * q, 512 * q + 512), ap(diag).indirect(ap(ji, 32 * q, 32 * q + 32)))], 75 + 512 * GA, [diag, ji], [sub(mk, q)], name="mask")
            ohk = subs(mk, 4)
        else:
            for q in range(4):
                op("V", lambda q=q: [ts(ap(mk, k, 2048, 16), ap(jw), ap(cols, k + t, k + t + 1), None, OP.is_equal) for k in range(4 * q, 4 * q + 4)],
                   4 * vc(H, 0.5), [jw, cols], [sub(mk, q)], name="mask")
            ohk = subs(mk, 1)
        oh = ap(mk, 0, 2048, 16)
        if not other("old"):
            lin("up", ap(up), oh, H, ohk, [up], scale=-2.0 ** 24, rate=0.5)
        su = al("au", 8)
        lin("su", ap(su), ap(s_), 8, [s_], [su])
        GM = members("mem1", gm[h], rec, REC, su, mk, tab, MEM)
        yield GM
        ty, tp = tile(h), tile()
        pe, pc_, u2, nu = tmp("pe", h, H, "ah"), tmp("pc", h, H, "ah"), tmp("u2", h, 256, "ah"), al("au", H)
        mm(tp, [(0, H, 1, oh, ap(par)), (0, H, 1, ap(ib), ap(lane, 0, 256, 2))], 256, [ib, par, sub(lane, 0)] + ohk)
        v1("pe", lambda: ts(ap(pe), ps(tp, 0, H), -4096.0, None, OP.max), H, got(tp), [pe], tp)
        if CFG["stack1"]:
            lin("pc", ap(pc_), ap(lane, 0, 256, 2), H, [sub(lane, 0)], [pc_], rate=0.5)
            n0, n0k, pold, poldk = ap(lane, 0, 256, 2), sub(lane, 0), ap(pc_), pc_
        else:
            n0k = tmp("n0", h, H, "ah")
            n0, pold, poldk = ap(n0k), ap(lane, 0, 256, 2), sub(lane, 0)
        nl, nlk = ap(u2, 0, 256, 2), sub(u2, 0)
        mm(ty, [(0, H, 1, ap(i64k), ap(ones, 0, H)), (0, H, 1, ap(i16n), ap(pe))], 256, [i64k, ones, i16n, pe])
        nc = CFG["chunks"]["feat"]
        cw = 2048 // nc
        mm(ty, [(k, H, 16, ap(gm[h], k, 2048, 16), ap(bo, 0, 128, 16)) for k in range(16)], 1024, [bo] + GM)
        v1("n0", lambda: V.tensor_tensor(n0, ps(ty, 0, H), ap(pe), OP.max), H, [pe] + got(ty), [n0k], ty)
        tn = tile()
        mm(tn, [(0, H, 1, n0, ap(ib))], 128, [n0k, ib])
        lin("nu", ap(nu), lambda: ps(tn, 0, H), H, got(tn), [nu], tn, bias=2048.0)
        for q in range(nc):
            pick("feat" + "abcd"[q], fb[h], cw * q, cw * q + cw, T.fw[:, FEAT0:FEAT0 + 4096], nu, cw // 16 * q, cw // 16 * (q + 1), ["feat"], [sub(fb[h], q)])
        FB = subs(fb[h], nc)
        if not last:
            send(h, ap(vb[t + 1, h]), ap(vb[t, h]), [vb[t, h], nu], [vb[t + 1, h]], 32768)
        tz, td = tile(), tile(h)
        mm(tz, [(0, H, 1, ap(ib), n0), (H, 2 * H, 1, ap(ib), ap(pe))][:1 if other("cmp1") else 2], 128 if other("cmp1") else 256, [ib, pe, n0k])
        if CFG["stack1"]:
            stacked("cmp1", sg1[h], lane, h, tz, 0, 1)
        else:
            compare("cmp1", sg1[h], gm[h], GM, ap(lane, 1, 256, 2), sub(lane, 1), lambda b, col, ck: mm(
                tz, [(k, H, 16, col(k), ap(bow, 0, 128, 16)) for k in range(4 * b, 4 * b + 4)], 256, [bow, tz["keys"][0]] + ck))
        settle("set1", tz, H, nl, [nlk], h, pe if other("cmp1") else None)
        by_max = [engine("dist" + "abcd"[b]) == "V" for b in range(4)]
        if all(by_max):
            mm(td, [(0, H, 1, ap(i128), n0), (0, H, 1, x, ap(bo16n))], 256, [i128, n0k, xk, bo16n])
        else:
            mm(td, [(0, H, 1, ap(i128), n0)], 128, [i128, n0k])
        if any(by_max):
            txp = tile()
            mm(txp, [(0, H, 1, ap(ib), x)], 128, [ib, xk] + FB)
        for b in range(4):
            ks = range(4 * b, 4 * b + 4)
            if by_max[b]:
                op("V", lambda ks=ks: [V.tensor_tensor(ap(db[h], H * k, H * k + H), ps(txp, 0, H), ap(fb[h], k, 2048, 16), OP.max) for k in ks],
                   4 * vc(H), FB + got(txp), [sub(db[h], b)], txp, name="dist" + "abcd"[b])
                if all(by_max):
                    mm(td, [(k, H, 16, ap(fb[h], k, 2048, 16), ap(bo16n, 0, 128, 16)) for k in ks], 256, [bo16n, td["keys"][0]] + FB)
                else:
                    mm(td, [(k, H, 16, l, ap(bo16n, 0, 128, 16)) for k in ks for l in (x, ap(fb[h], k, 2048, 16))], 512, [bo16n, xk, td["keys"][0]] + FB)
                mm(td, [(k, H, 16, ap(db[h], H * k, H * k + H), ap(bo32b, 0, 128, 16)) for k in ks], 256, [bo32b, sub(db[h], b), td["keys"][0]])
            else:
                tl = tile()
                calls = []
                for u in range(4):
                    calls.append((128 * u, 128 * u + 128, 1, ap(ib), ap(fb[h], 4 * b + u, 2048, 16)))
                    calls.append((128 * u, 128 * u + 128, 1, ap(ineg), x))
                mm(tl, calls, 1024, [ib, ineg, xk] + FB)
                op("S", lambda b=b, tl=tl: [S.activation(ap(db[h], 512 * b, 512 * b + 512), ps(tl, 0, 512), AF.Abs)], sc(512), got(tl), [sub(db[h], b)], tl, name="dist" + "abcd"[b])
                mm(td, [(k, H, 16, ap(db[h], H * k, H * k + H), ap(bo16, 0, 128, 16)) for k in ks], 256, [bo16, sub(db[h], b), td["keys"][0]])
        mm(td, [(0, H, 1, ap(i128n), nl), (H, 2 * H, 1, ap(ib), nl), (H, 2 * H - 1, 1, ap(ineg), ap(u2, 2, 256, 2)), (H + 15, 2 * H - 16, 16, ap(ib), ap(u2, 32, 256, 32))], 448,
           [nlk, ib, ineg, i128n])
        tv = tile()
        if other("newr"):
            sb = tmp("sb", h, H, "ah")
            op("S", lambda: [act("S", ap(sb), T.ramp[:, :].indirect(ap(su)), AF.Identity, -0.5, 1.0 / 4096)], 75 + H * GA, RAMP + [su], [sb], name="newr")
            mm(tv, [(H, 2 * H, 1, ap(ilow), oh), (H, 2 * H, 1, ap(ib), ap(vb[t, h])), (H, 2 * H, 1, ap(i4k), ap(sb))], 384, [ilow, ib, vb[t, h], i4k, sb] + ohk)
        if not (last and other("newr")):
            mm(tv, [(0, H, 1, ap(ilow), oh), (0, H, 1, ap(ib), ap(vb[t, h]))], 256, [ilow, ib, vb[t, h]] + ohk)
            lin("newm", new[:, :, 16:32], lambda: ps(tv, 0, H), H, got(tv), ["newm%d" % h], tv, bias=-LOW)
        if other("newr"):
            op("S", lambda: [act("S", new[:, :, 0:16], ps(tv, H, 2 * H), AF.Identity, 2048.0 - LOW)], sc(H), got(tv), ["newr%d" % h], tv, name="newr")
        else:
            gat("newr", lambda: V.tensor_tensor(new[:, :, 0:16], T.ramp[:, :].indirect(ap(su)), new[:, :, 16:32], OP.add), H, RAMP + [su, "newm%d" % h], ["newr%d" % h])
        kk, nt, sp2, ls = tmp("kk", h, H), tmp("nt", h, H), tmp("sp2", h, 256, "ah"), tmp("ls", h, H)
        lin("xc", ap(rst[h], 0, H, 16), ap(lane8), 8, [lane8, rst[h]], [sub(rst[h], 0)], bias=-shift0)
        v1("arg", lambda: V.tensor_tensor_scan(ap(kk), ap(d0), ps(td, 0, H), 0.0, OP.add, OP.min), H, [d0] + got(td), [kk], td)
        v1("arg", lambda: V.tensor_tensor(ap(nt), ps(td, 0, H), ap(kk), OP.not_equal), H, [kk], [nt], td)
        v1("arg", lambda: V.tensor_tensor(ap(sp2, H + 15, 2 * H, 16), ap(kk, 15, H, 16), ap(thr, 8 * h, 8 * h + 8), OP.is_lt), 8, [kk, thr], [sub(sp2, 1)])
        v1("arg", lambda: V.tensor_tensor_scan(ap(sp2, 0, H), ap(nt), ps(td, H, 2 * H), 0.0, OP.mult, OP.add), H, [nt], [sub(sp2, 0)], td)
        to = tile()
        mm(to, [(0, H, 1, ap(ib), ap(offm))] + [(16 * c, 16 * c + 16, 1, ap(shift, c, 1024, 8), ap(sp2, 15, 256, 16)) for c in range(8)],
           128 + 512, [ib, offm] + subs(shift, 4) + subs(sp2, 2))
        v1("ls", lambda: V.tensor_tensor_scan(ap(ls), ap(rst[h]), ps(to, 0, H), 0.0, OP.min, OP.max), H, [rst[h], sub(rst[h], 0)] + got(to), [ls], to)
        near = ap(ls, 15, H, 16)
        of = al("au", 8)
        lin("of", ap(of), ap(ls, 7, H, 16), 8, [ls], [of], bias=shift0)
        fs = tmp("fs", h, H, "ab")
        pick("fs", fs, 0, H, T.fw[:, strip(t, h):FEAT0 + 4096], of, 0, 8,
             ["feat"] + ["x%d%d" % (u, v) for u in range(t + 1) for v in range(NH) if 2 * u + v <= 2 * t + h], [fs])
        tx = tile()
        mm(tx, [(0, H, 1, ap(ihalf), x), (0, H, 1, ap(iquar), ap(ones, 0, H)), (0, H, 1, ap(ihalf), ap(fs))], 384, [ihalf, iquar, ones, xk, fs])
        if last:
            rounded("x2", ap(xout, H * h, H * h + H), sub(xout, h), tx, 0, H, MAGIC1, tmp("x1", h, H), got(tx))
        else:
            x2 = al("ab", H)
            rounded("x2", ap(x2), x2, tx, 0, H, MAGIC1, tmp("x1", h, H), got(tx))
            send(h, xap(t + 1, h), ap(x2), [x2], ["x%d%d" % (t + 1, h)], 32768)
        zs, sr = tmp("zs", h, H, "ah"), tmp("sr", h, H, "ah")
        sp, go = ap(zs, 15, H, 16), ap(g2, 32 * t + 16 * h, 32 * t + 16 * h + 8)
        su2, d, e, so, ko, gk = al("au", 8), al("af", 8), al("af", 8), al("af", 8), al("af", 8), sub(g2, NH * t + h)
        gat("sn", lambda: V.tensor_tensor(ap(sr), T.snr[:, strip(t, h):FEAT0 + 4096].indirect(ap(of)), ap(pen), OP.add), H, ["snr", "snpad", of, pen], [sr])
        v1("sn", lambda: V.tensor_tensor_scan(ap(zs), ap(rst16), ap(sr), 0.0, OP.add, OP.max), H, [rst16, sr], [zs], rate=0.5)
        lin("su2", ap(su2), sp, 8, [zs], [su2])
        v1("mv", lambda: V.tensor_tensor(ap(d), sp, ap(s_), OP.subtract), 8, [zs, s_], [d])
        v1("mv", lambda: V.tensor_tensor(ap(e), ap(d), near, OP.mult), 8, [d, ls], [e])
        v1("mv", lambda: ts(go, ap(e), 0.0, 2048.0, OP.not_equal, OP.mult), 8, [e], [gk])
        v1("mv", lambda: V.tensor_tensor(ap(ko), sp, go, OP.subtract), 8, [zs, gk], [ko])
        v1("mv", lambda: V.tensor_tensor(ap(so), ap(e), ap(s_), OP.add), 8, [e, s_], [so])
        eqb = tmp("eqb", h, H, "ab")
        gat("eqb", lambda: V.tensor_tensor(ap(eqb), ap(ko).indirect(ap(l_col)), ap(sr), OP.is_equal), H, [ko, sr, l_col], [eqb])
        tw = tile()
        mm(tw, [(0, 8, 1, ap(ib), sp)] + [(0, 8, 1, ap(wall, 15 - p, 143 - p), ap(eqb, p, H, 16)) for p in range(16)], 64 * 17, [ib, wall, zs, eqb])
        wl = al("au", 16)
        nm = 1 if last else 2
        op("V", lambda: [ts(ap(wl, m, 16, 2), ps(tw, 0, 8), ap(dum), float(MEM0 * m), OP.min, OP.add) for m in range(nm)], nm * vc(8), [dum] + got(tw), [wl], tw, name="wl")
        for m, (win, rw) in enumerate(((rec, REC), (tab[:, MEM0:MEM0 + 2048], MEM))[:nm]):
            if other("old"):
                raw, tu = tmp("raw%d" % m, h, H, "ah" if m else "af"), tile()
                op("S", lambda win=win, raw=raw: [act("S", ap(raw), win.indirect(ap(su2)))], 75 + H * GA, rw + [su2], [raw], name="old")
                mm(tu, [(0, H, 1, ap(ib if m else i32), ap(raw)), (0, H, 1, ap(ihigh), oh)], 256 if m else 640, [ib, i32, ihigh, raw] + ohk)
                op("S", lambda m=m, tu=tu: [act("S", old[:, :, 16 * m:16 * m + 16], ps(tu, 0, H))], sc(H), got(tu), ["old%d%d" % (h, m)], tu, name="old")
            else:
                gat("old", lambda m=m, win=win: V.tensor_tensor(old[:, :, 16 * m:16 * m + 16], win.indirect(ap(su2)), ap(up), OP.add), H, rw + [su2, up], ["old%d%d" % (h, m)])
        if not last:
            send(h, ap(sv[t + 1, h]), ap(so), [so], [sv[t + 1, h]], 4096)
        else:
            tys, ysb = tile(), al("af", H)
            mm(tys, [(p, H, 16, ap(i32, p, 128, 16), ap(so, 0, 8), 8) for p in range(16)], 16 * 4 * 8, [i32, so])
            lin("ys", ap(ysb, p1=8), lambda: ps(tys, 0, H, 1, 8), H, got(tys), [ysb], tys)
            dma("Y", [(T.ys[:, H * h:H * h + H], ap(ysb, p1=8))], 4096, r=[ysb])
        behind = yield wl
        GN = members("mem2", gn[h], rec, REC, su2, mk, tab, MEM, behind)
        zg = tmp("zg", h, H, "ab")
        gat("zg", lambda: V.tensor_tensor(ap(zg), go.indirect(ap(l_col)), ap(diag), OP.mult), H, [gk, l_col, diag], [zg])
        tr = tile()
        keepers = [(256, 512, 2, ap(ib), pold), (257, 512, 2, ap(ib), ap(lane, 1, 256, 2)), (256, 512, 1, ap(zg), ap(bo4n))]
        po = al("ah", 256)
        tk, oth = (tile(), tmp("oth", h, 256, "ah")) if other("cmp2") else (tr, None)
        mm(tk, keepers, 512, [ib, poldk, sub(lane, 1), zg, bo4n])
        if oth:
            lin("oth", ap(oth), lambda: ps(tk, 256, 512), 256, got(tk), [oth], tk)
        if CFG["stack2"]:
            tm = tile()
            mm(tm, [(k, H, 16, ap(gn[h], k, 2048, 16), ap(bo, 0, 128, 16)) for k in range(16)], 1024, [bo] + GN)
            lin("m2", ap(u2, 1, 256, 2), lambda: ps(tm, 0, H), H, got(tm), [sub(u2, 1)], tm)
            mm(tr, [(0, 256, 1, ap(i8n), ap(ones)), (0, 256, 1, ap(zg), ap(bo4p)), (0, 256, 1, ap(ib), ap(u2))], 768, [i8n, ones, zg, bo4p, ib] + subs(u2, 2))
            stacked("cmp2", sg2[h], u2, h, tr, 0, 2)
        else:
            mm(tr, [(0, 256, 1, ap(i8n), ap(ones)), (0, 256, 1, ap(zg), ap(bo4p)), (0, 256, 2, ap(ib), nl)], 640, [i8n, ones, zg, bo4p, ib, nlk])
            first = tr["keys"][-1]
            mm(tr, [(2 * k + 1, 256, 32, ap(gn[h], k, 2048, 16), ap(bo, 0, 128, 16)) for k in range(16)], 1024, [bo, first] + GN)

            def after(b, col, ck):
                calls = []
                for k in range(4 * b, 4 * b + 4):
                    calls.append((2 * k + 1, 256, 32, col(k), ap(bow, 0, 128, 16)))
                    calls.append((0, 256, 2, col(k), ap(iw)))
                mm(tr, calls, 768, [bow, iw, first] + ck)
            compare("cmp2", sg2[h], gn[h], GN, nl, nlk, after)
        settle("set2", tr, 256, ap(po), [po], h, oth)
        if not last:
            send(h, ap(pm[t + 1, h]), ap(po), [po], subs(pm[t + 1, h], 2), 65536)
        else:
            tf, yo = tile(), al("af", 256)
            mm(tf, [(H * m, H * m + H, 1, ap(po, m, 256, 2), ap(ib)) for m in range(2)], 256, [po, ib])
            v1("yo", lambda: ts(ap(yo), ps(tf, 0, 256), 2048.0, -1.0, OP.add, OP.max), 256, got(tf), [yo], tf)
            dma("Y", [(T.yp[:, H * h:H * h + H], ap(yo, 0, H)), (T.yq[:, H * h:H * h + H], ap(yo, H, 2 * H))], 131072, r=[yo])
        yield None

    thr = thl
    xout = al("af", 256)
    for t in range(RO):
        last = t == RO - 1
        wls = {}
        u, w = t % 2, 1 - t % 2
        tab, nxt = T[("tab", "tab1")[u]], T[("tab", "tab1")[w]]
        MEM, REC = ["mem%d" % (q + 4 * u) for q in range(4)], ["rec%d" % (q + 4 * u) for q in range(4)]
        MEMN, RECN = ["mem%d" % (q + 4 * w) for q in range(4)], ["rec%d" % (q + 4 * w) for q in range(4)]
        rec, RECR = (T.lmi[:, :], ["lmi%d" % q for q in range(4)]) if t == 0 else (tab[:, 0:2048], REC)
        cur[0] = (t, 1)
        upper = half(t, 1, tab, rec, MEM, RECR, thr, xout)
        first = next(upper)
        if t > 0:
            cur[0] = (t - 1, 0)
            lower.send(first)
        cur[0] = (t, 0)
        lists = [sub(pm[t, h], 1) for h in range(NH)]
        if t > 0:
            dma("Y", [(nxt[:, 0:MEM0], tab[:, 0:MEM0])], 1064960, r=REC + ["pad%d" % u] + lists[CFG["early"]:], w=RECN + ["pad%d" % w], name="copy")
        if not last:
            dma("Y", [(nxt[:, MEM0:2 * MEM0], tab[:, MEM0:2 * MEM0])], 1064960, r=MEM + ["padm%d" % u] + lists, w=MEMN + ["padm%d" % w], name="copy")
        cur[0] = (t, 1)
        wls[1] = next(upper)
        upper.send([])
        cur[0] = (t, 0)
        lower = half(t, 0, tab, rec, MEM, RECR, thr, xout)
        next(lower)
        wls[0] = next(lower)
        if last:
            lower.send([])
        win = nxt[:, 0:MEM0] if last else nxt[:, :]
        for h in (1, 0):
            cur[0] = (t, h)
            old, new = T["old%d" % h], T["new%d" % h]
            for c in range(7, -1, -1):
                if last:
                    op("V", lambda wl=wls[h], old=old, new=new, c=c, win=win: [V.tensor_tensor(win.indirect(ap(wl, 2 * c, 2 * c + 1)), old[:, c, 0:16], new[:, c, 0:16], OP.max)],
                       50 + 16 * SC, [wls[h], "old%d0" % h, "newr%d" % h], RECN + ["pad%d" % w], name="scat")
                else:
                    op("V", lambda wl=wls[h], old=old, new=new, c=c, win=win: [V.tensor_tensor(win.indirect(ap(wl, 2 * c, 2 * c + 2)), old[:, c, :], new[:, c, :], OP.max)],
                       50 + 32 * SC, [wls[h], "old%d0" % h, "old%d1" % h, "newr%d" % h, "newm%d" % h], RECN + MEMN + ["pad%d" % w, "padm%d" % w], name="scat")
        if not last:
            cnt, junk, cz, a1, a2, nthr, ta = al("af", 1), al("af", 32), al("ab", 16), al("ai", 16), al("ai", 16), al("af", 16), tile()
            op("S", lambda t=t, junk=junk, cnt=cnt: [S.activation(ap(junk), ap(g2, 32 * t, 32 * t + 32), AF.Identity, accum_out=ap(cnt))], sc(32) + 20,
               [sub(g2, NH * t + h) for h in range(NH)], [junk, cnt])
            sact(cz, bo8, scale=ap(cnt), r=[cnt])
            mm(ta, [(0, 16, 1, ap(ones, 0, 128), ap(cz))], 64, [ones, cz])
            lin("cnt", ap(a1), lambda ta=ta: ps(ta, 0, 16), 16, got(ta), [a1], ta, scale=1.0 / 128)
            vts(a2, a1, 496, None, OP.bitwise_and)
            v1("thr", lambda a2=a2, nthr=nthr: V.tensor_tensor(ap(nthr), ap(a2), ap(thl), OP.add), 16, [a2, thl], [nthr])
            thr = nthr
    dma("Y", [(T.yx[:, :], ap(xout))], 131072, r=subs(xout, 2))
    dma("Y", [(T.ylm[:, :], nxt[:, 0:2048])], 1048576, r=RECN)
    CFG["used"] = used
    return ops


def links(ops):
    lastw, readers = {}, {}
    for i, o in enumerate(ops):
        d = set(lastw[k] for k in o["r"] + o["w"] if k in lastw)
        for k in o["w"]:
            d.update(readers.get(k, []))
        d.discard(i)
        o["d"] = d
        for k in o["r"]:
            readers.setdefault(k, []).append(i)
        for k in o["w"]:
            lastw[k] = i
            readers[k] = []


def lay(ops):
    n = len(ops)
    succ = [[] for _ in ops]
    for i, o in enumerate(ops):
        for j in o["d"]:
            succ[j].append(i)

    def hop(i, e):
        a = ops[i]
        return 0.0 if a["e"] == e == "P" else 0.0 if a["k"] != "c" else CFG["same" if a["e"] == e else "psum" if a["e"] == "P" else "other"]
    way = [0.0] * n
    for i in reversed(range(n)):
        o = ops[i]
        due = CFG["pos"].get((o["name"], o["tv"][1]))
        way[i] = 1e9 - i if o["name"] == "load" else max([-1e6 if due is None else -due - CFG["period"] * o["tv"][0]] + [way[j] + 1e-3 * o["c"] for j in succ[i]])
    left = [len(o["d"]) for o in ops]
    rdy = [0.0] * n
    end = [0.0] * n
    free = {e: 0.0 for e in "VSPGY"}
    cand = {e: [] for e in "VSPGY"}
    for i, o in enumerate(ops):
        if not left[i]:
            cand[o["e"]].append(i)
    touch = [{} for _ in range(8)]
    holder = [None] * 8
    dmas = [0.0]
    seq = []

    def start(i):
        o = ops[i]
        st, t = max(rdy[i], free[o["e"]]), o["t"]
        if t is None:
            return st, None
        banks = [t["b"]] if t["b"] is not None else [b for b in ([t["own"]] if t["own"] is not None else range(NH, 8)) if holder[b] is None]
        if not banks:
            return None, None
        return min((max([st] + [end[j] + hop(j, o["e"]) for e, j in touch[b].items() if e != o["e"]]), b) for b in banks)
    while len(seq) < n:
        best = None
        table = {}
        for e in cand:
            table[e] = [(i,) + start(i) for i in cand[e]]
            table[e] = [x for x in table[e] if x[1] is not None]
            for i, st, b in table[e]:
                if best is None or st + CFG["slack"] * ops[i]["c"] < best[0]:
                    best = (st + CFG["slack"] * ops[i]["c"], e)
        i, st, b = max((x for x in table[best[1]] if x[1] <= best[0]), key=lambda x: (way[x[0]], -x[0]))
        o = ops[i]
        t = o["t"]
        if t is not None:
            o["d"] = o["d"] | set(j for e, j in touch[b].items() if e != o["e"])
            t["b"] = b
            touch[b][o["e"]] = i
            t["n"] -= 1
            holder[b] = t if t["n"] else None
        o["st"] = st
        free[o["e"]] = end[i] = st + o["c"]
        if o["k"] != "c":
            dmas[0] = max(dmas[0], end[i] + 900) + o["lat"]
            end[i] = dmas[0] + 800
        cand[o["e"]].remove(i)
        seq.append(i)
        for j in succ[i]:
            rdy[j] = max(rdy[j], end[i] + hop(i, ops[j]["e"]))
            left[j] -= 1
            if not left[j]:
                cand[ops[j]["e"]].append(j)
    CFG["span"] = max(end)
    return seq


def polish(ops, waits, seq, rounds):
    n = len(ops)
    above, dep = [], []
    for d in waits:
        far = 0
        for j in d:
            far |= above[j]
        dep.append(sorted(j for j in d if not far >> j & 1))
        above.append(far | sum(1 << j for j in d if not far >> j & 1))
    succ = [[] for _ in ops]
    for i, d in enumerate(dep):
        for j in d:
            succ[j].append(i)
    eng = ["VSPGY".index(o["e"]) for o in ops]
    cost = [o["c"] for o in ops]
    alt = [{"VSPGY".index(e): c for e, c in o["alt"]} if o["flex"] else None for o in ops]
    kind = ["cdr".index(o["k"]) for o in ops]
    extra = [o["lat"] for o in ops]
    ids = {}
    tile = [-1 if o["t"] is None else ids.setdefault(o["t"]["id"], len(ids)) for o in ops]
    uses, own = [0] * len(ids), [None] * len(ids)
    seen, sign, twin = {}, [], {}
    for i, o in enumerate(ops):
        if tile[i] >= 0:
            uses[tile[i]] += 1
            own[tile[i]] = o["t"]["own"]
        k = (o["name"], "" if o["flex"] else o["e"], o["tv"])
        seen[k] = seen.get(k, 0) + 1
        sign.append((k[0], k[1], o["tv"][1], seen[k]))
        twin[sign[i], o["tv"][0]] = i
    visit = [o["tv"][0] for o in ops]
    hop = [[CFG["same"] if a == b else CFG["other"] for b in range(5)] for a in range(5)]
    hop[2] = [CFG["psum"], CFG["psum"], 0.0, CFG["psum"], CFG["psum"]]

    def play(order):
        end, pred, free, last, dmas, dlast = [0.0] * n, [-1] * n, [0.0] * 5, [-1] * 5, 0.0, -1
        bank, left, held, touch = [-1] * len(uses), list(uses), [False] * 8, [[-1, -1, -1] for _ in range(8)]
        for i in order:
            e = eng[i]
            st, p = free[e], last[e]
            for j in dep[i]:
                x = end[j] if kind[j] else end[j] + hop[eng[j]][e]
                if x > st:
                    st, p = x, j
            t = tile[i]
            if t >= 0:
                b = bank[t]
                if b < 0:
                    soon = 1e18
                    for c in (range(NH, 8) if own[t] is None else (own[t],)):
                        if not held[c]:
                            u, v = touch[c][:2]
                            x = max(end[u] if u >= 0 else 0.0, end[v] if v >= 0 else 0.0)
                            if x < soon:
                                soon, b = x, c
                    if b < 0:
                        return 1e12, None, None, None, None
                    bank[t] = b
                tc = touch[b]
                for f in (0, 1, 2):
                    j = tc[f]
                    if f != e and j >= 0 and end[j] + hop[f][e] > st:
                        st, p = end[j] + hop[f][e], j
                tc[e] = i
                left[t] -= 1
                held[b] = left[t] > 0
            x = free[e] = st + cost[i]
            last[e] = i
            if kind[i]:
                if dmas > x + 900:
                    p = dlast
                dmas, dlast = max(dmas, x + 900) + extra[i], i
                x = dmas + 800
            end[i], pred[i] = x, p
        span = max(end)
        i, path = end.index(span), []
        while i >= 0:
            path.append(i)
            i = pred[i]
        return span + CFG["mean"] * sum(end) / n, path, end, bank, pred

    def move(order, pos, a, b, ahead):
        pa, pb = pos[a], pos[b]
        if pa >= pb:
            return False
        grp, todo = ({b}, [b]) if ahead else ({a}, [a])
        while todo:
            for j in (dep if ahead else succ)[todo.pop()]:
                if pa <= pos[j] <= pb and j not in grp:
                    if j in (a, b) or len(grp) > 11:
                        return False
                    grp.add(j)
                    todo.append(j)
        seg = order[pa:pb + 1]
        order[pa:pb + 1] = [x for x in seg if (x in grp) == ahead] + [x for x in seg if (x in grp) != ahead]
        for q in range(pa, pb + 1):
            pos[order[q]] = q
        return True
    seed = [CFG["seed"]]

    def draw():
        seed[0] = (seed[0] * 6364136223846793005 + 1442695040888963407) % 2 ** 64
        return (seed[0] >> 11) / 2.0 ** 53
    loads = len([o for o in ops if o["name"] == "load"])
    order = list(range(loads)) + [i for i in seq if i >= loads]
    span, path, end, _, pred = play(order)
    best = (span, order, list(eng), list(cost))
    for r in range(rounds):
        if r % 500 == 499:
            timed = sorted(order, key=lambda i: i - 1e9 if i < loads else end[i] - cost[i] - (extra[i] + 1700 if kind[i] else 0))
            at = {x: q for q, x in enumerate(timed)}
            if all(at[j] < at[i] for i in range(n) for j in dep[i]):
                res = play(timed)
                if res[0] <= span + 50:
                    order, (span, path, end, _, pred) = timed, res
        b = path[int(draw() * (len(path) - 1))] if draw() < CFG["onpath"] else int(draw() * n)
        a = pred[b]
        if a < 0:
            continue
        u, alike, trial, flips = draw(), draw() < (0.9 if r < 0.75 * rounds else 0.4), order, []
        if a in waits[b] or u < 0.2:
            x = b if draw() < 0.5 else a
            if alt[x] is None:
                continue
            to = 1 - eng[x]
            for y in ([twin[sign[x], t] for t in range(RO) if (sign[x], t) in twin] if alike and visit[x] >= 0 else [x]):
                if eng[y] != to:
                    flips.append((y, eng[y], cost[y]))
                    eng[y], cost[y] = to, alt[y][to]
        else:
            ahead = draw() < 0.5
            while ahead and pred[a] >= 0 and eng[pred[a]] == eng[b] and pred[a] not in waits[b] and draw() < CFG["jump"]:
                a = pred[a]
            pairs = [(a, b)]
            if alike and min(visit[a], visit[b]) >= 0:
                pairs = [(twin[sign[a], visit[a] + d], twin[sign[b], visit[b] + d]) for d in range(1 - RO, RO)
                         if min(visit[a], visit[b]) + d >= 0 and (sign[a], visit[a] + d) in twin and (sign[b], visit[b] + d) in twin]
            trial, pos = list(order), [0] * n
            for k, x in enumerate(trial):
                pos[x] = k
            if not [1 for x, y in pairs if move(trial, pos, x, y, ahead)] or trial[:loads] != order[:loads]:
                continue
        res = play(trial)
        if res[0] <= span or draw() < math.exp((span - res[0]) / (CFG["warm"] * (CFG["cool"] / CFG["warm"]) ** (r / rounds))):
            order, (span, path, end, _, pred) = trial, res
            if span < best[0]:
                best = (span, order, list(eng), list(cost))
        else:
            for y, e, c in flips:
                eng[y], cost[y] = e, c
    span, order, eng[:], cost[:] = best
    end, bank = play(order)[2:4]
    return max(end), order, ["VSPGY"[e] for e in eng], [None if t < 0 else bank[t] for t in tile]


PLAN = []


def plan(ops):
    links(ops)
    waits = [o["d"] for o in ops]
    if not PLAN:
        PLAN.append(polish(ops, waits, lay(ops), CFG["rounds"]))
    _, seq, eng, bank = PLAN[0]
    touch, sent = [{} for _ in range(8)], set()
    for i in seq:
        o = ops[i]
        o["e"], o["d"] = eng[i], waits[i]
        if o["k"] == "r":
            sent = {i}
        elif o["name"] == "copy":
            o["d"] = o["d"] | sent
        if bank[i] is not None:
            o["t"]["b"] = bank[i]
            o["d"] = o["d"] | set(j for e, j in touch[bank[i]].items() if e != o["e"])
            touch[bank[i]][o["e"]] = i
    return seq


def rank_program(g, core, T, topo):
    if T.rank_of(core) is None:
        return
    ops = build(g, core, T, topo)
    seq = plan(ops)
    queue = {"V": g.vector, "S": g.scalar, "P": g.tensor, "G": g, "Y": g.sync}
    count, waited, nd = {}, {}, [0]
    for i in seq:
        o = ops[i]
        e = o["e"]
        need = {}
        for j in o["d"]:
            p = ops[j]
            if p["e"] == "P" and e == "P":
                continue
            s, c = p["mark"]
            need[s] = max(need.get(s, 0), c)
        for s in sorted(need):
            if waited.get((e, s), 0) < need[s]:
                queue[e].wait_ge(T.sem[s], need[s])
                waited[e, s] = need[s]

        def chain(x, e=e):
            x.then_inc(T.sem["c" + e], 1)
            count["c" + e] = count.get("c" + e, 0) + 1
            queue[e].wait_ge(T.sem["c" + e], count["c" + e])
            waited[e, "c" + e] = count["c" + e]
        ins = o["fn"](e, chain) if o["flex"] else o["fn"]()
        if o["k"] == "r":
            count["left"] = count.get("left", 0) + o["n"]
            count[o["sem"]] = o["n"]
            o["mark"] = (o["sem"], o["n"])
            continue
        if o["k"] == "d":
            s, inc = "d%d" % nd[0], 16
            nd[0] += 1
        else:
            s, inc = "c" + e, 1
        for x in ins:
            x.then_inc(T.sem[s], inc)
            count[s] = count.get(s, 0) + inc
        o["mark"] = (s, count[s])
    for s in sorted(count):
        g.wait_ge(T.sem[s], count[s])
